import numpy as np
import ml_dtypes


def mxq(x, axis, fmt="e4m3"):
    dtype, down = {"e4m3": (ml_dtypes.float8_e4m3fn, 7), "e5m2": (ml_dtypes.float8_e5m2, 14)}[fmt]
    v = np.moveaxis(np.asarray(x, np.float32).astype(ml_dtypes.bfloat16).astype(np.float64), axis, -1)
    blocks = v.reshape(v.shape[:-1] + (-1, 32))
    amax = np.abs(blocks).max(-1, keepdims=True)
    byte = np.maximum(np.where(amax > 0, np.frexp(amax)[1] - 1 + 127, 0) - down, 1)
    scale = np.exp2(byte - 127.0)
    codes = (blocks / scale).astype(np.float32).astype(dtype).astype(np.float64)
    return np.moveaxis((codes * scale).reshape(v.shape), -1, axis)


WIDE = False


def mx_kscale(k):
    if not WIDE:
        return np.ones(k)
    levels = np.array([10, -10, 5, -5, 0])
    if k % 512:
        return np.exp2(np.random.permutation(np.resize(levels, k // 32))).repeat(32)
    a = np.empty((k // 512, 16))
    for p in range(k // 512):
        a[p, :8] = np.random.permutation(np.resize(levels, 8))
        for g in range(8):
            far = levels[np.abs(levels - a[p, g]) >= 10]
            a[p, g + 8] = far[np.random.randint(len(far))]
    return np.exp2(a.ravel()).repeat(32)


def f64(x):
    return np.asarray(x).astype(np.float64)


def striped(idx):
    return np.tile(idx.reshape(-1, 16).T, (8, 1)).astype(np.uint16)


def unstriped(offs):
    return offs[:16].T.reshape(-1).astype(np.int64)


E2M1 = np.array([0.0, 0.5, 1.0, 1.5, 2.0, 3.0, 4.0, 6.0, -0.0, -0.5, -1.0, -1.5, -2.0, -3.0, -4.0, -6.0])


def pack_weight(w, fmt):
    k, n = w.shape
    w = f64(np.asarray(w, np.float32).astype(ml_dtypes.bfloat16)).reshape(k // 32, 32, n)
    amax = np.abs(w).max(1)
    if fmt == "e4m3":
        byte = np.frexp(amax)[1] - 1 + 127 - 7
    else:
        mant, ex = np.frexp(amax / 6.0)
        byte = np.where(mant > 0.5, ex, ex - 1) + 127
    byte = np.clip(np.where(amax > 0, byte, 1), 1, 254)
    scaled = (w * np.exp2(127.0 - byte)[:, None, :]).reshape(k, n).astype(np.float32)
    by_word = np.ascontiguousarray(scaled.reshape(k // 512, 128, 4, n).transpose(0, 1, 3, 2))
    if fmt == "e4m3":
        words = by_word.astype(ml_dtypes.float8_e4m3fn).view(np.uint8)
    else:
        c = by_word.astype(ml_dtypes.float4_e2m1fn).view(np.uint8) & 0xF
        words = (c[..., 0::2] | (c[..., 1::2] << 4)).reshape(k // 512, 128, 2 * n)
    return np.ascontiguousarray(words), np.ascontiguousarray(byte.astype(np.uint8).reshape(k // 512, 16, n))


def unpack_weight(words, scales, fmt):
    g, _, n = scales.shape
    words = np.ascontiguousarray(words).reshape(g, 128, n, -1)
    if fmt == "e4m3":
        vals = words.view(ml_dtypes.float8_e4m3fn).astype(np.float64)
    else:
        nib = np.empty((g, 128, n, 4), np.uint8)
        nib[..., 0::2] = words & 0xF
        nib[..., 1::2] = words >> 4
        vals = E2M1[nib]
    vals = vals * np.repeat(np.exp2(scales.astype(np.float64) - 127.0), 8, axis=1)[..., None]
    return vals.transpose(0, 1, 3, 2).reshape(g * 512, n)


def gelu(v):
    return 0.5 * v * (1.0 + np.tanh(np.sqrt(2.0 / np.pi) * (v + 0.044715 * v**3)))


def striped8(idx):
    return np.concatenate([v.reshape(-1, 16).T for v in idx]).astype(np.uint16)


def unstriped8(offs):
    return np.stack([offs[16 * g:16 * g + 16].T.reshape(-1) for g in range(8)]).astype(np.int64)


def runs(v, idx8):
    k = np.arange(v.shape[0])
    return v[k[:, None], idx8[k % 512 // 64]]


K, K2, T, T2, S, H, N = 1024, 512, 2048, 4096, 1024, 1024, 256

def setup_inputs():
    n = np.random.standard_normal
    s = mx_kscale(K)[:, None]
    s2 = mx_kscale(K2)[:, None]
    u = mx_kscale(H)[:, None]
    tab_words, tab_scales = pack_weight(n((K, T)) * s, "e4m3")
    tab2_words, tab2_scales = pack_weight(n((K2, T2)) * s2, "e4m3")
    w4_words, w4_scales = pack_weight(1.5 * n((K, H)) / np.sqrt(K) / s, "e2m1")
    w8_words, w8_scales = pack_weight(0.8 * n((K2, H)) / np.sqrt(K2) / s2, "e4m3")
    return {
        "tab_words": tab_words, "tab_scales": tab_scales,
        "offs": striped8(np.stack([np.random.permutation(T)[:S] for _ in range(8)])),
        "tab2_words": tab2_words, "tab2_scales": tab2_scales,
        "offs2": striped(np.random.permutation(T2)[:S]),
        "w4_words": w4_words, "w4_scales": w4_scales,
        "wg": (1.5 * n((K2, H)) / np.sqrt(K2) / s2).astype(np.float32),
        "w8_words": w8_words, "w8_scales": w8_scales,
        "gain": (np.exp(0.3 * n(H)) * u[:, 0]).astype(np.float32),
        "wo": (1.5 * n((H, N)) / np.sqrt(H) / u).astype(np.float32),
    }

def reference(tab_words, tab_scales, offs, tab2_words, tab2_scales, offs2,
              w4_words, w4_scales, wg, w8_words, w8_scales, gain, wo):
    v = runs(unpack_weight(tab_words, tab_scales, "e4m3"), unstriped8(offs))
    v2 = unpack_weight(tab2_words, tab2_scales, "e4m3")[:, unstriped(offs2)]
    pocket = unpack_weight(w4_words, w4_scales, "e2m1").T @ v
    gate = mxq(f64(wg), 0, "e4m3").T @ v2
    shift = unpack_weight(w8_words, w8_scales, "e4m3").T @ v2
    b = pocket / (1.0 + np.exp(-gate)) + shift
    h = f64(gain)[:, None] * (b / (1.0 + np.exp(-b)))
    return mxq(f64(wo), 0, "e4m3").T @ mxq(h, 0, "e4m3")

@@ -1,0 +1,329 @@
+from contextlib import ExitStack
+
+import concourse.mybir as mybir
+from concourse.masks import make_identity
+
+K, K2, T, T2, S, H, N = 1024, 512, 2048, 4096, 1024, 1024, 256
+FLOPS = 2 * S * (K * H + 2 * K2 * H + H * N)
+
+F32 = mybir.dt.float32
+BF16 = mybir.dt.bfloat16
+I32 = mybir.dt.int32
+U32 = mybir.dt.uint32
+U16 = mybir.dt.uint16
+U8 = mybir.dt.uint8
+FP8X4 = mybir.dt.float8_e4m3fn_x4
+FP4X4 = mybir.dt.float4_e2m1fn_x4
+ACT = mybir.ActivationFunctionType
+ADD = mybir.AluOpType.add
+MULT = mybir.AluOpType.mult
+
+P = 128
+JC = 128
+NJ = S // JC
+NB = H // 512
+NCHUNK = NB * NJ
+PIECE = 512
+GATE_AHEAD = 2
+VECTOR_GAIN_FROM = 15
+PLACE_KIB = {
+    "tab2_w": 0, "wg_raw1": 0,
+    "tab_w0": 24, "words_raw0": 21, "v_picked": 25, "tab_w1": 31, "wg_codes0": 25.5,
+    "wo_raw0": 21, "h_bf5": 21, "words_raw1": 31, "wo_raw1": 35, "h_bf7": 35,
+    "tab_s": 40, "v2_plane": 40,
+    "tab2_s": 46, "v2_words0": 44.5, "v2_words1": 46.5, "staged": 49, "wg_raw0": 50,
+    "ws_raw": 60, "w4_codes0": 59, "w8_codes0": 61,
+}
+
+
+def tile_list_kinase_selectivity_kernel(
+    tc, tab_words, tab_scales, offs, tab2_words, tab2_scales, offs2,
+    w4_words, w4_scales, wg, w8_words, w8_scales, gain, wo, out,
+):
+    nc = tc.nc
+    with ExitStack() as ctx:
+        keep = ctx.enter_context(tc.tile_pool(name="keep", bufs=1))
+        ring = ctx.enter_context(tc.tile_pool(name="ring", bufs=3))
+        arena = ctx.enter_context(tc.tile_pool(name="arena", bufs=1))
+        psum = ctx.enter_context(tc.psum_pool(name="psum", bufs=2))
+
+        def held(shape, dtype, name):
+            if name in PLACE_KIB:
+                return arena.tile(shape, dtype, name=name, align_bytes=64, offset=int(1024 * PLACE_KIB[name]))
+            return keep.tile(shape, dtype, name=name, align_bytes=64)
+
+        lists = keep.tile([P, S // 16], U16, name="lists")
+        list2 = keep.tile([P, S // 16], U16, name="list2")
+        tab_s = held([P, T], U8, "tab_s")
+        tab2_s = held([P, T2], U8, "tab2_s")
+        ws_raw = held([P, 2, H], U8, "ws_raw")
+        planes = held([P, 5, S], U8, "planes")
+        gain_rows = held([P, P], F32, "gain_rows")
+        ident = held([P, P], F32, "ident")
+        wg_raw, w4_raw, w8_raw, wo_raw, tab_w = {}, {}, {}, {}, {}
+
+        nc.vector.memset(tab2_s[:].bitcast(I32), 0)
+        nc.vector.memset(ws_raw[:].bitcast(I32), 0)
+        nc.vector.memset(tab_s[:].bitcast(I32), 0)
+        nc.vector.memset(planes[:].bitcast(I32), 0)
+        nc.gpsimd.memset(gain_rows[:], 0.0)
+
+        def load_wg(b):
+            nc.sync.dma_start(
+                out=wg_raw[b], in_=wg.rearrange("(p j) c -> p j c", j=4)[:, :, 512 * b : 512 * (b + 1)]
+            )
+
+        def load_words(b):
+            nc.sync.dma_start(
+                out=w4_raw[b],
+                in_=w4_words.bitcast(I32).rearrange("a p c -> p a c")[:, :, 256 * b : 256 * (b + 1)],
+            )
+            nc.sync.dma_start(
+                out=w8_raw[b],
+                in_=w8_words[0].rearrange("p c i -> p (c i)").bitcast(I32)[:, 512 * b : 512 * (b + 1)],
+            )
+
+        def take_words_tile(b):
+            raw = held([P, 1024], I32, "words_raw%d" % b)
+            w4_raw[b] = raw[:, 0:512].rearrange("p (a c) -> p a c", a=2)
+            w8_raw[b] = raw[:, 512:1024]
+            load_words(b)
+
+        def load_table(tile, words):
+            nc.sync.dma_start(out=tile[:].bitcast(I32), in_=words.rearrange("p t i -> p (t i)").bitcast(I32))
+
+        tab_w[0] = held([P, T], U32, "tab_w0")
+        wg_raw[0] = held([P, 4, 512], F32, "wg_raw0")[:]
+        nc.sync.dma_start(lists[:], offs)
+        load_table(tab_w[0], tab_words[0])
+        nc.sync.dma_start(list2[:], offs2)
+        load_wg(0)
+        tab2_w = held([P, T2], U32, "tab2_w")
+        load_table(tab2_w, tab2_words[0])
+        nc.scalar.dma_start(out=ws_raw[:].bitcast(I32)[0:P:8, 0, :], in_=w8_scales[0].bitcast(I32))
+        nc.scalar.dma_start(
+            out=ws_raw[:].bitcast(I32)[1:P:8, :, :], in_=w4_scales.bitcast(I32).rearrange("a q c -> q a c")
+        )
+        for a in range(2):
+            nc.scalar.dma_start(out=tab_s[:].bitcast(I32)[a:P:8, :], in_=tab_scales[a].bitcast(I32))
+        for d in range(4):
+            nc.gpsimd.dma_start(
+                out=tab2_s[:].bitcast(I32)[32 * d : 32 * d + 4, :],
+                in_=tab2_scales[0, 4 * d : 4 * d + 4, :].bitcast(I32),
+            )
+        for b in range(NB):
+            nc.gpsimd.dma_start(
+                out=gain_rows[4 * b : 4 * b + 4, :].rearrange("t (u e) -> t u e", e=4),
+                in_=gain[512 * b : 512 * (b + 1)].rearrange("(u t e) -> t u e", t=4, e=4),
+            )
+        make_identity(nc, ident[:])
+
+        wg_bf = {}
+        wg_codes, wg_plane, w4_codes, w8_codes, wo_codes, wo_plane = {}, {}, {}, {}, {}, {}
+
+        def cast_wg(b):
+            wg_bf[b] = held([P, 4, P, 4], BF16, "wg_bf%d" % b)
+            nc.scalar.copy(
+                wg_bf[b][:].rearrange("p t (u e) j -> p t u e j", e=4),
+                wg_raw[b].rearrange("p j (u t e) -> p t u e j", t=4, e=4),
+            )
+
+        def quantise_wg(b):
+            wg_codes[b] = held([P, 512], U32, "wg_codes%d" % b)
+            wg_plane[b] = held([P, 512], U8, "wg_plane%d" % b)
+            nc.vector.quantize_mx(
+                out=wg_codes[b][:].bitcast(FP8X4), scales=wg_plane[b][:],
+                in_=wg_bf[b][:].rearrange("p t m j -> p (t m j)"),
+            )
+
+        def order_words(b):
+            w4_codes[b] = held([P, 2, 4, 256], U8, "w4_codes%d" % b)
+            nc.vector.tensor_copy(
+                w4_codes[b][:].bitcast(I32).rearrange("p a t (u w) -> p a t u w", w=2),
+                w4_raw[b].rearrange("p a (u t w) -> p a t u w", t=4, w=2),
+            )
+            w8_codes[b] = held([P, 4, P], U32, "w8_codes%d" % b)
+            nc.vector.tensor_copy(
+                w8_codes[b][:].bitcast(I32).rearrange("p t (u e) -> p t u e", e=4),
+                w8_raw[b].rearrange("p (u t e) -> p t u e", t=4, e=4),
+            )
+
+        def cast_wo(b):
+            grouped = held([P, N, 4], BF16, "wo_bf%d" % b)
+            nc.gpsimd.tensor_scalar(grouped[:], wo_raw[b].rearrange("p t n -> p n t"), 1.0, 0.0, MULT, ADD)
+            wo_codes[b] = held([P, N], U32, "wo_codes%d" % b)
+            wo_plane[b] = held([P, N], U8, "wo_plane%d" % b)
+            nc.vector.quantize_mx(
+                out=wo_codes[b][:].bitcast(FP8X4), scales=wo_plane[b][:],
+                in_=grouped[:].rearrange("p n t -> p (n t)"),
+            )
+
+        def gather_words(window, offsets, piece, name):
+            picked = held([P, PIECE], U32, name)
+            cols = slice(piece * PIECE // 16, (piece + 1) * PIECE // 16)
+            nc.vector.tensor_copy(picked[:], window[:].indirect(offsets[:, cols]))
+            return picked
+
+        v_plane = [planes[:, 0, :], planes[:, 2, :]]
+        w8_plane, w4_plane = planes[:, 1, :], [planes[:, 3, :], planes[:, 4, :]]
+        v_words = [[None, None], [None, None]]
+        v_words[0][0] = gather_words(tab_w[0], lists, 0, "v_words00")
+        v_words[0][1] = gather_words(tab_w[0], lists, 1, "v_words01")
+        take_words_tile(0)
+        tab_w[1] = held([P, T], U32, "tab_w1")
+        load_table(tab_w[1], tab_words[1])
+        v_picked = held([P, S], U8, "v_picked")
+        nc.vector.tensor_copy(v_picked[:], tab_s[:].indirect(lists[:]))
+        v2_plane = held([P, S], U8, "v2_plane")
+        nc.vector.tensor_copy(v2_plane[:], tab2_s[:].indirect(list2[:]))
+        cast_wg(0)
+        staged = held([P, 3, S], U8, "staged")
+        nc.vector.tensor_copy(
+            staged[:].bitcast(I32)[:, 1:3, :].rearrange("p x (b t u) -> p (x b) t u", b=NB, t=4),
+            ws_raw[:].bitcast(I32).rearrange("p x (b u t) -> p (x b) t u", b=NB, t=4),
+        )
+        nc.vector.tensor_copy(staged[:].bitcast(I32)[:, 0, :], v_picked[:].bitcast(I32))
+        for x in range(2):
+            for r in range(4):
+                queue = nc.gpsimd if (x, r) == (0, 0) else nc.scalar
+                queue.dma_start(
+                    out=planes[:].bitcast(I32)[r:P:32, 2 * x : 3 * x + 2, :],
+                    in_=staged[:].bitcast(I32)[8 * r + x : P : 32, 0 : x + 2, :],
+                )
+        quantise_wg(0)
+        v2_words = [gather_words(tab2_w, list2, 0, "v2_words0"), None]
+        order_words(0)
+        v2_words[1] = gather_words(tab2_w, list2, 1, "v2_words1")
+        wg_raw[1] = held([P, 4, 512], F32, "wg_raw1")[:]
+        load_wg(1)
+
+        gain_ps = psum.tile([P, 512], F32, name="gain_ps", tag="out")
+        nc.tensor.transpose(gain_ps[:, 0:P], gain_rows[:], ident[:])
+        gain_full = [held([P, JC, 4], F32, "gain_full%d" % b) for b in range(NB)]
+        for b in range(NB):
+            nc.scalar.activation(
+                gain_full[b][:], gain_ps[:, 4 * b : 4 * b + 4].unsqueeze(1).to_broadcast([P, JC, 4]), ACT.Copy
+            )
+
+        tanh_half, pocket, shift, gated, mixed, h_bf, h_codes, h_plane = {}, {}, {}, {}, {}, {}, {}, {}
+
+        def moving(pieces, plane, jq):
+            start = jq * JC
+            words = pieces[start // PIECE][:, start % PIECE : start % PIECE + JC]
+            return words.bitcast(FP8X4), plane[:, start : start + JC]
+
+        def gate_stage(c):
+            b, jq = divmod(c, NJ)
+            rhs, rhs_scale = moving(v2_words, v2_plane, jq)
+            bank = psum.tile([P, 4, JC], F32, name="gate", tag="gate")
+            for t in range(4):
+                cols = slice(t * P, (t + 1) * P)
+                nc.tensor.matmul_mx(
+                    bank[:, t, :], lhsT=wg_codes[b][:, cols].bitcast(FP8X4), lhsT_scale=wg_plane[b][:, cols],
+                    rhs=rhs, rhs_scale=rhs_scale, start=True, stop=True,
+                )
+            tanh_half[c] = held([P, JC, 4], F32, "tanh_half%d" % c)
+            nc.scalar.activation(tanh_half[c][:], bank[:].rearrange("p t j -> p j t"), ACT.Tanh, scale=0.5)
+
+        def products(c):
+            b, jq = divmod(c, NJ)
+            pocket[c] = psum.tile([P, 4, JC], F32, name="pocket", tag="pocket")
+            for t in range(4):
+                for a in range(2):
+                    rhs, rhs_scale = moving(v_words[a], v_plane[a], jq)
+                    nc.tensor.matmul_mx(
+                        pocket[c][:, t, :], lhsT=w4_codes[b][:, a, t, :].bitcast(FP4X4),
+                        lhsT_scale=w4_plane[a][:, (4 * b + t) * P : (4 * b + t + 1) * P],
+                        rhs=rhs, rhs_scale=rhs_scale, start=(a == 0), stop=(a == 1),
+                    )
+            shift[c] = psum.tile([P, 4, JC], F32, name="shift", tag="shift")
+            rhs, rhs_scale = moving(v2_words, v2_plane, jq)
+            for t in range(4):
+                nc.tensor.matmul_mx(
+                    shift[c][:, t, :], lhsT=w8_codes[b][:, t, :].bitcast(FP8X4),
+                    lhsT_scale=w8_plane[:, (4 * b + t) * P : (4 * b + t + 1) * P],
+                    rhs=rhs, rhs_scale=rhs_scale, start=True, stop=True,
+                )
+
+        def gate_pocket(c):
+            gated[c] = ring.tile([P, JC, 4], F32, name="gated", tag="gated")
+            nc.vector.scalar_tensor_tensor(
+                gated[c][:], tanh_half[c][:], 1.0, pocket[c][:].rearrange("p t j -> p j t"), ADD, MULT
+            )
+
+        def add_shift(c):
+            b = c // NJ
+            mixed = ring.tile([P, JC, 4], F32, name="mixed", tag="mixed")
+            nc.vector.scalar_tensor_tensor(
+                mixed[:], gated[c][:], 0.5, shift[c][:].rearrange("p t j -> p j t"), MULT, ADD
+            )
+            silu = ring.tile([P, JC, 4], F32, name="silu", tag="silu")
+            nc.scalar.activation(silu[:], mixed[:], ACT.Silu)
+            if c in (5, 7):
+                h_bf[c] = held([P, JC, 4], BF16, "h_bf%d" % c)
+            else:
+                h_bf[c] = ring.tile([P, JC, 4], BF16, name="h_bf", tag="h_bf", align_bytes=64)
+            engine = nc.gpsimd if c < VECTOR_GAIN_FROM else nc.vector
+            engine.tensor_tensor(h_bf[c][:], silu[:], gain_full[b][:], MULT)
+
+        def quantise_h(c):
+            h_codes[c] = held([P, JC], U32, "h_codes%d" % c)
+            h_plane[c] = held([P, JC], U8, "h_plane%d" % c)
+            nc.vector.quantize_mx(
+                out=h_codes[c][:].bitcast(FP8X4), scales=h_plane[c][:],
+                in_=h_bf[c][:].rearrange("p j t -> p (j t)"),
+            )
+
+        def last_product(jq):
+            bank = psum.tile([P, 2, JC], F32, name="out_bank", tag="out")
+            for nt in range(2):
+                cols = slice(nt * P, (nt + 1) * P)
+                for b in range(NB):
+                    c = b * NJ + jq
+                    nc.tensor.matmul_mx(
+                        bank[:, nt, :], lhsT=wo_codes[b][:, cols].bitcast(FP8X4), lhsT_scale=wo_plane[b][:, cols],
+                        rhs=h_codes[c][:].bitcast(FP8X4), rhs_scale=h_plane[c][:],
+                        start=(b == 0), stop=(b == NB - 1),
+                    )
+            result = ring.tile([P, 2, JC], F32, name="result", tag="result")
+            nc.scalar.copy(result[:], bank[:])
+            nc.sync.dma_start(
+                out=out.rearrange("(nt p) j -> p nt j", p=P)[:, :, jq * JC : (jq + 1) * JC], in_=result[:]
+            )
+
+        for c in range(GATE_AHEAD):
+            gate_stage(c)
+
+        def load_wo(b):
+            wo_raw[b] = held([P, 4, N], F32, "wo_raw%d" % b)[:]
+            rows = wo[512 * b : 512 * (b + 1), :].rearrange("(u t e) n -> e u t n", t=4, e=4)
+            for e in range(4):
+                nc.sync.dma_start(out=wo_raw[b][e:P:4, :, :], in_=rows[e])
+
+        load_wo(0)
+        v_words[1][0] = gather_words(tab_w[1], lists, 0, "v_words10")
+        products(0)
+        v_words[1][1] = gather_words(tab_w[1], lists, 1, "v_words11")
+        take_words_tile(1)
+        load_wo(1)
+
+        gate_pocket(0)
+        for c in range(NCHUNK + 2):
+            if c == 2:
+                cast_wg(1)
+                quantise_wg(1)
+            if c == 3:
+                order_words(1)
+            if c in (5, 7):
+                cast_wo((c - 5) // 2)
+            if c + GATE_AHEAD < NCHUNK:
+                gate_stage(c + GATE_AHEAD)
+            if c + 1 < NCHUNK:
+                products(c + 1)
+                gate_pocket(c + 1)
+            if c < NCHUNK:
+                add_shift(c)
+            if c >= 2:
+                quantise_h(c - 2)
+            if c - 2 >= NJ:
+                last_product(c - 2 - NJ)

@@ -25,12 +25,12 @@ NB = H // 512
 NCHUNK = NB * NJ
 PIECE = 512
 GATE_AHEAD = 2
-VECTOR_GAIN_FROM = 15
+VECTOR_GAIN_FROM = 14
 PLACE_KIB = {
     "tab2_w": 0, "wg_raw1": 0,
-    "tab_w0": 24, "words_raw0": 21, "v_picked": 25, "tab_w1": 31, "wg_codes0": 25.5,
-    "wo_raw0": 21, "h_bf5": 21, "words_raw1": 31, "wo_raw1": 35, "h_bf7": 35,
-    "tab_s": 40, "v2_plane": 40,
+    "tab_w0": 24, "words_raw0": 21, "v_picked": 30, "wg_codes0": 28.5, "tab_w1": 30.5,
+    "wo_raw0": 21, "silu3": 21, "words_raw1": 30.5, "wo_raw1": 34.5, "gated9": 34.5,
+    "tab_s": 40, "v2_picked": 40,
     "tab2_s": 46, "v2_words0": 44.5, "v2_words1": 46.5, "staged": 49, "wg_raw0": 50,
     "ws_raw": 60, "w4_codes0": 59, "w8_codes0": 61,
 }
@@ -57,14 +57,14 @@ def tile_list_kinase_selectivity_kernel(
         tab_s = held([P, T], U8, "tab_s")
         tab2_s = held([P, T2], U8, "tab2_s")
         ws_raw = held([P, 2, H], U8, "ws_raw")
-        planes = held([P, 5, S], U8, "planes")
+        planes = held([P, 6, S], U8, "planes")
         gain_rows = held([P, P], F32, "gain_rows")
         ident = held([P, P], F32, "ident")
         wg_raw, w4_raw, w8_raw, wo_raw, tab_w = {}, {}, {}, {}, {}
 
-        nc.vector.memset(tab2_s[:].bitcast(I32), 0)
         nc.vector.memset(ws_raw[:].bitcast(I32), 0)
         nc.vector.memset(tab_s[:].bitcast(I32), 0)
+        nc.vector.memset(tab2_s[:].bitcast(I32), 0)
         nc.vector.memset(planes[:].bitcast(I32), 0)
         nc.gpsimd.memset(gain_rows[:], 0.0)
 
@@ -106,11 +106,7 @@ def tile_list_kinase_selectivity_kernel(
         )
         for a in range(2):
             nc.scalar.dma_start(out=tab_s[:].bitcast(I32)[a:P:8, :], in_=tab_scales[a].bitcast(I32))
-        for d in range(4):
-            nc.gpsimd.dma_start(
-                out=tab2_s[:].bitcast(I32)[32 * d : 32 * d + 4, :],
-                in_=tab2_scales[0, 4 * d : 4 * d + 4, :].bitcast(I32),
-            )
+        nc.scalar.dma_start(out=tab2_s[:].bitcast(I32)[0:P:8, :], in_=tab2_scales[0].bitcast(I32))
         for b in range(NB):
             nc.gpsimd.dma_start(
                 out=gain_rows[4 * b : 4 * b + 4, :].rearrange("t (u e) -> t u e", e=4),
@@ -150,7 +146,10 @@ def tile_list_kinase_selectivity_kernel(
 
         def cast_wo(b):
             grouped = held([P, N, 4], BF16, "wo_bf%d" % b)
-            nc.gpsimd.tensor_scalar(grouped[:], wo_raw[b].rearrange("p t n -> p n t"), 1.0, 0.0, MULT, ADD)
+            if b == 0:
+                nc.scalar.copy(grouped[:], wo_raw[b].rearrange("p t n -> p n t"))
+            else:
+                nc.vector.tensor_copy(grouped[:], wo_raw[b].rearrange("p t n -> p n t"))
             wo_codes[b] = held([P, N], U32, "wo_codes%d" % b)
             wo_plane[b] = held([P, N], U8, "wo_plane%d" % b)
             nc.vector.quantize_mx(
@@ -164,32 +163,32 @@ def tile_list_kinase_selectivity_kernel(
             nc.vector.tensor_copy(picked[:], window[:].indirect(offsets[:, cols]))
             return picked
 
-        v_plane = [planes[:, 0, :], planes[:, 2, :]]
-        w8_plane, w4_plane = planes[:, 1, :], [planes[:, 3, :], planes[:, 4, :]]
+        v2_plane, v_plane = planes[:, 0, :], [planes[:, 1, :], planes[:, 3, :]]
+        w8_plane, w4_plane = planes[:, 2, :], [planes[:, 4, :], planes[:, 5, :]]
         v_words = [[None, None], [None, None]]
         v_words[0][0] = gather_words(tab_w[0], lists, 0, "v_words00")
         v_words[0][1] = gather_words(tab_w[0], lists, 1, "v_words01")
         take_words_tile(0)
-        tab_w[1] = held([P, T], U32, "tab_w1")
-        load_table(tab_w[1], tab_words[1])
         v_picked = held([P, S], U8, "v_picked")
         nc.vector.tensor_copy(v_picked[:], tab_s[:].indirect(lists[:]))
-        v2_plane = held([P, S], U8, "v2_plane")
-        nc.vector.tensor_copy(v2_plane[:], tab2_s[:].indirect(list2[:]))
+        v2_picked = held([P, S], U8, "v2_picked")
+        nc.vector.tensor_copy(v2_picked[:], tab2_s[:].indirect(list2[:]))
         cast_wg(0)
-        staged = held([P, 3, S], U8, "staged")
+        staged = held([P, 4, S], U8, "staged")
         nc.vector.tensor_copy(
-            staged[:].bitcast(I32)[:, 1:3, :].rearrange("p x (b t u) -> p (x b) t u", b=NB, t=4),
+            staged[:].bitcast(I32)[:, 2:4, :].rearrange("p x (b t u) -> p (x b) t u", b=NB, t=4),
             ws_raw[:].bitcast(I32).rearrange("p x (b u t) -> p (x b) t u", b=NB, t=4),
         )
-        nc.vector.tensor_copy(staged[:].bitcast(I32)[:, 0, :], v_picked[:].bitcast(I32))
+        nc.vector.tensor_copy(staged[:].bitcast(I32)[:, 0, :], v2_picked[:].bitcast(I32))
+        nc.vector.tensor_copy(staged[:].bitcast(I32)[:, 1, :], v_picked[:].bitcast(I32))
         for x in range(2):
             for r in range(4):
-                queue = nc.gpsimd if (x, r) == (0, 0) else nc.scalar
-                queue.dma_start(
-                    out=planes[:].bitcast(I32)[r:P:32, 2 * x : 3 * x + 2, :],
-                    in_=staged[:].bitcast(I32)[8 * r + x : P : 32, 0 : x + 2, :],
+                nc.scalar.dma_start(
+                    out=planes[:].bitcast(I32)[r:P:32, 3 * x : 3 * x + 3, :],
+                    in_=staged[:].bitcast(I32)[8 * r + x : P : 32, x : x + 3, :],
                 )
+        tab_w[1] = held([P, T], U32, "tab_w1")
+        load_table(tab_w[1], tab_words[1])
         quantise_wg(0)
         v2_words = [gather_words(tab2_w, list2, 0, "v2_words0"), None]
         order_words(0)
@@ -199,13 +198,13 @@ def tile_list_kinase_selectivity_kernel(
 
         gain_ps = psum.tile([P, 512], F32, name="gain_ps", tag="out")
         nc.tensor.transpose(gain_ps[:, 0:P], gain_rows[:], ident[:])
-        gain_full = [held([P, JC, 4], F32, "gain_full%d" % b) for b in range(NB)]
+        gain_full = [held([P, 2 * JC, 4], F32, "gain_full%d" % b) for b in range(NB)]
         for b in range(NB):
             nc.scalar.activation(
-                gain_full[b][:], gain_ps[:, 4 * b : 4 * b + 4].unsqueeze(1).to_broadcast([P, JC, 4]), ACT.Copy
+                gain_full[b][:], gain_ps[:, 4 * b : 4 * b + 4].unsqueeze(1).to_broadcast([P, 2 * JC, 4]), ACT.Copy
             )
 
-        tanh_half, pocket, shift, gated, mixed, h_bf, h_codes, h_plane = {}, {}, {}, {}, {}, {}, {}, {}
+        tanh_half, pocket, shift, gated, silu, h_bf, h_codes, h_plane = {}, {}, {}, {}, {}, {}, {}, {}
 
         def moving(pieces, plane, jq):
             start = jq * JC
@@ -246,49 +245,61 @@ def tile_list_kinase_selectivity_kernel(
                 )
 
         def gate_pocket(c):
-            gated[c] = ring.tile([P, JC, 4], F32, name="gated", tag="gated")
+            if "gated%d" % c in PLACE_KIB:
+                gated[c] = held([P, JC, 4], F32, "gated%d" % c)
+            else:
+                gated[c] = ring.tile([P, JC, 4], F32, name="gated", tag="gated")
             nc.vector.scalar_tensor_tensor(
                 gated[c][:], tanh_half[c][:], 1.0, pocket[c][:].rearrange("p t j -> p j t"), ADD, MULT
             )
 
         def add_shift(c):
-            b = c // NJ
+            pair, half = divmod(c, 2)
             mixed = ring.tile([P, JC, 4], F32, name="mixed", tag="mixed")
             nc.vector.scalar_tensor_tensor(
                 mixed[:], gated[c][:], 0.5, shift[c][:].rearrange("p t j -> p j t"), MULT, ADD
             )
-            silu = ring.tile([P, JC, 4], F32, name="silu", tag="silu")
-            nc.scalar.activation(silu[:], mixed[:], ACT.Silu)
-            if c in (5, 7):
-                h_bf[c] = held([P, JC, 4], BF16, "h_bf%d" % c)
-            else:
-                h_bf[c] = ring.tile([P, JC, 4], BF16, name="h_bf", tag="h_bf", align_bytes=64)
-            engine = nc.gpsimd if c < VECTOR_GAIN_FROM else nc.vector
-            engine.tensor_tensor(h_bf[c][:], silu[:], gain_full[b][:], MULT)
+            if half == 0:
+                if "silu%d" % pair in PLACE_KIB:
+                    silu[pair] = held([P, 2 * JC, 4], F32, "silu%d" % pair)
+                else:
+                    silu[pair] = ring.tile([P, 2 * JC, 4], F32, name="silu", tag="silu")
+            nc.scalar.activation(silu[pair][:, half * JC : (half + 1) * JC, :], mixed[:], ACT.Silu)
 
-        def quantise_h(c):
-            h_codes[c] = held([P, JC], U32, "h_codes%d" % c)
-            h_plane[c] = held([P, JC], U8, "h_plane%d" % c)
+        def apply_gain(engine, c, count):
+            pair, half = divmod(c, 2)
+            cols = slice(half * JC, (half + count) * JC)
+            h_bf[c] = ring.tile([P, count * JC, 4], BF16, name="h_bf", tag="h_bf", align_bytes=64)
+            engine.tensor_tensor(h_bf[c][:], silu[pair][:, cols, :], gain_full[c // NJ][:, cols, :], MULT)
+
+        def quantise_h(c, count):
+            pair, half = divmod(c, 2)
+            cols = slice(half * JC, (half + count) * JC)
+            if half == 0:
+                h_codes[pair] = held([P, 2 * JC], U32, "h_codes%d" % pair)
+                h_plane[pair] = held([P, 2 * JC], U8, "h_plane%d" % pair)
             nc.vector.quantize_mx(
-                out=h_codes[c][:].bitcast(FP8X4), scales=h_plane[c][:],
+                out=h_codes[pair][:, cols].bitcast(FP8X4), scales=h_plane[pair][:, cols],
                 in_=h_bf[c][:].rearrange("p j t -> p (j t)"),
             )
 
-        def last_product(jq):
-            bank = psum.tile([P, 2, JC], F32, name="out_bank", tag="out")
+        def last_product(jq, count):
+            width = count * JC
+            within = slice(jq % 2 * JC, jq % 2 * JC + width)
+            bank = psum.tile([P, 2, width], F32, name="out_bank", tag="out")
             for nt in range(2):
                 cols = slice(nt * P, (nt + 1) * P)
                 for b in range(NB):
-                    c = b * NJ + jq
+                    pair = (b * NJ + jq) // 2
                     nc.tensor.matmul_mx(
                         bank[:, nt, :], lhsT=wo_codes[b][:, cols].bitcast(FP8X4), lhsT_scale=wo_plane[b][:, cols],
-                        rhs=h_codes[c][:].bitcast(FP8X4), rhs_scale=h_plane[c][:],
+                        rhs=h_codes[pair][:, within].bitcast(FP8X4), rhs_scale=h_plane[pair][:, within],
                         start=(b == 0), stop=(b == NB - 1),
                     )
-            result = ring.tile([P, 2, JC], F32, name="result", tag="result")
+            result = ring.tile([P, 2, width], F32, name="result", tag="result")
             nc.scalar.copy(result[:], bank[:])
             nc.sync.dma_start(
-                out=out.rearrange("(nt p) j -> p nt j", p=P)[:, :, jq * JC : (jq + 1) * JC], in_=result[:]
+                out=out.rearrange("(nt p) j -> p nt j", p=P)[:, :, jq * JC : jq * JC + width], in_=result[:]
             )
 
         for c in range(GATE_AHEAD):
@@ -308,7 +319,7 @@ def tile_list_kinase_selectivity_kernel(
         load_wo(1)
 
         gate_pocket(0)
-        for c in range(NCHUNK + 2):
+        for c in range(NCHUNK):
             if c == 2:
                 cast_wg(1)
                 quantise_wg(1)
@@ -321,9 +332,15 @@ def tile_list_kinase_selectivity_kernel(
             if c + 1 < NCHUNK:
                 products(c + 1)
                 gate_pocket(c + 1)
-            if c < NCHUNK:
-                add_shift(c)
-            if c >= 2:
-                quantise_h(c - 2)
-            if c - 2 >= NJ:
-                last_product(c - 2 - NJ)
+            add_shift(c)
+            if c % 2 == 1 and c < VECTOR_GAIN_FROM:
+                apply_gain(nc.gpsimd, c - 1, 2)
+            if c % 2 == 1 and c >= 3:
+                quantise_h(c - 3, 2)
+                if c - 3 >= NJ:
+                    last_product(c - 3 - NJ, 2)
+        for c in range(VECTOR_GAIN_FROM, NCHUNK):
+            apply_gain(nc.vector, c, 1)
+        for c in range(VECTOR_GAIN_FROM, NCHUNK):
+            quantise_h(c, 1)
+            last_product(c - NJ, 1)

@@ -24,16 +24,17 @@ NJ = S // JC
 NB = H // 512
 NCHUNK = NB * NJ
 PIECE = 512
-GATE_AHEAD = 2
+PRODUCTS_AHEAD = 2
+LATE_GATES_FROM = 4
+QUANTISE_BEHIND = 6
 VECTOR_GAIN_FROM = 14
 PLACE_KIB = {
-    "tab2_w": 0, "wg_raw1": 0,
-    "tab_w0": 24, "words_raw0": 21, "v_picked": 30, "wg_codes0": 28.5, "tab_w1": 30.5,
-    "wo_raw0": 21, "silu3": 21, "words_raw1": 30.5, "wo_raw1": 34.5, "gated9": 34.5,
-    "tab_s": 40, "v2_picked": 40,
-    "tab2_s": 46, "v2_words0": 44.5, "v2_words1": 46.5, "staged": 49, "wg_raw0": 50,
-    "ws_raw": 60, "w4_codes0": 59, "w8_codes0": 61,
+    "wg_raw0": 0, "tab_s": 7.5, "words_raw0": 9,
+    "tab2_s": 14, "tab_w0": 17.5,
+    "words_raw1": 16, "wo_raw0": 20, "wo_raw1": 24,
+    "tab2_w": 28, "tab_w1": 28, "wg_raw1": 36,
 }
+V0, V2, W8, W4A, W4B, V1 = range(6)
 
 
 def tile_list_kinase_selectivity_kernel(
@@ -43,9 +44,9 @@ def tile_list_kinase_selectivity_kernel(
     nc = tc.nc
     with ExitStack() as ctx:
         keep = ctx.enter_context(tc.tile_pool(name="keep", bufs=1))
-        ring = ctx.enter_context(tc.tile_pool(name="ring", bufs=3))
+        ring = ctx.enter_context(tc.tile_pool(name="ring", bufs=4))
         arena = ctx.enter_context(tc.tile_pool(name="arena", bufs=1))
-        psum = ctx.enter_context(tc.psum_pool(name="psum", bufs=2))
+        psum = ctx.enter_context(tc.psum_pool(name="psum", bufs=3))
 
         def held(shape, dtype, name):
             if name in PLACE_KIB:
@@ -56,57 +57,60 @@ def tile_list_kinase_selectivity_kernel(
         list2 = keep.tile([P, S // 16], U16, name="list2")
         tab_s = held([P, T], U8, "tab_s")
         tab2_s = held([P, T2], U8, "tab2_s")
-        ws_raw = held([P, 2, H], U8, "ws_raw")
+        ws_raw = held([P, 3, H], U8, "ws_raw")
         planes = held([P, 6, S], U8, "planes")
         gain_rows = held([P, P], F32, "gain_rows")
         ident = held([P, P], F32, "ident")
         wg_raw, w4_raw, w8_raw, wo_raw, tab_w = {}, {}, {}, {}, {}
 
-        nc.vector.memset(ws_raw[:].bitcast(I32), 0)
-        nc.vector.memset(tab_s[:].bitcast(I32), 0)
+        nc.gpsimd.memset(tab_s[:].bitcast(I32), 0)
         nc.vector.memset(tab2_s[:].bitcast(I32), 0)
-        nc.vector.memset(planes[:].bitcast(I32), 0)
+        nc.vector.memset(ws_raw[:].bitcast(I32), 0)
         nc.gpsimd.memset(gain_rows[:], 0.0)
 
         def load_wg(b):
+            wg_raw[b] = held([P, 4, 512], F32, "wg_raw%d" % b)
             nc.sync.dma_start(
-                out=wg_raw[b], in_=wg.rearrange("(p j) c -> p j c", j=4)[:, :, 512 * b : 512 * (b + 1)]
+                out=wg_raw[b][:], in_=wg.rearrange("(p j) c -> p j c", j=4)[:, :, 512 * b : 512 * (b + 1)]
             )
 
         def load_words(b):
-            nc.sync.dma_start(
-                out=w4_raw[b],
-                in_=w4_words.bitcast(I32).rearrange("a p c -> p a c")[:, :, 256 * b : 256 * (b + 1)],
-            )
+            raw = held([P, 1024], I32, "words_raw%d" % b)
+            w4_raw[b] = raw[:, 0:512].rearrange("p (a c) -> p a c", a=2)
+            w8_raw[b] = raw[:, 512:1024]
             nc.sync.dma_start(
                 out=w8_raw[b],
                 in_=w8_words[0].rearrange("p c i -> p (c i)").bitcast(I32)[:, 512 * b : 512 * (b + 1)],
             )
+            nc.sync.dma_start(
+                out=w4_raw[b],
+                in_=w4_words.bitcast(I32).rearrange("a p c -> p a c")[:, :, 256 * b : 256 * (b + 1)],
+            )
 
-        def take_words_tile(b):
-            raw = held([P, 1024], I32, "words_raw%d" % b)
-            w4_raw[b] = raw[:, 0:512].rearrange("p (a c) -> p a c", a=2)
-            w8_raw[b] = raw[:, 512:1024]
-            load_words(b)
-
-        def load_table(tile, words):
+        def load_table(name, words, width):
+            tile = held([P, width], U32, name)
             nc.sync.dma_start(out=tile[:].bitcast(I32), in_=words.rearrange("p t i -> p (t i)").bitcast(I32))
+            return tile
 
-        tab_w[0] = held([P, T], U32, "tab_w0")
-        wg_raw[0] = held([P, 4, 512], F32, "wg_raw0")[:]
+        def load_wo(b):
+            wo_raw[b] = held([P, 4, N], F32, "wo_raw%d" % b)
+            rows = wo[512 * b : 512 * (b + 1), :].rearrange("(u t e) n -> e u t n", t=4, e=4)
+            for e in range(4):
+                nc.sync.dma_start(out=wo_raw[b][e:P:4, :, :], in_=rows[e])
+
         nc.sync.dma_start(lists[:], offs)
-        load_table(tab_w[0], tab_words[0])
         nc.sync.dma_start(list2[:], offs2)
-        load_wg(0)
-        tab2_w = held([P, T2], U32, "tab2_w")
-        load_table(tab2_w, tab2_words[0])
+        tab2_w = load_table("tab2_w", tab2_words[0], T2)
+        tab_s32 = tab_s[:].bitcast(I32)
+        nc.scalar.dma_start(out=tab_s32[0:P:8, :], in_=tab_scales[0].bitcast(I32))
+        second = tab_scales[1].bitcast(I32).rearrange("(i o) c -> o i c", o=2)
+        nc.scalar.dma_start(out=tab_s32[4:P:16, :], in_=second[0])
+        nc.scalar.dma_start(out=tab_s32[1:P:16, :], in_=second[1])
+        nc.scalar.dma_start(out=tab2_s[:].bitcast(I32)[0:P:8, :], in_=tab2_scales[0].bitcast(I32))
         nc.scalar.dma_start(out=ws_raw[:].bitcast(I32)[0:P:8, 0, :], in_=w8_scales[0].bitcast(I32))
         nc.scalar.dma_start(
-            out=ws_raw[:].bitcast(I32)[1:P:8, :, :], in_=w4_scales.bitcast(I32).rearrange("a q c -> q a c")
+            out=ws_raw[:].bitcast(I32)[0:P:8, 1:3, :], in_=w4_scales.bitcast(I32).rearrange("a q c -> q a c")
         )
-        for a in range(2):
-            nc.scalar.dma_start(out=tab_s[:].bitcast(I32)[a:P:8, :], in_=tab_scales[a].bitcast(I32))
-        nc.scalar.dma_start(out=tab2_s[:].bitcast(I32)[0:P:8, :], in_=tab2_scales[0].bitcast(I32))
         for b in range(NB):
             nc.gpsimd.dma_start(
                 out=gain_rows[4 * b : 4 * b + 4, :].rearrange("t (u e) -> t u e", e=4),
@@ -114,14 +118,15 @@ def tile_list_kinase_selectivity_kernel(
             )
         make_identity(nc, ident[:])
 
-        wg_bf = {}
+        wg_bf, wo_bf = {}, {}
         wg_codes, wg_plane, w4_codes, w8_codes, wo_codes, wo_plane = {}, {}, {}, {}, {}, {}
 
-        def cast_wg(b):
-            wg_bf[b] = held([P, 4, P, 4], BF16, "wg_bf%d" % b)
+        def cast_wg(b, slots):
+            if b not in wg_bf:
+                wg_bf[b] = held([P, 4, P, 4], BF16, "wg_bf%d" % b)
             nc.scalar.copy(
-                wg_bf[b][:].rearrange("p t (u e) j -> p t u e j", e=4),
-                wg_raw[b].rearrange("p j (u t e) -> p t u e j", t=4, e=4),
+                wg_bf[b][:].rearrange("p t (u e) j -> p t u j e", e=4)[:, slots],
+                wg_raw[b][:].rearrange("p j (u t e) -> p t u j e", t=4, e=4)[:, slots],
             )
 
         def quantise_wg(b):
@@ -133,76 +138,78 @@ def tile_list_kinase_selectivity_kernel(
             )
 
         def order_words(b):
-            w4_codes[b] = held([P, 2, 4, 256], U8, "w4_codes%d" % b)
-            nc.vector.tensor_copy(
-                w4_codes[b][:].bitcast(I32).rearrange("p a t (u w) -> p a t u w", w=2),
-                w4_raw[b].rearrange("p a (u t w) -> p a t u w", t=4, w=2),
-            )
             w8_codes[b] = held([P, 4, P], U32, "w8_codes%d" % b)
             nc.vector.tensor_copy(
                 w8_codes[b][:].bitcast(I32).rearrange("p t (u e) -> p t u e", e=4),
                 w8_raw[b].rearrange("p (u t e) -> p t u e", t=4, e=4),
             )
+            w4_codes[b] = held([P, 2, 4, 256], U8, "w4_codes%d" % b)
+            nc.vector.tensor_copy(
+                w4_codes[b][:].bitcast(I32).rearrange("p a t (u w) -> p a t u w", w=2),
+                w4_raw[b].rearrange("p a (u t w) -> p a t u w", t=4, w=2),
+            )
 
         def cast_wo(b):
-            grouped = held([P, N, 4], BF16, "wo_bf%d" % b)
-            if b == 0:
-                nc.scalar.copy(grouped[:], wo_raw[b].rearrange("p t n -> p n t"))
-            else:
-                nc.vector.tensor_copy(grouped[:], wo_raw[b].rearrange("p t n -> p n t"))
+            wo_bf[b] = held([P, N, 4], BF16, "wo_bf%d" % b)
+            nc.scalar.copy(
+                wo_bf[b][:].rearrange("p (c i) t -> p c t i", i=4),
+                wo_raw[b][:].rearrange("p t (c i) -> p c t i", i=4),
+            )
+
+        def quantise_wo(b):
             wo_codes[b] = held([P, N], U32, "wo_codes%d" % b)
             wo_plane[b] = held([P, N], U8, "wo_plane%d" % b)
             nc.vector.quantize_mx(
                 out=wo_codes[b][:].bitcast(FP8X4), scales=wo_plane[b][:],
-                in_=grouped[:].rearrange("p n t -> p (n t)"),
+                in_=wo_bf[b][:].rearrange("p n t -> p (n t)"),
             )
 
-        def gather_words(window, offsets, piece, name):
-            picked = held([P, PIECE], U32, name)
-            cols = slice(piece * PIECE // 16, (piece + 1) * PIECE // 16)
-            nc.vector.tensor_copy(picked[:], window[:].indirect(offsets[:, cols]))
-            return picked
+        def gather_words(window, offsets, name):
+            pieces = []
+            for piece in range(S // PIECE):
+                picked = held([P, PIECE], U32, "%s%d" % (name, piece))
+                cols = slice(piece * PIECE // 16, (piece + 1) * PIECE // 16)
+                nc.vector.tensor_copy(picked[:], window[:].indirect(offsets[:, cols]))
+                pieces.append(picked)
+            return pieces
 
-        v2_plane, v_plane = planes[:, 0, :], [planes[:, 1, :], planes[:, 3, :]]
-        w8_plane, w4_plane = planes[:, 2, :], [planes[:, 4, :], planes[:, 5, :]]
-        v_words = [[None, None], [None, None]]
-        v_words[0][0] = gather_words(tab_w[0], lists, 0, "v_words00")
-        v_words[0][1] = gather_words(tab_w[0], lists, 1, "v_words01")
-        take_words_tile(0)
+        planes32 = planes[:].bitcast(I32)
         v_picked = held([P, S], U8, "v_picked")
         nc.vector.tensor_copy(v_picked[:], tab_s[:].indirect(lists[:]))
+        load_wg(0)
+        load_words(0)
         v2_picked = held([P, S], U8, "v2_picked")
         nc.vector.tensor_copy(v2_picked[:], tab2_s[:].indirect(list2[:]))
-        cast_wg(0)
-        staged = held([P, 4, S], U8, "staged")
+        tab_w[0] = load_table("tab_w0", tab_words[0], T)
+        nc.vector.tensor_copy(planes32[:, V0, :], v_picked[:].bitcast(I32))
+        nc.vector.tensor_copy(planes32[:, V1, :], v_picked[:].bitcast(I32))
         nc.vector.tensor_copy(
-            staged[:].bitcast(I32)[:, 2:4, :].rearrange("p x (b t u) -> p (x b) t u", b=NB, t=4),
+            planes32[:, W8 : W4B + 1, :].rearrange("p x (b t u) -> p (x b) t u", b=NB, t=4),
             ws_raw[:].bitcast(I32).rearrange("p x (b u t) -> p (x b) t u", b=NB, t=4),
         )
-        nc.vector.tensor_copy(staged[:].bitcast(I32)[:, 0, :], v2_picked[:].bitcast(I32))
-        nc.vector.tensor_copy(staged[:].bitcast(I32)[:, 1, :], v_picked[:].bitcast(I32))
-        for x in range(2):
-            for r in range(4):
-                nc.scalar.dma_start(
-                    out=planes[:].bitcast(I32)[r:P:32, 3 * x : 3 * x + 3, :],
-                    in_=staged[:].bitcast(I32)[8 * r + x : P : 32, x : x + 3, :],
-                )
-        tab_w[1] = held([P, T], U32, "tab_w1")
-        load_table(tab_w[1], tab_words[1])
-        quantise_wg(0)
-        v2_words = [gather_words(tab2_w, list2, 0, "v2_words0"), None]
-        order_words(0)
-        v2_words[1] = gather_words(tab2_w, list2, 1, "v2_words1")
-        wg_raw[1] = held([P, 4, 512], F32, "wg_raw1")[:]
+        nc.vector.tensor_copy(planes32[:, V2, :], v2_picked[:].bitcast(I32))
+        for r in range(1, 4):
+            nc.scalar.dma_start(out=planes32[r:P:32, 0:V1, :], in_=planes32[8 * r : P : 32, 0:V1, :])
+        for r, source in ((0, 4), (2, 20), (3, 17)):
+            nc.scalar.dma_start(out=planes32[r:P:32, V1, :], in_=planes32[source:P:32, V1, :])
+        v2_plane, v_plane = planes[:, V2, :], [planes[:, V0, :], planes[:, V1, :]]
+        w8_plane, w4_plane = planes[:, W8, :], [planes[:, W4A, :], planes[:, W4B, :]]
+
+        v2_words = gather_words(tab2_w, list2, "v2_words")
+        tab_w[1] = load_table("tab_w1", tab_words[1], T)
         load_wg(1)
 
-        gain_ps = psum.tile([P, 512], F32, name="gain_ps", tag="out")
+        gain_ps = psum.tile([P, 512], F32, name="gain_ps", tag="gate", bufs=2)
         nc.tensor.transpose(gain_ps[:, 0:P], gain_rows[:], ident[:])
         gain_full = [held([P, 2 * JC, 4], F32, "gain_full%d" % b) for b in range(NB)]
         for b in range(NB):
             nc.scalar.activation(
                 gain_full[b][:], gain_ps[:, 4 * b : 4 * b + 4].unsqueeze(1).to_broadcast([P, 2 * JC, 4]), ACT.Copy
             )
+
+        cast_wg(0, slice(0, 4))
+        order_words(0)
+        quantise_wg(0)
 
         tanh_half, pocket, shift, gated, silu, h_bf, h_codes, h_plane = {}, {}, {}, {}, {}, {}, {}, {}
 
@@ -214,7 +221,7 @@ def tile_list_kinase_selectivity_kernel(
         def gate_stage(c):
             b, jq = divmod(c, NJ)
             rhs, rhs_scale = moving(v2_words, v2_plane, jq)
-            bank = psum.tile([P, 4, JC], F32, name="gate", tag="gate")
+            bank = psum.tile([P, 4, JC], F32, name="gate", tag="gate", bufs=2)
             for t in range(4):
                 cols = slice(t * P, (t + 1) * P)
                 nc.tensor.matmul_mx(
@@ -245,10 +252,7 @@ def tile_list_kinase_selectivity_kernel(
                 )
 
         def gate_pocket(c):
-            if "gated%d" % c in PLACE_KIB:
-                gated[c] = held([P, JC, 4], F32, "gated%d" % c)
-            else:
-                gated[c] = ring.tile([P, JC, 4], F32, name="gated", tag="gated")
+            gated[c] = ring.tile([P, JC, 4], F32, name="gated", tag="gated")
             nc.vector.scalar_tensor_tensor(
                 gated[c][:], tanh_half[c][:], 1.0, pocket[c][:].rearrange("p t j -> p j t"), ADD, MULT
             )
@@ -260,10 +264,7 @@ def tile_list_kinase_selectivity_kernel(
                 mixed[:], gated[c][:], 0.5, shift[c][:].rearrange("p t j -> p j t"), MULT, ADD
             )
             if half == 0:
-                if "silu%d" % pair in PLACE_KIB:
-                    silu[pair] = held([P, 2 * JC, 4], F32, "silu%d" % pair)
-                else:
-                    silu[pair] = ring.tile([P, 2 * JC, 4], F32, name="silu", tag="silu")
+                silu[pair] = ring.tile([P, 2 * JC, 4], F32, name="silu", tag="silu")
             nc.scalar.activation(silu[pair][:, half * JC : (half + 1) * JC, :], mixed[:], ACT.Silu)
 
         def apply_gain(engine, c, count):
@@ -282,11 +283,13 @@ def tile_list_kinase_selectivity_kernel(
                 out=h_codes[pair][:, cols].bitcast(FP8X4), scales=h_plane[pair][:, cols],
                 in_=h_bf[c][:].rearrange("p j t -> p (j t)"),
             )
+            if c >= NJ:
+                last_product(c - NJ, count)
 
         def last_product(jq, count):
             width = count * JC
             within = slice(jq % 2 * JC, jq % 2 * JC + width)
-            bank = psum.tile([P, 2, width], F32, name="out_bank", tag="out")
+            bank = psum.tile([P, 2, width], F32, name="out_bank", tag="gate", bufs=2)
             for nt in range(2):
                 cols = slice(nt * P, (nt + 1) * P)
                 for b in range(NB):
@@ -296,51 +299,48 @@ def tile_list_kinase_selectivity_kernel(
                         rhs=h_codes[pair][:, within].bitcast(FP8X4), rhs_scale=h_plane[pair][:, within],
                         start=(b == 0), stop=(b == NB - 1),
                     )
-            result = ring.tile([P, 2, width], F32, name="result", tag="result")
+            result = held([P, 2, width], F32, "result%d" % jq)
             nc.scalar.copy(result[:], bank[:])
             nc.sync.dma_start(
                 out=out.rearrange("(nt p) j -> p nt j", p=P)[:, :, jq * JC : jq * JC + width], in_=result[:]
             )
 
-        for c in range(GATE_AHEAD):
+        for c in range(NJ):
             gate_stage(c)
+        v_words = [gather_words(tab_w[0], lists, "v_words0")]
+        load_words(1)
+        for b in range(NB):
+            load_wo(b)
+        v_words.append(gather_words(tab_w[1], lists, "v_words1"))
 
-        def load_wo(b):
-            wo_raw[b] = held([P, 4, N], F32, "wo_raw%d" % b)[:]
-            rows = wo[512 * b : 512 * (b + 1), :].rearrange("(u t e) n -> e u t n", t=4, e=4)
-            for e in range(4):
-                nc.sync.dma_start(out=wo_raw[b][e:P:4, :, :], in_=rows[e])
-
-        load_wo(0)
-        v_words[1][0] = gather_words(tab_w[1], lists, 0, "v_words10")
-        products(0)
-        v_words[1][1] = gather_words(tab_w[1], lists, 1, "v_words11")
-        take_words_tile(1)
-        load_wo(1)
-
+        for c in range(PRODUCTS_AHEAD):
+            products(c)
         gate_pocket(0)
         for c in range(NCHUNK):
-            if c == 2:
-                cast_wg(1)
-                quantise_wg(1)
             if c == 3:
                 order_words(1)
+            if c == LATE_GATES_FROM:
+                quantise_wg(1)
+            if LATE_GATES_FROM <= c < LATE_GATES_FROM + NJ:
+                gate_stage(NJ + c - LATE_GATES_FROM)
+            if c + PRODUCTS_AHEAD < NCHUNK:
+                products(c + PRODUCTS_AHEAD)
+            if c + 1 < NCHUNK:
+                gate_pocket(c + 1)
+            if c % 2 == 0 and c >= QUANTISE_BEHIND:
+                quantise_h(c - QUANTISE_BEHIND, 2)
+            if c in (8, 10):
+                quantise_wo((c - 8) // 2)
+            add_shift(c)
+            if c < 4:
+                cast_wg(1, slice(c, c + 1))
             if c in (5, 7):
                 cast_wo((c - 5) // 2)
-            if c + GATE_AHEAD < NCHUNK:
-                gate_stage(c + GATE_AHEAD)
-            if c + 1 < NCHUNK:
-                products(c + 1)
-                gate_pocket(c + 1)
-            add_shift(c)
             if c % 2 == 1 and c < VECTOR_GAIN_FROM:
                 apply_gain(nc.gpsimd, c - 1, 2)
-            if c % 2 == 1 and c >= 3:
-                quantise_h(c - 3, 2)
-                if c - 3 >= NJ:
-                    last_product(c - 3 - NJ, 2)
+        quantise_h(10, 2)
         for c in range(VECTOR_GAIN_FROM, NCHUNK):
             apply_gain(nc.vector, c, 1)
+        quantise_h(12, 2)
         for c in range(VECTOR_GAIN_FROM, NCHUNK):
             quantise_h(c, 1)
-            last_product(c - NJ, 1)

@@ -29,10 +29,9 @@ LATE_GATES_FROM = 4
 QUANTISE_BEHIND = 6
 VECTOR_GAIN_FROM = 14
 PLACE_KIB = {
-    "wg_raw0": 0, "tab_s": 7.5, "words_raw0": 9,
-    "tab2_s": 14, "tab_w0": 17.5,
-    "words_raw1": 16, "wo_raw0": 20, "wo_raw1": 24,
-    "tab2_w": 28, "tab_w1": 28, "wg_raw1": 36,
+    "words_raw0": 0, "tab2_w": 3, "words_raw1": 4, "wo_raw0": 8, "wo_raw1": 12,
+    "tab_s": 20, "tab_w0": 21.5,
+    "tab_w1": 30, "v2_picked": 37.5, "wg_raw1": 38,
 }
 V0, V2, W8, W4A, W4B, V1 = range(6)
 
@@ -100,7 +99,8 @@ def tile_list_kinase_selectivity_kernel(
 
         nc.sync.dma_start(lists[:], offs)
         nc.sync.dma_start(list2[:], offs2)
-        tab2_w = load_table("tab2_w", tab2_words[0], T2)
+        load_words(0)
+        load_wg(0)
         tab_s32 = tab_s[:].bitcast(I32)
         nc.scalar.dma_start(out=tab_s32[0:P:8, :], in_=tab_scales[0].bitcast(I32))
         second = tab_scales[1].bitcast(I32).rearrange("(i o) c -> o i c", o=2)
@@ -173,14 +173,15 @@ def tile_list_kinase_selectivity_kernel(
                 pieces.append(picked)
             return pieces
 
+        order_words(0)
+        tab2_w = load_table("tab2_w", tab2_words[0], T2)
+        cast_wg(0, slice(0, 4))
         planes32 = planes[:].bitcast(I32)
         v_picked = held([P, S], U8, "v_picked")
         nc.vector.tensor_copy(v_picked[:], tab_s[:].indirect(lists[:]))
-        load_wg(0)
-        load_words(0)
+        tab_w[0] = load_table("tab_w0", tab_words[0], T)
         v2_picked = held([P, S], U8, "v2_picked")
         nc.vector.tensor_copy(v2_picked[:], tab2_s[:].indirect(list2[:]))
-        tab_w[0] = load_table("tab_w0", tab_words[0], T)
         nc.vector.tensor_copy(planes32[:, V0, :], v_picked[:].bitcast(I32))
         nc.vector.tensor_copy(planes32[:, V1, :], v_picked[:].bitcast(I32))
         nc.vector.tensor_copy(
@@ -189,15 +190,19 @@ def tile_list_kinase_selectivity_kernel(
         )
         nc.vector.tensor_copy(planes32[:, V2, :], v2_picked[:].bitcast(I32))
         for r in range(1, 4):
-            nc.scalar.dma_start(out=planes32[r:P:32, 0:V1, :], in_=planes32[8 * r : P : 32, 0:V1, :])
+            nc.sync.dma_start(out=planes32[r:P:32, 0:V1, :], in_=planes32[8 * r : P : 32, 0:V1, :])
         for r, source in ((0, 4), (2, 20), (3, 17)):
-            nc.scalar.dma_start(out=planes32[r:P:32, V1, :], in_=planes32[source:P:32, V1, :])
+            nc.sync.dma_start(out=planes32[r:P:32, V1, :], in_=planes32[source:P:32, V1, :])
         v2_plane, v_plane = planes[:, V2, :], [planes[:, V0, :], planes[:, V1, :]]
         w8_plane, w4_plane = planes[:, W8, :], [planes[:, W4A, :], planes[:, W4B, :]]
 
-        v2_words = gather_words(tab2_w, list2, "v2_words")
         tab_w[1] = load_table("tab_w1", tab_words[1], T)
         load_wg(1)
+        quantise_wg(0)
+        v2_words = gather_words(tab2_w, list2, "v2_words")
+        load_words(1)
+        for b in range(NB):
+            load_wo(b)
 
         gain_ps = psum.tile([P, 512], F32, name="gain_ps", tag="gate", bufs=2)
         nc.tensor.transpose(gain_ps[:, 0:P], gain_rows[:], ident[:])
@@ -206,10 +211,6 @@ def tile_list_kinase_selectivity_kernel(
             nc.scalar.activation(
                 gain_full[b][:], gain_ps[:, 4 * b : 4 * b + 4].unsqueeze(1).to_broadcast([P, 2 * JC, 4]), ACT.Copy
             )
-
-        cast_wg(0, slice(0, 4))
-        order_words(0)
-        quantise_wg(0)
 
         tanh_half, pocket, shift, gated, silu, h_bf, h_codes, h_plane = {}, {}, {}, {}, {}, {}, {}, {}
 
@@ -308,9 +309,6 @@ def tile_list_kinase_selectivity_kernel(
         for c in range(NJ):
             gate_stage(c)
         v_words = [gather_words(tab_w[0], lists, "v_words0")]
-        load_words(1)
-        for b in range(NB):
-            load_wo(b)
         v_words.append(gather_words(tab_w[1], lists, "v_words1"))
 
         for c in range(PRODUCTS_AHEAD):

@@ -1,7 +1,6 @@
 from contextlib import ExitStack
 
 import concourse.mybir as mybir
-from concourse.masks import make_identity
 
 K, K2, T, T2, S, H, N = 1024, 512, 2048, 4096, 1024, 1024, 256
 FLOPS = 2 * S * (K * H + 2 * K2 * H + H * N)
@@ -26,12 +25,12 @@ NCHUNK = NB * NJ
 PIECE = 512
 PRODUCTS_AHEAD = 2
 LATE_GATES_FROM = 4
-QUANTISE_BEHIND = 6
+QUANTISE_BEHIND = 4
 VECTOR_GAIN_FROM = 14
 PLACE_KIB = {
     "words_raw0": 0, "tab2_w": 3, "words_raw1": 4, "wo_raw0": 8, "wo_raw1": 12,
     "tab_s": 20, "tab_w0": 21.5,
-    "tab_w1": 30, "v2_picked": 37.5, "wg_raw1": 38,
+    "tab_w1": 29.75, "v2_picked": 37.5, "gains": 37.75, "wg_raw1": 38,
 }
 V0, V2, W8, W4A, W4B, V1 = range(6)
 
@@ -58,14 +57,11 @@ def tile_list_kinase_selectivity_kernel(
         tab2_s = held([P, T2], U8, "tab2_s")
         ws_raw = held([P, 3, H], U8, "ws_raw")
         planes = held([P, 6, S], U8, "planes")
-        gain_rows = held([P, P], F32, "gain_rows")
-        ident = held([P, P], F32, "ident")
         wg_raw, w4_raw, w8_raw, wo_raw, tab_w = {}, {}, {}, {}, {}
 
         nc.gpsimd.memset(tab_s[:].bitcast(I32), 0)
         nc.vector.memset(tab2_s[:].bitcast(I32), 0)
         nc.vector.memset(ws_raw[:].bitcast(I32), 0)
-        nc.gpsimd.memset(gain_rows[:], 0.0)
 
         def load_wg(b):
             wg_raw[b] = held([P, 4, 512], F32, "wg_raw%d" % b)
@@ -111,12 +107,6 @@ def tile_list_kinase_selectivity_kernel(
         nc.scalar.dma_start(
             out=ws_raw[:].bitcast(I32)[0:P:8, 1:3, :], in_=w4_scales.bitcast(I32).rearrange("a q c -> q a c")
         )
-        for b in range(NB):
-            nc.gpsimd.dma_start(
-                out=gain_rows[4 * b : 4 * b + 4, :].rearrange("t (u e) -> t u e", e=4),
-                in_=gain[512 * b : 512 * (b + 1)].rearrange("(u t e) -> t u e", t=4, e=4),
-            )
-        make_identity(nc, ident[:])
 
         wg_bf, wo_bf = {}, {}
         wg_codes, wg_plane, w4_codes, w8_codes, wo_codes, wo_plane = {}, {}, {}, {}, {}, {}
@@ -197,20 +187,16 @@ def tile_list_kinase_selectivity_kernel(
         w8_plane, w4_plane = planes[:, W8, :], [planes[:, W4A, :], planes[:, W4B, :]]
 
         tab_w[1] = load_table("tab_w1", tab_words[1], T)
+        gains = held([P, NB, 16], F32, "gains")
+        gain_runs = gain.rearrange("(b u x) -> u b x", b=NB, x=16)
+        for e in range(4):
+            nc.sync.dma_start(out=gains[e:P:4, :, 0:13], in_=gain_runs[:, :, e : e + 13])
         load_wg(1)
         quantise_wg(0)
         v2_words = gather_words(tab2_w, list2, "v2_words")
         load_words(1)
         for b in range(NB):
             load_wo(b)
-
-        gain_ps = psum.tile([P, 512], F32, name="gain_ps", tag="gate", bufs=2)
-        nc.tensor.transpose(gain_ps[:, 0:P], gain_rows[:], ident[:])
-        gain_full = [held([P, 2 * JC, 4], F32, "gain_full%d" % b) for b in range(NB)]
-        for b in range(NB):
-            nc.scalar.activation(
-                gain_full[b][:], gain_ps[:, 4 * b : 4 * b + 4].unsqueeze(1).to_broadcast([P, 2 * JC, 4]), ACT.Copy
-            )
 
         tanh_half, pocket, shift, gated, silu, h_bf, h_codes, h_plane = {}, {}, {}, {}, {}, {}, {}, {}
 
@@ -272,7 +258,7 @@ def tile_list_kinase_selectivity_kernel(
             pair, half = divmod(c, 2)
             cols = slice(half * JC, (half + count) * JC)
             h_bf[c] = ring.tile([P, count * JC, 4], BF16, name="h_bf", tag="h_bf", align_bytes=64)
-            engine.tensor_tensor(h_bf[c][:], silu[pair][:, cols, :], gain_full[c // NJ][:, cols, :], MULT)
+            engine.tensor_tensor(h_bf[c][:], silu[pair][:, cols, :], gains[:, c // NJ, 0:13:4].unsqueeze(1).to_broadcast([P, count * JC, 4]), MULT)
 
         def quantise_h(c, count):
             pair, half = divmod(c, 2)
@@ -334,11 +320,10 @@ def tile_list_kinase_selectivity_kernel(
                 cast_wg(1, slice(c, c + 1))
             if c in (5, 7):
                 cast_wo((c - 5) // 2)
-            if c % 2 == 1 and c < VECTOR_GAIN_FROM:
-                apply_gain(nc.gpsimd, c - 1, 2)
-        quantise_h(10, 2)
+            if c % 2 == 0 and c >= 2:
+                apply_gain(nc.vector, c - 2, 2)
+        quantise_h(12, 2)
         for c in range(VECTOR_GAIN_FROM, NCHUNK):
             apply_gain(nc.vector, c, 1)
-        quantise_h(12, 2)
         for c in range(VECTOR_GAIN_FROM, NCHUNK):
             quantise_h(c, 1)

@@ -30,7 +30,7 @@ VECTOR_GAIN_FROM = 14
 PLACE_KIB = {
     "words_raw0": 0, "tab2_w": 3, "words_raw1": 4, "wo_raw0": 8, "wo_raw1": 12,
     "tab_s": 20, "tab_w0": 21.5,
-    "tab_w1": 29.75, "v2_picked": 37.5, "gains": 37.75, "wg_raw1": 38,
+    "tab_w1": 29.75, "v2_picked": 37.5, "gain_raw": 37.75, "wg_raw1": 38,
 }
 V0, V2, W8, W4A, W4B, V1 = range(6)
 
@@ -187,10 +187,10 @@ def tile_list_kinase_selectivity_kernel(
         w8_plane, w4_plane = planes[:, W8, :], [planes[:, W4A, :], planes[:, W4B, :]]
 
         tab_w[1] = load_table("tab_w1", tab_words[1], T)
-        gains = held([P, NB, 16], F32, "gains")
+        gain_raw = held([P, NB, 16], F32, "gain_raw")
         gain_runs = gain.rearrange("(b u x) -> u b x", b=NB, x=16)
         for e in range(4):
-            nc.sync.dma_start(out=gains[e:P:4, :, 0:13], in_=gain_runs[:, :, e : e + 13])
+            nc.sync.dma_start(out=gain_raw[e:P:4, :, 0:13], in_=gain_runs[:, :, e : e + 13])
         load_wg(1)
         quantise_wg(0)
         v2_words = gather_words(tab2_w, list2, "v2_words")
@@ -258,7 +258,7 @@ def tile_list_kinase_selectivity_kernel(
             pair, half = divmod(c, 2)
             cols = slice(half * JC, (half + count) * JC)
             h_bf[c] = ring.tile([P, count * JC, 4], BF16, name="h_bf", tag="h_bf", align_bytes=64)
-            engine.tensor_tensor(h_bf[c][:], silu[pair][:, cols, :], gains[:, c // NJ, 0:13:4].unsqueeze(1).to_broadcast([P, count * JC, 4]), MULT)
+            engine.tensor_tensor(h_bf[c][:], silu[pair][:, cols, :], gains[:, c // NJ, :].unsqueeze(1).to_broadcast([P, count * JC, 4]), MULT)
 
         def quantise_h(c, count):
             pair, half = divmod(c, 2)
@@ -296,6 +296,9 @@ def tile_list_kinase_selectivity_kernel(
             gate_stage(c)
         v_words = [gather_words(tab_w[0], lists, "v_words0")]
         v_words.append(gather_words(tab_w[1], lists, "v_words1"))
+
+        gains = held([P, NB, 4], F32, "gains")
+        nc.scalar.copy(gains[:], gain_raw[:, :, 0:13:4])
 
         for c in range(PRODUCTS_AHEAD):
             products(c)

@@ -25,14 +25,15 @@ NCHUNK = NB * NJ
 PIECE = 512
 PRODUCTS_AHEAD = 2
 LATE_GATES_FROM = 4
-QUANTISE_BEHIND = 4
 VECTOR_GAIN_FROM = 14
+VECTOR_SHARE = 64
 PLACE_KIB = {
-    "words_raw0": 0, "tab2_w": 3, "words_raw1": 4, "wo_raw0": 8, "wo_raw1": 12,
+    "tab2_s": 0, "tab2_w": 3.5, "wo_raw0": 8, "wo_raw1": 12,
     "tab_s": 20, "tab_w0": 21.5,
-    "tab_w1": 29.75, "v2_picked": 37.5, "gain_raw": 37.75, "wg_raw1": 38,
+    "tab_w1": 30, "staged": 37.5, "gain_raw": 38.5, "wg_raw1": 41,
 }
-V0, V2, W8, W4A, W4B, V1 = range(6)
+V2, W8, W4A, W4B = range(4)
+LAST_ROWS = P - 16
 
 
 def tile_list_kinase_selectivity_kernel(
@@ -56,30 +57,19 @@ def tile_list_kinase_selectivity_kernel(
         tab_s = held([P, T], U8, "tab_s")
         tab2_s = held([P, T2], U8, "tab2_s")
         ws_raw = held([P, 3, H], U8, "ws_raw")
-        planes = held([P, 6, S], U8, "planes")
-        wg_raw, w4_raw, w8_raw, wo_raw, tab_w = {}, {}, {}, {}, {}
+        planes = held([P, 4, S], U8, "planes")
+        wg_raw, wo_raw, tab_w = {}, {}, {}
 
         nc.gpsimd.memset(tab_s[:].bitcast(I32), 0)
-        nc.vector.memset(tab2_s[:].bitcast(I32), 0)
-        nc.vector.memset(ws_raw[:].bitcast(I32), 0)
+        nc.vector.memset(tab2_s[:].bitcast(I32)[0:96, :], 0)
+        nc.vector.memset(tab2_s[:].bitcast(I32)[96:LAST_ROWS, :], 0)
+        nc.gpsimd.memset(ws_raw[:].bitcast(I32)[96:LAST_ROWS], 0)
+        nc.gpsimd.memset(planes[:].bitcast(I32), 0)
 
         def load_wg(b):
             wg_raw[b] = held([P, 4, 512], F32, "wg_raw%d" % b)
             nc.sync.dma_start(
                 out=wg_raw[b][:], in_=wg.rearrange("(p j) c -> p j c", j=4)[:, :, 512 * b : 512 * (b + 1)]
-            )
-
-        def load_words(b):
-            raw = held([P, 1024], I32, "words_raw%d" % b)
-            w4_raw[b] = raw[:, 0:512].rearrange("p (a c) -> p a c", a=2)
-            w8_raw[b] = raw[:, 512:1024]
-            nc.sync.dma_start(
-                out=w8_raw[b],
-                in_=w8_words[0].rearrange("p c i -> p (c i)").bitcast(I32)[:, 512 * b : 512 * (b + 1)],
-            )
-            nc.sync.dma_start(
-                out=w4_raw[b],
-                in_=w4_words.bitcast(I32).rearrange("a p c -> p a c")[:, :, 256 * b : 256 * (b + 1)],
             )
 
         def load_table(name, words, width):
@@ -93,23 +83,26 @@ def tile_list_kinase_selectivity_kernel(
             for e in range(4):
                 nc.sync.dma_start(out=wo_raw[b][e:P:4, :, :], in_=rows[e])
 
-        nc.sync.dma_start(lists[:], offs)
         nc.sync.dma_start(list2[:], offs2)
-        load_words(0)
+        nc.sync.dma_start(out=tab2_s[:].bitcast(I32)[LAST_ROWS:P, :], in_=tab2_scales[0].bitcast(I32))
+        nc.sync.dma_start(lists[:], offs)
+        w8_raw = held([P, H], I32, "w8_raw")
+        nc.sync.dma_start(out=w8_raw[:], in_=w8_words[0].rearrange("p c i -> p (c i)").bitcast(I32))
+        w4_raw = held([P, 2, H // 2], I32, "w4_raw")
+        nc.sync.dma_start(out=w4_raw[:], in_=w4_words.bitcast(I32).rearrange("a p c -> p a c"))
         load_wg(0)
         tab_s32 = tab_s[:].bitcast(I32)
         nc.scalar.dma_start(out=tab_s32[0:P:8, :], in_=tab_scales[0].bitcast(I32))
         second = tab_scales[1].bitcast(I32).rearrange("(i o) c -> o i c", o=2)
         nc.scalar.dma_start(out=tab_s32[4:P:16, :], in_=second[0])
         nc.scalar.dma_start(out=tab_s32[1:P:16, :], in_=second[1])
-        nc.scalar.dma_start(out=tab2_s[:].bitcast(I32)[0:P:8, :], in_=tab2_scales[0].bitcast(I32))
-        nc.scalar.dma_start(out=ws_raw[:].bitcast(I32)[0:P:8, 0, :], in_=w8_scales[0].bitcast(I32))
+        nc.scalar.dma_start(out=ws_raw[:].bitcast(I32)[LAST_ROWS:P, 0, :], in_=w8_scales[0].bitcast(I32))
         nc.scalar.dma_start(
-            out=ws_raw[:].bitcast(I32)[0:P:8, 1:3, :], in_=w4_scales.bitcast(I32).rearrange("a q c -> q a c")
+            out=ws_raw[:].bitcast(I32)[LAST_ROWS:P, 1:3, :], in_=w4_scales.bitcast(I32).rearrange("a q c -> q a c")
         )
 
         wg_bf, wo_bf = {}, {}
-        wg_codes, wg_plane, w4_codes, w8_codes, wo_codes, wo_plane = {}, {}, {}, {}, {}, {}
+        wg_codes, wg_plane, wo_codes, wo_plane = {}, {}, {}, {}
 
         def cast_wg(b, slots):
             if b not in wg_bf:
@@ -125,18 +118,6 @@ def tile_list_kinase_selectivity_kernel(
             nc.vector.quantize_mx(
                 out=wg_codes[b][:].bitcast(FP8X4), scales=wg_plane[b][:],
                 in_=wg_bf[b][:].rearrange("p t m j -> p (t m j)"),
-            )
-
-        def order_words(b):
-            w8_codes[b] = held([P, 4, P], U32, "w8_codes%d" % b)
-            nc.vector.tensor_copy(
-                w8_codes[b][:].bitcast(I32).rearrange("p t (u e) -> p t u e", e=4),
-                w8_raw[b].rearrange("p (u t e) -> p t u e", t=4, e=4),
-            )
-            w4_codes[b] = held([P, 2, 4, 256], U8, "w4_codes%d" % b)
-            nc.vector.tensor_copy(
-                w4_codes[b][:].bitcast(I32).rearrange("p a t (u w) -> p a t u w", w=2),
-                w4_raw[b].rearrange("p a (u t w) -> p a t u w", t=4, w=2),
             )
 
         def cast_wo(b):
@@ -163,27 +144,37 @@ def tile_list_kinase_selectivity_kernel(
                 pieces.append(picked)
             return pieces
 
-        order_words(0)
+        v2_picked = held([P, S], U8, "v2_picked")
+        nc.vector.tensor_copy(v2_picked[:], tab2_s[:].indirect(list2[:]))
         tab2_w = load_table("tab2_w", tab2_words[0], T2)
+        staged = held([P, 4, S // 4], I32, "staged")
+        nc.vector.tensor_copy(
+            staged[96:P, W8 : W4B + 1, :].rearrange("p x (b t u) -> p (x b) t u", b=NB, t=4),
+            ws_raw[:].bitcast(I32)[96:P].rearrange("p x (b u t) -> p (x b) t u", b=NB, t=4),
+        )
+        nc.vector.tensor_copy(staged[96:P, V2, :], v2_picked[:].bitcast(I32)[96:P, :])
+        for r in range(4):
+            nc.sync.dma_start(out=planes[:].bitcast(I32)[r:P:32], in_=staged[LAST_ROWS + r : P : 4])
+        w8_codes = held([P, NB, 4, P], U32, "w8_codes")
+        nc.vector.tensor_copy(
+            w8_codes[:].bitcast(I32).rearrange("p b t (u e) -> p b t u e", e=4),
+            w8_raw[:].rearrange("p (b u t e) -> p b t u e", b=NB, t=4, e=4),
+        )
+        w4_codes = held([P, 2, NB, 4, 256], U8, "w4_codes")
+        nc.vector.tensor_copy(
+            w4_codes[:].bitcast(I32).rearrange("p a b t (u w) -> p (a b) t u w", w=2),
+            w4_raw[:].rearrange("p a (b u t w) -> p (a b) t u w", b=NB, t=4, w=2),
+        )
         cast_wg(0, slice(0, 4))
-        planes32 = planes[:].bitcast(I32)
         v_picked = held([P, S], U8, "v_picked")
         nc.vector.tensor_copy(v_picked[:], tab_s[:].indirect(lists[:]))
         tab_w[0] = load_table("tab_w0", tab_words[0], T)
-        v2_picked = held([P, S], U8, "v2_picked")
-        nc.vector.tensor_copy(v2_picked[:], tab2_s[:].indirect(list2[:]))
-        nc.vector.tensor_copy(planes32[:, V0, :], v_picked[:].bitcast(I32))
-        nc.vector.tensor_copy(planes32[:, V1, :], v_picked[:].bitcast(I32))
-        nc.vector.tensor_copy(
-            planes32[:, W8 : W4B + 1, :].rearrange("p x (b t u) -> p (x b) t u", b=NB, t=4),
-            ws_raw[:].bitcast(I32).rearrange("p x (b u t) -> p (x b) t u", b=NB, t=4),
-        )
-        nc.vector.tensor_copy(planes32[:, V2, :], v2_picked[:].bitcast(I32))
-        for r in range(1, 4):
-            nc.sync.dma_start(out=planes32[r:P:32, 0:V1, :], in_=planes32[8 * r : P : 32, 0:V1, :])
-        for r, source in ((0, 4), (2, 20), (3, 17)):
-            nc.sync.dma_start(out=planes32[r:P:32, V1, :], in_=planes32[source:P:32, V1, :])
-        v2_plane, v_plane = planes[:, V2, :], [planes[:, V0, :], planes[:, V1, :]]
+        v_planes = held([P, 2, S], U8, "v_planes")
+        picked32 = v_picked[:].bitcast(I32)
+        nc.vector.tensor_copy(v_planes[:].bitcast(I32), picked32.unsqueeze(1).to_broadcast([P, 2, S // 4]))
+        for a, r, source in ((0, 1, 8), (0, 2, 16), (0, 3, 24), (1, 0, 4), (1, 2, 20), (1, 3, 17)):
+            nc.sync.dma_start(out=v_planes[:].bitcast(I32)[r:P:32, a, :], in_=picked32[source:P:32, :])
+        v2_plane, v_plane = planes[:, V2, :], [v_planes[:, 0, :], v_planes[:, 1, :]]
         w8_plane, w4_plane = planes[:, W8, :], [planes[:, W4A, :], planes[:, W4B, :]]
 
         tab_w[1] = load_table("tab_w1", tab_words[1], T)
@@ -194,7 +185,6 @@ def tile_list_kinase_selectivity_kernel(
         load_wg(1)
         quantise_wg(0)
         v2_words = gather_words(tab2_w, list2, "v2_words")
-        load_words(1)
         for b in range(NB):
             load_wo(b)
 
@@ -225,7 +215,7 @@ def tile_list_kinase_selectivity_kernel(
                 for a in range(2):
                     rhs, rhs_scale = moving(v_words[a], v_plane[a], jq)
                     nc.tensor.matmul_mx(
-                        pocket[c][:, t, :], lhsT=w4_codes[b][:, a, t, :].bitcast(FP4X4),
+                        pocket[c][:, t, :], lhsT=w4_codes[:, a, b, t, :].bitcast(FP4X4),
                         lhsT_scale=w4_plane[a][:, (4 * b + t) * P : (4 * b + t + 1) * P],
                         rhs=rhs, rhs_scale=rhs_scale, start=(a == 0), stop=(a == 1),
                     )
@@ -233,7 +223,7 @@ def tile_list_kinase_selectivity_kernel(
             rhs, rhs_scale = moving(v2_words, v2_plane, jq)
             for t in range(4):
                 nc.tensor.matmul_mx(
-                    shift[c][:, t, :], lhsT=w8_codes[b][:, t, :].bitcast(FP8X4),
+                    shift[c][:, t, :], lhsT=w8_codes[:, b, t, :].bitcast(FP8X4),
                     lhsT_scale=w8_plane[:, (4 * b + t) * P : (4 * b + t + 1) * P],
                     rhs=rhs, rhs_scale=rhs_scale, start=True, stop=True,
                 )
@@ -254,11 +244,14 @@ def tile_list_kinase_selectivity_kernel(
                 silu[pair] = ring.tile([P, 2 * JC, 4], F32, name="silu", tag="silu")
             nc.scalar.activation(silu[pair][:, half * JC : (half + 1) * JC, :], mixed[:], ACT.Silu)
 
-        def apply_gain(engine, c, count):
+        def apply_gain(engine, c, count, first, last):
             pair, half = divmod(c, 2)
-            cols = slice(half * JC, (half + count) * JC)
-            h_bf[c] = ring.tile([P, count * JC, 4], BF16, name="h_bf", tag="h_bf", align_bytes=64)
-            engine.tensor_tensor(h_bf[c][:], silu[pair][:, cols, :], gains[:, c // NJ, :].unsqueeze(1).to_broadcast([P, count * JC, 4]), MULT)
+            if c not in h_bf:
+                h_bf[c] = ring.tile([P, count * JC, 4], BF16, name="h_bf", tag="h_bf", align_bytes=64, bufs=3)
+            engine.tensor_tensor(
+                h_bf[c][:, first:last, :], silu[pair][:, half * JC + first : half * JC + last, :],
+                gains[:, c // NJ, :].unsqueeze(1).to_broadcast([P, last - first, 4]), MULT,
+            )
 
         def quantise_h(c, count):
             pair, half = divmod(c, 2)
@@ -276,7 +269,10 @@ def tile_list_kinase_selectivity_kernel(
         def last_product(jq, count):
             width = count * JC
             within = slice(jq % 2 * JC, jq % 2 * JC + width)
-            bank = psum.tile([P, 2, width], F32, name="out_bank", tag="gate", bufs=2)
+            if count == 1:
+                bank = psum.tile([P, 2, width], F32, name="out_bank", tag="pocket")
+            else:
+                bank = psum.tile([P, 2, width], F32, name="out_bank", tag="gate", bufs=2)
             for nt in range(2):
                 cols = slice(nt * P, (nt + 1) * P)
                 for b in range(NB):
@@ -304,29 +300,28 @@ def tile_list_kinase_selectivity_kernel(
             products(c)
         gate_pocket(0)
         for c in range(NCHUNK):
-            if c == 3:
-                order_words(1)
-            if c == LATE_GATES_FROM:
-                quantise_wg(1)
             if LATE_GATES_FROM <= c < LATE_GATES_FROM + NJ:
                 gate_stage(NJ + c - LATE_GATES_FROM)
             if c + PRODUCTS_AHEAD < NCHUNK:
                 products(c + PRODUCTS_AHEAD)
             if c + 1 < NCHUNK:
                 gate_pocket(c + 1)
-            if c % 2 == 0 and c >= QUANTISE_BEHIND:
-                quantise_h(c - QUANTISE_BEHIND, 2)
-            if c in (8, 10):
-                quantise_wo((c - 8) // 2)
             add_shift(c)
             if c < 4:
                 cast_wg(1, slice(c, c + 1))
             if c in (5, 7):
                 cast_wo((c - 5) // 2)
-            if c % 2 == 0 and c >= 2:
-                apply_gain(nc.vector, c - 2, 2)
+            if c % 2 == 1 and c < VECTOR_GAIN_FROM:
+                apply_gain(nc.vector, c - 1, 2, 0, VECTOR_SHARE)
+                if c == 3:
+                    quantise_wg(1)
+                if c in (7, 9):
+                    quantise_wo((c - 7) // 2)
+                if c >= 3:
+                    quantise_h(c - 3, 2)
+                apply_gain(nc.gpsimd, c - 1, 2, VECTOR_SHARE, 2 * JC)
+        apply_gain(nc.vector, 14, 1, 0, JC)
         quantise_h(12, 2)
-        for c in range(VECTOR_GAIN_FROM, NCHUNK):
-            apply_gain(nc.vector, c, 1)
-        for c in range(VECTOR_GAIN_FROM, NCHUNK):
-            quantise_h(c, 1)
+        quantise_h(14, 1)
+        apply_gain(nc.vector, 15, 1, 0, JC)
+        quantise_h(15, 1)

@@ -24,13 +24,14 @@ NB = H // 512
 NCHUNK = NB * NJ
 PIECE = 512
 PRODUCTS_AHEAD = 2
-LATE_GATES_FROM = 4
+LATE_GATES_FROM = 3
 VECTOR_GAIN_FROM = 14
-VECTOR_SHARE = 64
+VECTOR_SHARE = 32
 PLACE_KIB = {
-    "tab2_s": 0, "tab2_w": 3.5, "wo_raw0": 8, "wo_raw1": 12,
-    "tab_s": 20, "tab_w0": 21.5,
-    "tab_w1": 30, "staged": 37.5, "gain_raw": 38.5, "wg_raw1": 41,
+    "tab2_w": 0, "wo_raw0": 8, "wo_raw1": 12,
+    "v2_picked": 20, "tab_w0": 20.5,
+    "h_bf_even": 50, "h_bf_odd": 52,
+    "tab_w1": 30, "wg_bf0": 37.5, "gain_raw": 38.5, "wg_raw1": 41,
 }
 V2, W8, W4A, W4B = range(4)
 LAST_ROWS = P - 16
@@ -47,9 +48,10 @@ def tile_list_kinase_selectivity_kernel(
         arena = ctx.enter_context(tc.tile_pool(name="arena", bufs=1))
         psum = ctx.enter_context(tc.psum_pool(name="psum", bufs=3))
 
-        def held(shape, dtype, name):
-            if name in PLACE_KIB:
-                return arena.tile(shape, dtype, name=name, align_bytes=64, offset=int(1024 * PLACE_KIB[name]))
+        def held(shape, dtype, name, place=None):
+            place = place or name
+            if place in PLACE_KIB:
+                return arena.tile(shape, dtype, name=name, align_bytes=64, offset=int(1024 * PLACE_KIB[place]))
             return keep.tile(shape, dtype, name=name, align_bytes=64)
 
         lists = keep.tile([P, S // 16], U16, name="lists")
@@ -92,10 +94,11 @@ def tile_list_kinase_selectivity_kernel(
         nc.sync.dma_start(out=w4_raw[:], in_=w4_words.bitcast(I32).rearrange("a p c -> p a c"))
         load_wg(0)
         tab_s32 = tab_s[:].bitcast(I32)
-        nc.scalar.dma_start(out=tab_s32[0:P:8, :], in_=tab_scales[0].bitcast(I32))
+        nc.sync.dma_start(out=tab_s32[0:P:8, :], in_=tab_scales[0].bitcast(I32))
         second = tab_scales[1].bitcast(I32).rearrange("(i o) c -> o i c", o=2)
-        nc.scalar.dma_start(out=tab_s32[4:P:16, :], in_=second[0])
-        nc.scalar.dma_start(out=tab_s32[1:P:16, :], in_=second[1])
+        nc.sync.dma_start(out=tab_s32[4:P:16, :], in_=second[0])
+        nc.sync.dma_start(out=tab_s32[1:P:16, :], in_=second[1])
+        tab2_w = load_table("tab2_w", tab2_words[0], T2)
         nc.scalar.dma_start(out=ws_raw[:].bitcast(I32)[LAST_ROWS:P, 0, :], in_=w8_scales[0].bitcast(I32))
         nc.scalar.dma_start(
             out=ws_raw[:].bitcast(I32)[LAST_ROWS:P, 1:3, :], in_=w4_scales.bitcast(I32).rearrange("a q c -> q a c")
@@ -146,7 +149,6 @@ def tile_list_kinase_selectivity_kernel(
 
         v2_picked = held([P, S], U8, "v2_picked")
         nc.vector.tensor_copy(v2_picked[:], tab2_s[:].indirect(list2[:]))
-        tab2_w = load_table("tab2_w", tab2_words[0], T2)
         staged = held([P, 4, S // 4], I32, "staged")
         nc.vector.tensor_copy(
             staged[96:P, W8 : W4B + 1, :].rearrange("p x (b t u) -> p (x b) t u", b=NB, t=4),
@@ -155,6 +157,7 @@ def tile_list_kinase_selectivity_kernel(
         nc.vector.tensor_copy(staged[96:P, V2, :], v2_picked[:].bitcast(I32)[96:P, :])
         for r in range(4):
             nc.sync.dma_start(out=planes[:].bitcast(I32)[r:P:32], in_=staged[LAST_ROWS + r : P : 4])
+        tab_w[0] = load_table("tab_w0", tab_words[0], T)
         w8_codes = held([P, NB, 4, P], U32, "w8_codes")
         nc.vector.tensor_copy(
             w8_codes[:].bitcast(I32).rearrange("p b t (u e) -> p b t u e", e=4),
@@ -168,7 +171,6 @@ def tile_list_kinase_selectivity_kernel(
         cast_wg(0, slice(0, 4))
         v_picked = held([P, S], U8, "v_picked")
         nc.vector.tensor_copy(v_picked[:], tab_s[:].indirect(lists[:]))
-        tab_w[0] = load_table("tab_w0", tab_words[0], T)
         v_planes = held([P, 2, S], U8, "v_planes")
         picked32 = v_picked[:].bitcast(I32)
         nc.vector.tensor_copy(v_planes[:].bitcast(I32), picked32.unsqueeze(1).to_broadcast([P, 2, S // 4]))
@@ -177,13 +179,13 @@ def tile_list_kinase_selectivity_kernel(
         v2_plane, v_plane = planes[:, V2, :], [v_planes[:, 0, :], v_planes[:, 1, :]]
         w8_plane, w4_plane = planes[:, W8, :], [planes[:, W4A, :], planes[:, W4B, :]]
 
+        quantise_wg(0)
         tab_w[1] = load_table("tab_w1", tab_words[1], T)
         gain_raw = held([P, NB, 16], F32, "gain_raw")
         gain_runs = gain.rearrange("(b u x) -> u b x", b=NB, x=16)
         for e in range(4):
             nc.sync.dma_start(out=gain_raw[e:P:4, :, 0:13], in_=gain_runs[:, :, e : e + 13])
         load_wg(1)
-        quantise_wg(0)
         v2_words = gather_words(tab2_w, list2, "v2_words")
         for b in range(NB):
             load_wo(b)
@@ -247,7 +249,8 @@ def tile_list_kinase_selectivity_kernel(
         def apply_gain(engine, c, count, first, last):
             pair, half = divmod(c, 2)
             if c not in h_bf:
-                h_bf[c] = ring.tile([P, count * JC, 4], BF16, name="h_bf", tag="h_bf", align_bytes=64, bufs=3)
+                place = None if count == 1 else "h_bf_even" if pair in (0, 2, 4) else "h_bf_odd"
+                h_bf[c] = held([P, count * JC, 4], BF16, "h_bf%d" % c, place)
             engine.tensor_tensor(
                 h_bf[c][:, first:last, :], silu[pair][:, half * JC + first : half * JC + last, :],
                 gains[:, c // NJ, :].unsqueeze(1).to_broadcast([P, last - first, 4]), MULT,
@@ -296,6 +299,7 @@ def tile_list_kinase_selectivity_kernel(
         gains = held([P, NB, 4], F32, "gains")
         nc.scalar.copy(gains[:], gain_raw[:, :, 0:13:4])
 
+        cast_wg(1, slice(0, 4))
         for c in range(PRODUCTS_AHEAD):
             products(c)
         gate_pocket(0)
@@ -306,22 +310,24 @@ def tile_list_kinase_selectivity_kernel(
                 products(c + PRODUCTS_AHEAD)
             if c + 1 < NCHUNK:
                 gate_pocket(c + 1)
+            if c == 1:
+                quantise_wg(1)
+            if c % 2 == 0 and c >= 2:
+                if c in (8, 10):
+                    quantise_wo((c - 8) // 2)
+                if c >= 4:
+                    apply_gain(nc.vector, c - 4, 2, 0, VECTOR_SHARE)
+                if c >= 6:
+                    quantise_h(c - 6, 2)
+                if c == 14:
+                    quantise_h(10, 2)
+                apply_gain(nc.gpsimd, c - 2, 2, JC if c == 14 else VECTOR_SHARE, 2 * JC)
             add_shift(c)
-            if c < 4:
-                cast_wg(1, slice(c, c + 1))
             if c in (5, 7):
                 cast_wo((c - 5) // 2)
-            if c % 2 == 1 and c < VECTOR_GAIN_FROM:
-                apply_gain(nc.vector, c - 1, 2, 0, VECTOR_SHARE)
-                if c == 3:
-                    quantise_wg(1)
-                if c in (7, 9):
-                    quantise_wo((c - 7) // 2)
-                if c >= 3:
-                    quantise_h(c - 3, 2)
-                apply_gain(nc.gpsimd, c - 1, 2, VECTOR_SHARE, 2 * JC)
+        apply_gain(nc.vector, 12, 2, 0, JC)
         apply_gain(nc.vector, 14, 1, 0, JC)
         quantise_h(12, 2)
-        quantise_h(14, 1)
         apply_gain(nc.vector, 15, 1, 0, JC)
+        quantise_h(14, 1)
         quantise_h(15, 1)

@@ -26,12 +26,13 @@ PIECE = 512
 PRODUCTS_AHEAD = 2
 LATE_GATES_FROM = 3
 VECTOR_GAIN_FROM = 14
-VECTOR_SHARE = 32
+VECTOR_SHARE = 72
+LAST_VECTOR_SHARE = 176
 PLACE_KIB = {
     "tab2_w": 0, "wo_raw0": 8, "wo_raw1": 12,
-    "v2_picked": 20, "tab_w0": 20.5,
+    "tab_w1": 16, "v2_picked": 23.5, "tab_w0": 24,
     "h_bf_even": 50, "h_bf_odd": 52,
-    "tab_w1": 30, "wg_bf0": 37.5, "gain_raw": 38.5, "wg_raw1": 41,
+    "words_raw1": 34, "wg_bf0": 37.5, "gain_raw": 38.5, "wg_raw1": 41,
 }
 V2, W8, W4A, W4B = range(4)
 LAST_ROWS = P - 16
@@ -60,7 +61,7 @@ def tile_list_kinase_selectivity_kernel(
         tab2_s = held([P, T2], U8, "tab2_s")
         ws_raw = held([P, 3, H], U8, "ws_raw")
         planes = held([P, 4, S], U8, "planes")
-        wg_raw, wo_raw, tab_w = {}, {}, {}
+        wg_raw, w4_raw, w8_raw, wo_raw, tab_w = {}, {}, {}, {}, {}
 
         nc.gpsimd.memset(tab_s[:].bitcast(I32), 0)
         nc.vector.memset(tab2_s[:].bitcast(I32)[0:96, :], 0)
@@ -72,6 +73,19 @@ def tile_list_kinase_selectivity_kernel(
             wg_raw[b] = held([P, 4, 512], F32, "wg_raw%d" % b)
             nc.sync.dma_start(
                 out=wg_raw[b][:], in_=wg.rearrange("(p j) c -> p j c", j=4)[:, :, 512 * b : 512 * (b + 1)]
+            )
+
+        def load_words(b):
+            raw = held([P, 1024], I32, "words_raw%d" % b)
+            w8_raw[b] = raw[:, 0:512]
+            w4_raw[b] = raw[:, 512:1024].rearrange("p (a c) -> p a c", a=2)
+            nc.sync.dma_start(
+                out=w8_raw[b],
+                in_=w8_words[0].rearrange("p c i -> p (c i)").bitcast(I32)[:, 512 * b : 512 * (b + 1)],
+            )
+            nc.sync.dma_start(
+                out=w4_raw[b],
+                in_=w4_words.bitcast(I32).rearrange("a p c -> p a c")[:, :, 256 * b : 256 * (b + 1)],
             )
 
         def load_table(name, words, width):
@@ -88,10 +102,7 @@ def tile_list_kinase_selectivity_kernel(
         nc.sync.dma_start(list2[:], offs2)
         nc.sync.dma_start(out=tab2_s[:].bitcast(I32)[LAST_ROWS:P, :], in_=tab2_scales[0].bitcast(I32))
         nc.sync.dma_start(lists[:], offs)
-        w8_raw = held([P, H], I32, "w8_raw")
-        nc.sync.dma_start(out=w8_raw[:], in_=w8_words[0].rearrange("p c i -> p (c i)").bitcast(I32))
-        w4_raw = held([P, 2, H // 2], I32, "w4_raw")
-        nc.sync.dma_start(out=w4_raw[:], in_=w4_words.bitcast(I32).rearrange("a p c -> p a c"))
+        load_words(0)
         load_wg(0)
         tab_s32 = tab_s[:].bitcast(I32)
         nc.sync.dma_start(out=tab_s32[0:P:8, :], in_=tab_scales[0].bitcast(I32))
@@ -105,7 +116,7 @@ def tile_list_kinase_selectivity_kernel(
         )
 
         wg_bf, wo_bf = {}, {}
-        wg_codes, wg_plane, wo_codes, wo_plane = {}, {}, {}, {}
+        wg_codes, wg_plane, w4_codes, w8_codes, wo_codes, wo_plane = {}, {}, {}, {}, {}, {}
 
         def cast_wg(b, slots):
             if b not in wg_bf:
@@ -121,6 +132,18 @@ def tile_list_kinase_selectivity_kernel(
             nc.vector.quantize_mx(
                 out=wg_codes[b][:].bitcast(FP8X4), scales=wg_plane[b][:],
                 in_=wg_bf[b][:].rearrange("p t m j -> p (t m j)"),
+            )
+
+        def order_words(b):
+            w8_codes[b] = held([P, 4, P], U32, "w8_codes%d" % b)
+            nc.vector.tensor_copy(
+                w8_codes[b][:].bitcast(I32).rearrange("p t (u e) -> p t u e", e=4),
+                w8_raw[b].rearrange("p (u t e) -> p t u e", t=4, e=4),
+            )
+            w4_codes[b] = held([P, 2, 4, 256], U8, "w4_codes%d" % b)
+            nc.vector.tensor_copy(
+                w4_codes[b][:].bitcast(I32).rearrange("p a t (u w) -> p a t u w", w=2),
+                w4_raw[b].rearrange("p a (u t w) -> p a t u w", t=4, w=2),
             )
 
         def cast_wo(b):
@@ -158,16 +181,8 @@ def tile_list_kinase_selectivity_kernel(
         for r in range(4):
             nc.sync.dma_start(out=planes[:].bitcast(I32)[r:P:32], in_=staged[LAST_ROWS + r : P : 4])
         tab_w[0] = load_table("tab_w0", tab_words[0], T)
-        w8_codes = held([P, NB, 4, P], U32, "w8_codes")
-        nc.vector.tensor_copy(
-            w8_codes[:].bitcast(I32).rearrange("p b t (u e) -> p b t u e", e=4),
-            w8_raw[:].rearrange("p (b u t e) -> p b t u e", b=NB, t=4, e=4),
-        )
-        w4_codes = held([P, 2, NB, 4, 256], U8, "w4_codes")
-        nc.vector.tensor_copy(
-            w4_codes[:].bitcast(I32).rearrange("p a b t (u w) -> p (a b) t u w", w=2),
-            w4_raw[:].rearrange("p a (b u t w) -> p (a b) t u w", b=NB, t=4, w=2),
-        )
+        tab_w[1] = load_table("tab_w1", tab_words[1], T)
+        order_words(0)
         cast_wg(0, slice(0, 4))
         v_picked = held([P, S], U8, "v_picked")
         nc.vector.tensor_copy(v_picked[:], tab_s[:].indirect(lists[:]))
@@ -180,12 +195,12 @@ def tile_list_kinase_selectivity_kernel(
         w8_plane, w4_plane = planes[:, W8, :], [planes[:, W4A, :], planes[:, W4B, :]]
 
         quantise_wg(0)
-        tab_w[1] = load_table("tab_w1", tab_words[1], T)
+        load_wg(1)
+        load_words(1)
         gain_raw = held([P, NB, 16], F32, "gain_raw")
         gain_runs = gain.rearrange("(b u x) -> u b x", b=NB, x=16)
         for e in range(4):
             nc.sync.dma_start(out=gain_raw[e:P:4, :, 0:13], in_=gain_runs[:, :, e : e + 13])
-        load_wg(1)
         v2_words = gather_words(tab2_w, list2, "v2_words")
         for b in range(NB):
             load_wo(b)
@@ -217,7 +232,7 @@ def tile_list_kinase_selectivity_kernel(
                 for a in range(2):
                     rhs, rhs_scale = moving(v_words[a], v_plane[a], jq)
                     nc.tensor.matmul_mx(
-                        pocket[c][:, t, :], lhsT=w4_codes[:, a, b, t, :].bitcast(FP4X4),
+                        pocket[c][:, t, :], lhsT=w4_codes[b][:, a, t, :].bitcast(FP4X4),
                         lhsT_scale=w4_plane[a][:, (4 * b + t) * P : (4 * b + t + 1) * P],
                         rhs=rhs, rhs_scale=rhs_scale, start=(a == 0), stop=(a == 1),
                     )
@@ -225,7 +240,7 @@ def tile_list_kinase_selectivity_kernel(
             rhs, rhs_scale = moving(v2_words, v2_plane, jq)
             for t in range(4):
                 nc.tensor.matmul_mx(
-                    shift[c][:, t, :], lhsT=w8_codes[:, b, t, :].bitcast(FP8X4),
+                    shift[c][:, t, :], lhsT=w8_codes[b][:, t, :].bitcast(FP8X4),
                     lhsT_scale=w8_plane[:, (4 * b + t) * P : (4 * b + t + 1) * P],
                     rhs=rhs, rhs_scale=rhs_scale, start=True, stop=True,
                 )
@@ -311,6 +326,7 @@ def tile_list_kinase_selectivity_kernel(
             if c + 1 < NCHUNK:
                 gate_pocket(c + 1)
             if c == 1:
+                order_words(1)
                 quantise_wg(1)
             if c % 2 == 0 and c >= 2:
                 if c in (8, 10):
@@ -321,11 +337,11 @@ def tile_list_kinase_selectivity_kernel(
                     quantise_h(c - 6, 2)
                 if c == 14:
                     quantise_h(10, 2)
-                apply_gain(nc.gpsimd, c - 2, 2, JC if c == 14 else VECTOR_SHARE, 2 * JC)
+                apply_gain(nc.gpsimd, c - 2, 2, LAST_VECTOR_SHARE if c == 14 else VECTOR_SHARE, 2 * JC)
             add_shift(c)
             if c in (5, 7):
                 cast_wo((c - 5) // 2)
-        apply_gain(nc.vector, 12, 2, 0, JC)
+        apply_gain(nc.vector, 12, 2, 0, LAST_VECTOR_SHARE)
         apply_gain(nc.vector, 14, 1, 0, JC)
         quantise_h(12, 2)
         apply_gain(nc.vector, 15, 1, 0, JC)

@@ -24,14 +24,14 @@ NB = H // 512
 NCHUNK = NB * NJ
 PIECE = 512
 PRODUCTS_AHEAD = 2
-LATE_GATES_FROM = 3
+LATE_GATES_FROM = 5
 VECTOR_GAIN_FROM = 14
 VECTOR_SHARE = 72
 LAST_VECTOR_SHARE = 176
 PLACE_KIB = {
     "tab2_w": 0, "wo_raw0": 8, "wo_raw1": 12,
     "tab_w1": 16, "v2_picked": 23.5, "tab_w0": 24,
-    "h_bf_even": 50, "h_bf_odd": 52,
+    "h_bf_even": 50, "h_bf_odd": 52, "wg_bf1": 52,
     "words_raw1": 34, "wg_bf0": 37.5, "gain_raw": 38.5, "wg_raw1": 41,
 }
 V2, W8, W4A, W4B = range(4)
@@ -195,12 +195,12 @@ def tile_list_kinase_selectivity_kernel(
         w8_plane, w4_plane = planes[:, W8, :], [planes[:, W4A, :], planes[:, W4B, :]]
 
         quantise_wg(0)
-        load_wg(1)
-        load_words(1)
         gain_raw = held([P, NB, 16], F32, "gain_raw")
         gain_runs = gain.rearrange("(b u x) -> u b x", b=NB, x=16)
         for e in range(4):
             nc.sync.dma_start(out=gain_raw[e:P:4, :, 0:13], in_=gain_runs[:, :, e : e + 13])
+        load_wg(1)
+        load_words(1)
         v2_words = gather_words(tab2_w, list2, "v2_words")
         for b in range(NB):
             load_wo(b)
@@ -314,7 +314,7 @@ def tile_list_kinase_selectivity_kernel(
         gains = held([P, NB, 4], F32, "gains")
         nc.scalar.copy(gains[:], gain_raw[:, :, 0:13:4])
 
-        cast_wg(1, slice(0, 4))
+        cast_wg(1, slice(0, 1))
         for c in range(PRODUCTS_AHEAD):
             products(c)
         gate_pocket(0)
@@ -325,20 +325,22 @@ def tile_list_kinase_selectivity_kernel(
                 products(c + PRODUCTS_AHEAD)
             if c + 1 < NCHUNK:
                 gate_pocket(c + 1)
-            if c == 1:
-                order_words(1)
-                quantise_wg(1)
             if c % 2 == 0 and c >= 2:
                 if c in (8, 10):
                     quantise_wo((c - 8) // 2)
                 if c >= 4:
                     apply_gain(nc.vector, c - 4, 2, 0, VECTOR_SHARE)
+                if c == 4:
+                    order_words(1)
+                    quantise_wg(1)
                 if c >= 6:
                     quantise_h(c - 6, 2)
                 if c == 14:
                     quantise_h(10, 2)
                 apply_gain(nc.gpsimd, c - 2, 2, LAST_VECTOR_SHARE if c == 14 else VECTOR_SHARE, 2 * JC)
             add_shift(c)
+            if c < 3:
+                cast_wg(1, slice(c + 1, c + 2))
             if c in (5, 7):
                 cast_wo((c - 5) // 2)
         apply_gain(nc.vector, 12, 2, 0, LAST_VECTOR_SHARE)

@@ -29,12 +29,12 @@ VECTOR_GAIN_FROM = 14
 VECTOR_SHARE = 72
 LAST_VECTOR_SHARE = 176
 PLACE_KIB = {
-    "tab2_w": 0, "wo_raw0": 8, "wo_raw1": 12,
+    "tab2_w": 0, "late": 4, "wo_raw0": 8, "wo_raw1": 12,
     "tab_w1": 16, "v2_picked": 23.5, "tab_w0": 24,
     "h_bf_even": 50, "h_bf_odd": 52, "wg_bf1": 52,
     "words_raw1": 34, "wg_bf0": 37.5, "gain_raw": 38.5, "wg_raw1": 41,
 }
-V2, W8, W4A, W4B = range(4)
+W8, W4A, W4B = range(3)
 LAST_ROWS = P - 16
 
 
@@ -60,7 +60,7 @@ def tile_list_kinase_selectivity_kernel(
         tab_s = held([P, T], U8, "tab_s")
         tab2_s = held([P, T2], U8, "tab2_s")
         ws_raw = held([P, 3, H], U8, "ws_raw")
-        planes = held([P, 4, S], U8, "planes")
+        planes = held([P, S + 3 * H], U8, "planes")
         wg_raw, w4_raw, w8_raw, wo_raw, tab_w = {}, {}, {}, {}, {}
 
         nc.gpsimd.memset(tab_s[:].bitcast(I32), 0)
@@ -146,11 +146,12 @@ def tile_list_kinase_selectivity_kernel(
                 w4_raw[b].rearrange("p a (u t w) -> p a t u w", t=4, w=2),
             )
 
-        def cast_wo(b):
-            wo_bf[b] = held([P, N, 4], BF16, "wo_bf%d" % b)
+        def cast_wo(b, groups):
+            if b not in wo_bf:
+                wo_bf[b] = held([P, N, 4], BF16, "wo_bf%d" % b)
             nc.scalar.copy(
-                wo_bf[b][:].rearrange("p (c i) t -> p c t i", i=4),
-                wo_raw[b][:].rearrange("p t (c i) -> p c t i", i=4),
+                wo_bf[b][:].rearrange("p (c i) t -> p c t i", i=4)[:, groups],
+                wo_raw[b][:].rearrange("p t (c i) -> p c t i", i=4)[:, groups],
             )
 
         def quantise_wo(b):
@@ -172,14 +173,14 @@ def tile_list_kinase_selectivity_kernel(
 
         v2_picked = held([P, S], U8, "v2_picked")
         nc.vector.tensor_copy(v2_picked[:], tab2_s[:].indirect(list2[:]))
-        staged = held([P, 4, S // 4], I32, "staged")
-        nc.vector.tensor_copy(
-            staged[96:P, W8 : W4B + 1, :].rearrange("p x (b t u) -> p (x b) t u", b=NB, t=4),
-            ws_raw[:].bitcast(I32)[96:P].rearrange("p x (b u t) -> p (x b) t u", b=NB, t=4),
-        )
-        nc.vector.tensor_copy(staged[96:P, V2, :], v2_picked[:].bitcast(I32)[96:P, :])
+        planes32 = planes[:].bitcast(I32)
+        first_half = (S + 3 * 512) // 4
+        staged = held([P, first_half], I32, "staged")
+        ws_by_half = ws_raw[:].bitcast(I32)[96:P].rearrange("p x (b u t) -> p b t x u", b=NB, t=4)
+        nc.vector.tensor_copy(staged[96:P, S // 4 :].rearrange("p (x t u) -> p t x u", x=3, t=4), ws_by_half[:, 0])
+        nc.vector.tensor_copy(staged[96:P, 0 : S // 4], v2_picked[:].bitcast(I32)[96:P, :])
         for r in range(4):
-            nc.sync.dma_start(out=planes[:].bitcast(I32)[r:P:32], in_=staged[LAST_ROWS + r : P : 4])
+            nc.sync.dma_start(out=planes32[r:P:32, 0:first_half], in_=staged[LAST_ROWS + r : P : 4, :])
         tab_w[0] = load_table("tab_w0", tab_words[0], T)
         tab_w[1] = load_table("tab_w1", tab_words[1], T)
         order_words(0)
@@ -191,8 +192,11 @@ def tile_list_kinase_selectivity_kernel(
         nc.vector.tensor_copy(v_planes[:].bitcast(I32), picked32.unsqueeze(1).to_broadcast([P, 2, S // 4]))
         for a, r, source in ((0, 1, 8), (0, 2, 16), (0, 3, 24), (1, 0, 4), (1, 2, 20), (1, 3, 17)):
             nc.sync.dma_start(out=v_planes[:].bitcast(I32)[r:P:32, a, :], in_=picked32[source:P:32, :])
-        v2_plane, v_plane = planes[:, V2, :], [v_planes[:, 0, :], v_planes[:, 1, :]]
-        w8_plane, w4_plane = planes[:, W8, :], [planes[:, W4A, :], planes[:, W4B, :]]
+        v2_plane, v_plane = planes[:, 0:S], [v_planes[:, 0, :], v_planes[:, 1, :]]
+
+        def weight_plane(x, b, t):
+            start = S + (3 * b + x) * 512 + t * P
+            return planes[:, start : start + P]
 
         quantise_wg(0)
         gain_raw = held([P, NB, 16], F32, "gain_raw")
@@ -202,6 +206,10 @@ def tile_list_kinase_selectivity_kernel(
         load_wg(1)
         load_words(1)
         v2_words = gather_words(tab2_w, list2, "v2_words")
+        late = held([P, 3 * 512 // 4], I32, "late")
+        nc.vector.tensor_copy(late[96:P].rearrange("p (x t u) -> p t x u", x=3, t=4), ws_by_half[:, 1])
+        for r in range(4):
+            nc.sync.dma_start(out=planes32[r:P:32, first_half:], in_=late[LAST_ROWS + r : P : 4, :])
         for b in range(NB):
             load_wo(b)
 
@@ -233,7 +241,7 @@ def tile_list_kinase_selectivity_kernel(
                     rhs, rhs_scale = moving(v_words[a], v_plane[a], jq)
                     nc.tensor.matmul_mx(
                         pocket[c][:, t, :], lhsT=w4_codes[b][:, a, t, :].bitcast(FP4X4),
-                        lhsT_scale=w4_plane[a][:, (4 * b + t) * P : (4 * b + t + 1) * P],
+                        lhsT_scale=weight_plane(W4A + a, b, t),
                         rhs=rhs, rhs_scale=rhs_scale, start=(a == 0), stop=(a == 1),
                     )
             shift[c] = psum.tile([P, 4, JC], F32, name="shift", tag="shift")
@@ -241,7 +249,7 @@ def tile_list_kinase_selectivity_kernel(
             for t in range(4):
                 nc.tensor.matmul_mx(
                     shift[c][:, t, :], lhsT=w8_codes[b][:, t, :].bitcast(FP8X4),
-                    lhsT_scale=w8_plane[:, (4 * b + t) * P : (4 * b + t + 1) * P],
+                    lhsT_scale=weight_plane(W8, b, t),
                     rhs=rhs, rhs_scale=rhs_scale, start=True, stop=True,
                 )
 
@@ -287,21 +295,29 @@ def tile_list_kinase_selectivity_kernel(
         def last_product(jq, count):
             width = count * JC
             within = slice(jq % 2 * JC, jq % 2 * JC + width)
-            if count == 1:
-                bank = psum.tile([P, 2, width], F32, name="out_bank", tag="pocket")
+            if jq == NJ - 1:
+                banks = [psum.tile([P, width], F32, name="out_bank", tag=tag)[:] for tag in ("pocket", "shift")]
             else:
-                bank = psum.tile([P, 2, width], F32, name="out_bank", tag="gate", bufs=2)
+                if count == 1:
+                    bank = psum.tile([P, 2, width], F32, name="out_bank", tag="pocket")
+                else:
+                    bank = psum.tile([P, 2, width], F32, name="out_bank", tag="gate", bufs=2)
+                banks = [bank[:, 0, :], bank[:, 1, :]]
             for nt in range(2):
                 cols = slice(nt * P, (nt + 1) * P)
                 for b in range(NB):
                     pair = (b * NJ + jq) // 2
                     nc.tensor.matmul_mx(
-                        bank[:, nt, :], lhsT=wo_codes[b][:, cols].bitcast(FP8X4), lhsT_scale=wo_plane[b][:, cols],
+                        banks[nt], lhsT=wo_codes[b][:, cols].bitcast(FP8X4), lhsT_scale=wo_plane[b][:, cols],
                         rhs=h_codes[pair][:, within].bitcast(FP8X4), rhs_scale=h_plane[pair][:, within],
                         start=(b == 0), stop=(b == NB - 1),
                     )
             result = held([P, 2, width], F32, "result%d" % jq)
-            nc.scalar.copy(result[:], bank[:])
+            if jq == NJ - 1:
+                nc.vector.tensor_copy(result[:, 0, :], banks[0])
+                nc.scalar.copy(result[:, 1, :], banks[1])
+            else:
+                nc.scalar.copy(result[:], bank[:])
             nc.sync.dma_start(
                 out=out.rearrange("(nt p) j -> p nt j", p=P)[:, :, jq * JC : jq * JC + width], in_=result[:]
             )
@@ -341,8 +357,10 @@ def tile_list_kinase_selectivity_kernel(
             add_shift(c)
             if c < 3:
                 cast_wg(1, slice(c + 1, c + 2))
+            if c == 3:
+                cast_wo(0, slice(0, 64))
             if c in (5, 7):
-                cast_wo((c - 5) // 2)
+                cast_wo(1, slice(16 * (c - 5), 16 * (c - 3)))
         apply_gain(nc.vector, 12, 2, 0, LAST_VECTOR_SHARE)
         apply_gain(nc.vector, 14, 1, 0, JC)
         quantise_h(12, 2)

@@ -22,20 +22,27 @@ JC = 128
 NJ = S // JC
 NB = H // 512
 NCHUNK = NB * NJ
-PIECE = 512
 PRODUCTS_AHEAD = 2
-LATE_GATES_FROM = 5
-VECTOR_GAIN_FROM = 14
-VECTOR_SHARE = 72
-LAST_VECTOR_SHARE = 176
-PLACE_KIB = {
-    "tab2_w": 0, "late": 4, "wo_raw0": 8, "wo_raw1": 12,
-    "tab_w1": 16, "v2_picked": 23.5, "tab_w0": 24,
-    "h_bf_even": 50, "h_bf_odd": 52, "wg_bf1": 52,
-    "words_raw1": 34, "wg_bf0": 37.5, "gain_raw": 38.5, "wg_raw1": 41,
-}
+LATE_GATES_FROM = 6
+BATCHES = ((0, 3), (3, 7), (7, 11), (11, 13))
+VISIT_AT = (5, 9, 13, 15)
+VECTOR_SHARE = (0, 64, 64, 0)
+KIB = 1024
+PLACE = {"h_bf": 0, "tanh_half0": 4 * KIB, "v_words1_512": 4 * KIB}
+EARLY_GATE_BANKS = ("gate", "gate", "shift", "shift", "shift", "gate", "gate", "shift")
 W8, W4A, W4B = range(3)
 LAST_ROWS = P - 16
+
+
+def powers_of_two(first, last, most):
+    pieces = []
+    while first < last:
+        count = most
+        while first + count > last:
+            count = count // 2
+        pieces.append((first, count))
+        first = first + count
+    return pieces
 
 
 def tile_list_kinase_selectivity_kernel(
@@ -51,8 +58,8 @@ def tile_list_kinase_selectivity_kernel(
 
         def held(shape, dtype, name, place=None):
             place = place or name
-            if place in PLACE_KIB:
-                return arena.tile(shape, dtype, name=name, align_bytes=64, offset=int(1024 * PLACE_KIB[place]))
+            if place in PLACE:
+                return arena.tile(shape, dtype, name=name, align_bytes=64, offset=PLACE[place])
             return keep.tile(shape, dtype, name=name, align_bytes=64)
 
         lists = keep.tile([P, S // 16], U16, name="lists")
@@ -63,11 +70,13 @@ def tile_list_kinase_selectivity_kernel(
         planes = held([P, S + 3 * H], U8, "planes")
         wg_raw, w4_raw, w8_raw, wo_raw, tab_w = {}, {}, {}, {}, {}
 
-        nc.gpsimd.memset(tab_s[:].bitcast(I32), 0)
+        v_planes = [held([P, S], U8, "v_plane%d" % a) for a in range(2)]
         nc.vector.memset(tab2_s[:].bitcast(I32)[0:96, :], 0)
-        nc.vector.memset(tab2_s[:].bitcast(I32)[96:LAST_ROWS, :], 0)
-        nc.gpsimd.memset(ws_raw[:].bitcast(I32)[96:LAST_ROWS], 0)
+        nc.gpsimd.memset(tab2_s[:].bitcast(I32)[96:LAST_ROWS, :], 0)
+        nc.gpsimd.memset(tab_s[:].bitcast(I32), 0)
+        nc.vector.memset(ws_raw[:].bitcast(I32)[96:LAST_ROWS], 0)
         nc.gpsimd.memset(planes[:].bitcast(I32), 0)
+        nc.gpsimd.memset(v_planes[1][:].bitcast(I32), 0)
 
         def load_wg(b):
             wg_raw[b] = held([P, 4, 512], F32, "wg_raw%d" % b)
@@ -75,14 +84,14 @@ def tile_list_kinase_selectivity_kernel(
                 out=wg_raw[b][:], in_=wg.rearrange("(p j) c -> p j c", j=4)[:, :, 512 * b : 512 * (b + 1)]
             )
 
-        def load_words(b):
-            raw = held([P, 1024], I32, "words_raw%d" % b)
-            w8_raw[b] = raw[:, 0:512]
-            w4_raw[b] = raw[:, 512:1024].rearrange("p (a c) -> p a c", a=2)
+        def load_w8(b, raw):
+            w8_raw[b] = raw
             nc.sync.dma_start(
-                out=w8_raw[b],
-                in_=w8_words[0].rearrange("p c i -> p (c i)").bitcast(I32)[:, 512 * b : 512 * (b + 1)],
+                out=raw, in_=w8_words[0].rearrange("p c i -> p (c i)").bitcast(I32)[:, 512 * b : 512 * (b + 1)]
             )
+
+        def load_w4(b, raw):
+            w4_raw[b] = raw.rearrange("p (a c) -> p a c", a=2)
             nc.sync.dma_start(
                 out=w4_raw[b],
                 in_=w4_words.bitcast(I32).rearrange("a p c -> p a c")[:, :, 256 * b : 256 * (b + 1)],
@@ -95,25 +104,25 @@ def tile_list_kinase_selectivity_kernel(
 
         def load_wo(b):
             wo_raw[b] = held([P, 4, N], F32, "wo_raw%d" % b)
-            rows = wo[512 * b : 512 * (b + 1), :].rearrange("(u t e) n -> e u t n", t=4, e=4)
-            for e in range(4):
-                nc.sync.dma_start(out=wo_raw[b][e:P:4, :, :], in_=rows[e])
+            rows = wo[512 * b : 512 * (b + 1), :].rearrange("(u t e) n -> t u e n", t=4, e=4)
+            for t in range(4):
+                nc.sync.dma_start(out=wo_raw[b][:, t, :], in_=rows[t])
 
         nc.sync.dma_start(list2[:], offs2)
         nc.sync.dma_start(out=tab2_s[:].bitcast(I32)[LAST_ROWS:P, :], in_=tab2_scales[0].bitcast(I32))
         nc.sync.dma_start(lists[:], offs)
-        load_words(0)
-        load_wg(0)
-        tab_s32 = tab_s[:].bitcast(I32)
-        nc.sync.dma_start(out=tab_s32[0:P:8, :], in_=tab_scales[0].bitcast(I32))
-        second = tab_scales[1].bitcast(I32).rearrange("(i o) c -> o i c", o=2)
-        nc.sync.dma_start(out=tab_s32[4:P:16, :], in_=second[0])
-        nc.sync.dma_start(out=tab_s32[1:P:16, :], in_=second[1])
-        tab2_w = load_table("tab2_w", tab2_words[0], T2)
-        nc.scalar.dma_start(out=ws_raw[:].bitcast(I32)[LAST_ROWS:P, 0, :], in_=w8_scales[0].bitcast(I32))
-        nc.scalar.dma_start(
+        nc.sync.dma_start(
             out=ws_raw[:].bitcast(I32)[LAST_ROWS:P, 1:3, :], in_=w4_scales.bitcast(I32).rearrange("a q c -> q a c")
         )
+        nc.sync.dma_start(out=ws_raw[:].bitcast(I32)[LAST_ROWS:P, 0, :], in_=w8_scales[0].bitcast(I32))
+        load_w4(0, held([P, 512], I32, "w4_raw0")[:])
+        load_wg(0)
+        tab_s32 = tab_s[:].bitcast(I32)
+        by_parity = tab_scales[0].bitcast(I32).rearrange("(i o) c -> o i c", o=2)
+        for o in range(2):
+            nc.sync.dma_start(out=tab_s32[o:P:16, :], in_=by_parity[o])
+        nc.sync.dma_start(out=tab_s32[4:P:8, :], in_=tab_scales[1].bitcast(I32))
+        tab2_w = load_table("tab2_w", tab2_words[0], T2)
 
         wg_bf, wo_bf = {}, {}
         wg_codes, wg_plane, w4_codes, w8_codes, wo_codes, wo_plane = {}, {}, {}, {}, {}, {}
@@ -134,41 +143,44 @@ def tile_list_kinase_selectivity_kernel(
                 in_=wg_bf[b][:].rearrange("p t m j -> p (t m j)"),
             )
 
-        def order_words(b):
+        def order_w8(b):
             w8_codes[b] = held([P, 4, P], U32, "w8_codes%d" % b)
             nc.vector.tensor_copy(
                 w8_codes[b][:].bitcast(I32).rearrange("p t (u e) -> p t u e", e=4),
                 w8_raw[b].rearrange("p (u t e) -> p t u e", t=4, e=4),
             )
+
+        def order_w4(b):
             w4_codes[b] = held([P, 2, 4, 256], U8, "w4_codes%d" % b)
             nc.vector.tensor_copy(
                 w4_codes[b][:].bitcast(I32).rearrange("p a t (u w) -> p a t u w", w=2),
                 w4_raw[b].rearrange("p a (u t w) -> p a t u w", t=4, w=2),
             )
 
+        wo_bf_both = held([P, NB, N, 4], BF16, "wo_bf")
+
         def cast_wo(b, groups):
-            if b not in wo_bf:
-                wo_bf[b] = held([P, N, 4], BF16, "wo_bf%d" % b)
             nc.scalar.copy(
-                wo_bf[b][:].rearrange("p (c i) t -> p c t i", i=4)[:, groups],
+                wo_bf_both[:, b].rearrange("p (c i) t -> p c t i", i=4)[:, groups],
                 wo_raw[b][:].rearrange("p t (c i) -> p c t i", i=4)[:, groups],
             )
 
-        def quantise_wo(b):
-            wo_codes[b] = held([P, N], U32, "wo_codes%d" % b)
-            wo_plane[b] = held([P, N], U8, "wo_plane%d" % b)
+        def quantise_wo():
+            codes = held([P, NB * N], U32, "wo_codes")
+            plane = held([P, NB * N], U8, "wo_plane")
             nc.vector.quantize_mx(
-                out=wo_codes[b][:].bitcast(FP8X4), scales=wo_plane[b][:],
-                in_=wo_bf[b][:].rearrange("p n t -> p (n t)"),
+                out=codes[:].bitcast(FP8X4), scales=plane[:], in_=wo_bf_both[:].rearrange("p b n t -> p (b n t)")
             )
+            for b in range(NB):
+                wo_codes[b], wo_plane[b] = codes[:, b * N : (b + 1) * N], plane[:, b * N : (b + 1) * N]
 
-        def gather_words(window, offsets, name):
+        def gather_words(window, offsets, name, widths, start=0):
             pieces = []
-            for piece in range(S // PIECE):
-                picked = held([P, PIECE], U32, "%s%d" % (name, piece))
-                cols = slice(piece * PIECE // 16, (piece + 1) * PIECE // 16)
-                nc.vector.tensor_copy(picked[:], window[:].indirect(offsets[:, cols]))
-                pieces.append(picked)
+            for width in widths:
+                picked = held([P, width], U32, "%s_%d" % (name, start))
+                nc.vector.tensor_copy(picked[:], window[:].indirect(offsets[:, start // 16 : (start + width) // 16]))
+                pieces.append((start, width, picked))
+                start = start + width
             return pieces
 
         v2_picked = held([P, S], U8, "v2_picked")
@@ -180,50 +192,53 @@ def tile_list_kinase_selectivity_kernel(
         nc.vector.tensor_copy(staged[96:P, S // 4 :].rearrange("p (x t u) -> p t x u", x=3, t=4), ws_by_half[:, 0])
         nc.vector.tensor_copy(staged[96:P, 0 : S // 4], v2_picked[:].bitcast(I32)[96:P, :])
         for r in range(4):
-            nc.sync.dma_start(out=planes32[r:P:32, 0:first_half], in_=staged[LAST_ROWS + r : P : 4, :])
+            nc.sync.dma_start(out=planes32[r:P:32, 0:first_half], in_=staged[LAST_ROWS + r : P : 4, 0:first_half])
         tab_w[0] = load_table("tab_w0", tab_words[0], T)
-        tab_w[1] = load_table("tab_w1", tab_words[1], T)
-        order_words(0)
+        order_w4(0)
         cast_wg(0, slice(0, 4))
         v_picked = held([P, S], U8, "v_picked")
         nc.vector.tensor_copy(v_picked[:], tab_s[:].indirect(lists[:]))
-        v_planes = held([P, 2, S], U8, "v_planes")
         picked32 = v_picked[:].bitcast(I32)
-        nc.vector.tensor_copy(v_planes[:].bitcast(I32), picked32.unsqueeze(1).to_broadcast([P, 2, S // 4]))
-        for a, r, source in ((0, 1, 8), (0, 2, 16), (0, 3, 24), (1, 0, 4), (1, 2, 20), (1, 3, 17)):
-            nc.sync.dma_start(out=v_planes[:].bitcast(I32)[r:P:32, a, :], in_=picked32[source:P:32, :])
-        v2_plane, v_plane = planes[:, 0:S], [v_planes[:, 0, :], v_planes[:, 1, :]]
+        nc.vector.tensor_copy(v_planes[0][:].bitcast(I32), picked32)
+        for a, r, source in ((1, 0, 4), (1, 1, 12), (1, 2, 20), (1, 3, 28), (0, 2, 16), (0, 3, 17)):
+            nc.sync.dma_start(out=v_planes[a][:].bitcast(I32)[r:P:32, :], in_=picked32[source:P:32, :])
+        tab_w[1] = load_table("tab_w1", tab_words[1], T)
+        load_w8(0, held([P, 512], I32, "w8_raw0")[:])
+        v2_plane, v_plane = planes[:, 0:S], [v_planes[0][:], v_planes[1][:]]
 
         def weight_plane(x, b, t):
             start = S + (3 * b + x) * 512 + t * P
             return planes[:, start : start + P]
 
         quantise_wg(0)
+        late = held([P, 3 * 512 // 4], I32, "late")
+        nc.vector.tensor_copy(late[96:P].rearrange("p (x t u) -> p t x u", x=3, t=4), ws_by_half[:, 1])
+        v2_words = gather_words(tab2_w, list2, "v2_words", (512, 512))
         gain_raw = held([P, NB, 16], F32, "gain_raw")
         gain_runs = gain.rearrange("(b u x) -> u b x", b=NB, x=16)
         for e in range(4):
             nc.sync.dma_start(out=gain_raw[e:P:4, :, 0:13], in_=gain_runs[:, :, e : e + 13])
         load_wg(1)
-        load_words(1)
-        v2_words = gather_words(tab2_w, list2, "v2_words")
-        late = held([P, 3 * 512 // 4], I32, "late")
-        nc.vector.tensor_copy(late[96:P].rearrange("p (x t u) -> p t x u", x=3, t=4), ws_by_half[:, 1])
+        load_w4(1, held([P, 512], I32, "w4_raw1")[:])
+        load_w8(1, held([P, 512], I32, "w8_raw1")[:])
         for r in range(4):
             nc.sync.dma_start(out=planes32[r:P:32, first_half:], in_=late[LAST_ROWS + r : P : 4, :])
-        for b in range(NB):
-            load_wo(b)
 
-        tanh_half, pocket, shift, gated, silu, h_bf, h_codes, h_plane = {}, {}, {}, {}, {}, {}, {}, {}
+        tanh_half, pocket, shift, gated, silu, h_bf = {}, {}, {}, {}, {}, {}
+        h_codes = held([P, NCHUNK * JC], U32, "h_codes")
+        h_plane = held([P, NCHUNK * JC], U8, "h_plane")
 
         def moving(pieces, plane, jq):
             start = jq * JC
-            words = pieces[start // PIECE][:, start % PIECE : start % PIECE + JC]
+            first, width, picked = [piece for piece in pieces if piece[0] <= start < piece[0] + piece[1]][0]
+            words = picked[:, start - first : start - first + JC]
             return words.bitcast(FP8X4), plane[:, start : start + JC]
 
         def gate_stage(c):
             b, jq = divmod(c, NJ)
             rhs, rhs_scale = moving(v2_words, v2_plane, jq)
-            bank = psum.tile([P, 4, JC], F32, name="gate", tag="gate", bufs=2)
+            tag = EARLY_GATE_BANKS[c] if c < NJ else "gate"
+            bank = psum.tile([P, 4, JC], F32, name="gate", tag=tag, bufs=2 if tag == "gate" else 3)
             for t in range(4):
                 cols = slice(t * P, (t + 1) * P)
                 nc.tensor.matmul_mx(
@@ -233,7 +248,7 @@ def tile_list_kinase_selectivity_kernel(
             tanh_half[c] = held([P, JC, 4], F32, "tanh_half%d" % c)
             nc.scalar.activation(tanh_half[c][:], bank[:].rearrange("p t j -> p j t"), ACT.Tanh, scale=0.5)
 
-        def products(c):
+        def pocket_stage(c):
             b, jq = divmod(c, NJ)
             pocket[c] = psum.tile([P, 4, JC], F32, name="pocket", tag="pocket")
             for t in range(4):
@@ -244,6 +259,9 @@ def tile_list_kinase_selectivity_kernel(
                         lhsT_scale=weight_plane(W4A + a, b, t),
                         rhs=rhs, rhs_scale=rhs_scale, start=(a == 0), stop=(a == 1),
                     )
+
+        def shift_stage(c):
+            b, jq = divmod(c, NJ)
             shift[c] = psum.tile([P, 4, JC], F32, name="shift", tag="shift")
             rhs, rhs_scale = moving(v2_words, v2_plane, jq)
             for t in range(4):
@@ -259,57 +277,44 @@ def tile_list_kinase_selectivity_kernel(
                 gated[c][:], tanh_half[c][:], 1.0, pocket[c][:].rearrange("p t j -> p j t"), ADD, MULT
             )
 
+        silu = held([P, NCHUNK * JC, 4], F32, "silu")
+
         def add_shift(c):
-            pair, half = divmod(c, 2)
             mixed = ring.tile([P, JC, 4], F32, name="mixed", tag="mixed")
             nc.vector.scalar_tensor_tensor(
                 mixed[:], gated[c][:], 0.5, shift[c][:].rearrange("p t j -> p j t"), MULT, ADD
             )
-            if half == 0:
-                silu[pair] = ring.tile([P, 2 * JC, 4], F32, name="silu", tag="silu")
-            nc.scalar.activation(silu[pair][:, half * JC : (half + 1) * JC, :], mixed[:], ACT.Silu)
+            nc.scalar.activation(silu[:, c * JC : (c + 1) * JC, :], mixed[:], ACT.Silu)
 
-        def apply_gain(engine, c, count, first, last):
-            pair, half = divmod(c, 2)
-            if c not in h_bf:
-                place = None if count == 1 else "h_bf_even" if pair in (0, 2, 4) else "h_bf_odd"
-                h_bf[c] = held([P, count * JC, 4], BF16, "h_bf%d" % c, place)
+        def apply_gain(engine, base, first, last):
             engine.tensor_tensor(
-                h_bf[c][:, first:last, :], silu[pair][:, half * JC + first : half * JC + last, :],
-                gains[:, c // NJ, :].unsqueeze(1).to_broadcast([P, last - first, 4]), MULT,
+                h_bf[base][:, first - base * JC : last - base * JC, :], silu[:, first:last, :],
+                gains[:, first // S, :].unsqueeze(1).to_broadcast([P, last - first, 4]), MULT,
             )
 
-        def quantise_h(c, count):
-            pair, half = divmod(c, 2)
-            cols = slice(half * JC, (half + count) * JC)
-            if half == 0:
-                h_codes[pair] = held([P, 2 * JC], U32, "h_codes%d" % pair)
-                h_plane[pair] = held([P, 2 * JC], U8, "h_plane%d" % pair)
+        def quantise_h(base, c, count):
+            cols = slice(c * JC, (c + count) * JC)
             nc.vector.quantize_mx(
-                out=h_codes[pair][:, cols].bitcast(FP8X4), scales=h_plane[pair][:, cols],
-                in_=h_bf[c][:].rearrange("p j t -> p (j t)"),
+                out=h_codes[:, cols].bitcast(FP8X4), scales=h_plane[:, cols],
+                in_=h_bf[base][:, (c - base) * JC : (c - base + count) * JC, :].rearrange("p j t -> p (j t)"),
             )
-            if c >= NJ:
-                last_product(c - NJ, count)
+            for first, chunks in powers_of_two(max(c, NJ), c + count, 2):
+                last_product(first - NJ, chunks)
 
         def last_product(jq, count):
             width = count * JC
-            within = slice(jq % 2 * JC, jq % 2 * JC + width)
             if jq == NJ - 1:
                 banks = [psum.tile([P, width], F32, name="out_bank", tag=tag)[:] for tag in ("pocket", "shift")]
             else:
-                if count == 1:
-                    bank = psum.tile([P, 2, width], F32, name="out_bank", tag="pocket")
-                else:
-                    bank = psum.tile([P, 2, width], F32, name="out_bank", tag="gate", bufs=2)
+                bank = psum.tile([P, 2, width], F32, name="out_bank", tag="gate", bufs=2)
                 banks = [bank[:, 0, :], bank[:, 1, :]]
             for nt in range(2):
                 cols = slice(nt * P, (nt + 1) * P)
                 for b in range(NB):
-                    pair = (b * NJ + jq) // 2
+                    entries = slice(b * S + jq * JC, b * S + jq * JC + width)
                     nc.tensor.matmul_mx(
                         banks[nt], lhsT=wo_codes[b][:, cols].bitcast(FP8X4), lhsT_scale=wo_plane[b][:, cols],
-                        rhs=h_codes[pair][:, within].bitcast(FP8X4), rhs_scale=h_plane[pair][:, within],
+                        rhs=h_codes[:, entries].bitcast(FP8X4), rhs_scale=h_plane[:, entries],
                         start=(b == 0), stop=(b == NB - 1),
                     )
             result = held([P, 2, width], F32, "result%d" % jq)
@@ -322,48 +327,74 @@ def tile_list_kinase_selectivity_kernel(
                 out=out.rearrange("(nt p) j -> p nt j", p=P)[:, :, jq * JC : jq * JC + width], in_=result[:]
             )
 
+        def gpsimd_batch(i):
+            first, last = BATCHES[i]
+            h_bf[first] = held([P, (last - first) * JC, 4], BF16, "h_bf%d" % first, "h_bf")
+            c = first
+            while c < last:
+                after = min(c + (1 if i == 0 else 2), last, NJ if c < NJ else NCHUNK)
+                pending.append((after - 1, first, c * JC, after * JC - (VECTOR_SHARE[i] if after == last else 0)))
+                c = after
+
+        def visit(i):
+            first, last = BATCHES[i]
+            if VECTOR_SHARE[i]:
+                apply_gain(nc.vector, first, last * JC - VECTOR_SHARE[i], last * JC)
+            if i == 0:
+                order_w4(1)
+                order_w8(1)
+                quantise_wg(1)
+            if i == 2:
+                quantise_wo()
+            for c, count in powers_of_two(first, last, 4):
+                quantise_h(first, c, count)
+            if i + 1 < len(BATCHES):
+                gpsimd_batch(i + 1)
+
+        def issue_gpsimd(done):
+            while pending and pending[0][0] <= done:
+                ready, base, first, last = pending.pop(0)
+                apply_gain(nc.gpsimd, base, first, last)
+
         for c in range(NJ):
             gate_stage(c)
-        v_words = [gather_words(tab_w[0], lists, "v_words0")]
-        v_words.append(gather_words(tab_w[1], lists, "v_words1"))
+        v_words = [gather_words(tab_w[0], lists, "v_words0", (1024,))]
+        for b in range(NB):
+            load_wo(b)
+        v_words.append(gather_words(tab_w[1], lists, "v_words1", (256,)))
+        order_w8(0)
+        v_words[1].extend(gather_words(tab_w[1], lists, "v_words1", (256,), 256))
 
         gains = held([P, NB, 4], F32, "gains")
         nc.scalar.copy(gains[:], gain_raw[:, :, 0:13:4])
 
-        cast_wg(1, slice(0, 1))
+        pending = []
+        gpsimd_batch(0)
         for c in range(PRODUCTS_AHEAD):
-            products(c)
+            pocket_stage(c)
+            shift_stage(c)
         gate_pocket(0)
         for c in range(NCHUNK):
             if LATE_GATES_FROM <= c < LATE_GATES_FROM + NJ:
                 gate_stage(NJ + c - LATE_GATES_FROM)
             if c + PRODUCTS_AHEAD < NCHUNK:
-                products(c + PRODUCTS_AHEAD)
+                pocket_stage(c + PRODUCTS_AHEAD)
+                shift_stage(c + PRODUCTS_AHEAD)
             if c + 1 < NCHUNK:
                 gate_pocket(c + 1)
-            if c % 2 == 0 and c >= 2:
-                if c in (8, 10):
-                    quantise_wo((c - 8) // 2)
-                if c >= 4:
-                    apply_gain(nc.vector, c - 4, 2, 0, VECTOR_SHARE)
-                if c == 4:
-                    order_words(1)
-                    quantise_wg(1)
-                if c >= 6:
-                    quantise_h(c - 6, 2)
-                if c == 14:
-                    quantise_h(10, 2)
-                apply_gain(nc.gpsimd, c - 2, 2, LAST_VECTOR_SHARE if c == 14 else VECTOR_SHARE, 2 * JC)
+            if c == 0:
+                v_words[1].extend(gather_words(tab_w[1], lists, "v_words1", (512,), 512))
+            if c in VISIT_AT[:-1]:
+                visit(VISIT_AT.index(c))
+            issue_gpsimd(c - 1)
             add_shift(c)
-            if c < 3:
-                cast_wg(1, slice(c + 1, c + 2))
-            if c == 3:
-                cast_wo(0, slice(0, 64))
-            if c in (5, 7):
-                cast_wo(1, slice(16 * (c - 5), 16 * (c - 3)))
-        apply_gain(nc.vector, 12, 2, 0, LAST_VECTOR_SHARE)
-        apply_gain(nc.vector, 14, 1, 0, JC)
-        quantise_h(12, 2)
-        apply_gain(nc.vector, 15, 1, 0, JC)
-        quantise_h(14, 1)
-        quantise_h(15, 1)
+            if 1 <= c < 5:
+                cast_wg(1, slice(c - 1, c))
+            if c in (8, 9, 10, 11):
+                cast_wo((c - 8) // 2, slice(32 * (c % 2), 32 * (c % 2 + 1)))
+        visit(len(BATCHES) - 1)
+        for c in range(BATCHES[-1][1], NCHUNK):
+            h_bf[c] = held([P, JC, 4], BF16, "h_bf%d" % c)
+            apply_gain(nc.vector, c, c * JC, (c + 1) * JC)
+        for c in range(BATCHES[-1][1], NCHUNK):
+            quantise_h(c, c, 1)

@@ -23,12 +23,20 @@ NJ = S // JC
 NB = H // 512
 NCHUNK = NB * NJ
 PRODUCTS_AHEAD = 2
-LATE_GATES_FROM = 6
-BATCHES = ((0, 3), (3, 7), (7, 11), (11, 13))
-VISIT_AT = (5, 9, 13, 15)
-VECTOR_SHARE = (0, 64, 64, 0)
+LATE_GATES_FROM = 4
+GPSIMD_RUNS = ((0, 1), (1, 2), (2, 3), (3, 4), (4, 6), (6, 8), (8, 10), (10, 12))
+SPANS = ((0, 2), (2, 12), (12, 14), (14, 16))
+VISIT_AT = 3
 KIB = 1024
-PLACE = {"h_bf": 0, "tanh_half0": 4 * KIB, "v_words1_512": 4 * KIB}
+PLACE = {
+    "tanh_half2": 0, "v_words1_512": 0,
+    "mixed3": 2 * KIB, "w8_raw1": 3 * KIB, "h_bf2": 4 * KIB, "w4_raw1": 6 * KIB, "wg_bf1": 12 * KIB, "gated5": 14 * KIB,
+    "silu0": 16 * KIB, "w4_codes1": 16 * KIB, "wg_plane1": 18 * KIB, "w8_codes1": 19 * KIB,
+    "tanh_half5": 26 * KIB, "tanh_half6": 28 * KIB, "tanh_half7": 30 * KIB, "tanh_half4": 32 * KIB,
+    "mixed11": 34 * KIB, "wo_bf": 34 * KIB, "h_bf12": 34 * KIB,
+    "silu2": 40 * KIB, "h_bf14": 42 * KIB, "wo_plane": 44 * KIB,
+    "h_plane0": 45 * KIB, "h_plane2": 46 * KIB, "h_plane4": 47 * KIB, "h_plane8": 48 * KIB, "h_plane10": 49 * KIB,
+}
 EARLY_GATE_BANKS = ("gate", "gate", "shift", "shift", "shift", "gate", "gate", "shift")
 W8, W4A, W4B = range(3)
 LAST_ROWS = P - 16
@@ -186,13 +194,14 @@ def tile_list_kinase_selectivity_kernel(
         v2_picked = held([P, S], U8, "v2_picked")
         nc.vector.tensor_copy(v2_picked[:], tab2_s[:].indirect(list2[:]))
         planes32 = planes[:].bitcast(I32)
-        first_half = (S + 3 * 512) // 4
-        staged = held([P, first_half], I32, "staged")
-        ws_by_half = ws_raw[:].bitcast(I32)[96:P].rearrange("p x (b u t) -> p b t x u", b=NB, t=4)
-        nc.vector.tensor_copy(staged[96:P, S // 4 :].rearrange("p (x t u) -> p t x u", x=3, t=4), ws_by_half[:, 0])
+        staged = held([P, (S + 3 * H) // 4], I32, "staged")
+        nc.vector.tensor_copy(
+            staged[96:P, S // 4 :].rearrange("p (b x t u) -> p b t x u", b=NB, x=3, t=4),
+            ws_raw[:].bitcast(I32)[96:P].rearrange("p x (b u t) -> p b t x u", b=NB, t=4),
+        )
         nc.vector.tensor_copy(staged[96:P, 0 : S // 4], v2_picked[:].bitcast(I32)[96:P, :])
         for r in range(4):
-            nc.sync.dma_start(out=planes32[r:P:32, 0:first_half], in_=staged[LAST_ROWS + r : P : 4, 0:first_half])
+            nc.sync.dma_start(out=planes32[r:P:32, :], in_=staged[LAST_ROWS + r : P : 4, :])
         tab_w[0] = load_table("tab_w0", tab_words[0], T)
         order_w4(0)
         cast_wg(0, slice(0, 4))
@@ -211,22 +220,18 @@ def tile_list_kinase_selectivity_kernel(
             return planes[:, start : start + P]
 
         quantise_wg(0)
-        late = held([P, 3 * 512 // 4], I32, "late")
-        nc.vector.tensor_copy(late[96:P].rearrange("p (x t u) -> p t x u", x=3, t=4), ws_by_half[:, 1])
         v2_words = gather_words(tab2_w, list2, "v2_words", (512, 512))
+        load_wg(1)
         gain_raw = held([P, NB, 16], F32, "gain_raw")
         gain_runs = gain.rearrange("(b u x) -> u b x", b=NB, x=16)
         for e in range(4):
             nc.sync.dma_start(out=gain_raw[e:P:4, :, 0:13], in_=gain_runs[:, :, e : e + 13])
-        load_wg(1)
         load_w4(1, held([P, 512], I32, "w4_raw1")[:])
         load_w8(1, held([P, 512], I32, "w8_raw1")[:])
-        for r in range(4):
-            nc.sync.dma_start(out=planes32[r:P:32, first_half:], in_=late[LAST_ROWS + r : P : 4, :])
 
         tanh_half, pocket, shift, gated, silu, h_bf = {}, {}, {}, {}, {}, {}
         h_codes = held([P, NCHUNK * JC], U32, "h_codes")
-        h_plane = held([P, NCHUNK * JC], U8, "h_plane")
+        h_plane, run_left = {}, {}
 
         def moving(pieces, plane, jq):
             start = jq * JC
@@ -245,7 +250,8 @@ def tile_list_kinase_selectivity_kernel(
                     bank[:, t, :], lhsT=wg_codes[b][:, cols].bitcast(FP8X4), lhsT_scale=wg_plane[b][:, cols],
                     rhs=rhs, rhs_scale=rhs_scale, start=True, stop=True,
                 )
-            tanh_half[c] = held([P, JC, 4], F32, "tanh_half%d" % c)
+            slot = c if c < NJ else NJ - 4 + (c - NJ) % 4
+            tanh_half[c] = held([P, JC, 4], F32, "tanh_half%d" % c, "tanh_half%d" % slot)
             nc.scalar.activation(tanh_half[c][:], bank[:].rearrange("p t j -> p j t"), ACT.Tanh, scale=0.5)
 
         def pocket_stage(c):
@@ -271,35 +277,53 @@ def tile_list_kinase_selectivity_kernel(
                     rhs=rhs, rhs_scale=rhs_scale, start=True, stop=True,
                 )
 
+        def work_tile(kind, c):
+            if "%s%d" % (kind, c) in PLACE:
+                return held([P, JC, 4], F32, "%s%d" % (kind, c))
+            return ring.tile([P, JC, 4], F32, name=kind, tag=kind)
+
         def gate_pocket(c):
-            gated[c] = ring.tile([P, JC, 4], F32, name="gated", tag="gated")
+            gated[c] = work_tile("gated", c)
             nc.vector.scalar_tensor_tensor(
                 gated[c][:], tanh_half[c][:], 1.0, pocket[c][:].rearrange("p t j -> p j t"), ADD, MULT
             )
 
-        silu = held([P, NCHUNK * JC, 4], F32, "silu")
+        spans = SPANS
+        base_of = {c: first for first, last in spans for c in range(first, last)}
+        size_of = {first: last - first for first, last in spans}
 
         def add_shift(c):
-            mixed = ring.tile([P, JC, 4], F32, name="mixed", tag="mixed")
+            mixed = work_tile("mixed", c)
             nc.vector.scalar_tensor_tensor(
                 mixed[:], gated[c][:], 0.5, shift[c][:].rearrange("p t j -> p j t"), MULT, ADD
             )
-            nc.scalar.activation(silu[:, c * JC : (c + 1) * JC, :], mixed[:], ACT.Silu)
+            base = base_of[c]
+            if c == base:
+                silu[base] = held([P, size_of[base] * JC, 4], F32, "silu%d" % base)
+            nc.scalar.activation(silu[base][:, (c - base) * JC : (c - base + 1) * JC, :], mixed[:], ACT.Silu)
 
         def apply_gain(engine, base, first, last):
+            if base not in h_bf:
+                h_bf[base] = held([P, size_of[base] * JC, 4], BF16, "h_bf%d" % base)
+            cols = slice((first - base) * JC, (last - base) * JC)
+            halves = (last - 1) // NJ - first // NJ + 1
+            width = (last - first) * JC // halves
             engine.tensor_tensor(
-                h_bf[base][:, first - base * JC : last - base * JC, :], silu[:, first:last, :],
-                gains[:, first // S, :].unsqueeze(1).to_broadcast([P, last - first, 4]), MULT,
+                h_bf[base][:, cols, :].rearrange("p (b j) t -> p b j t", b=halves),
+                silu[base][:, cols, :].rearrange("p (b j) t -> p b j t", b=halves),
+                gains[:, first // NJ : first // NJ + halves, :].unsqueeze(2).to_broadcast([P, halves, width, 4]), MULT,
             )
 
         def quantise_h(base, c, count):
             cols = slice(c * JC, (c + count) * JC)
+            plane = held([P, count * JC], U8, "h_plane%d" % c)
+            for k in range(count):
+                h_plane[c + k] = plane[:, k * JC :]
+                run_left[c + k] = count - k
             nc.vector.quantize_mx(
-                out=h_codes[:, cols].bitcast(FP8X4), scales=h_plane[:, cols],
+                out=h_codes[:, cols].bitcast(FP8X4), scales=plane[:],
                 in_=h_bf[base][:, (c - base) * JC : (c - base + count) * JC, :].rearrange("p j t -> p (j t)"),
             )
-            for first, chunks in powers_of_two(max(c, NJ), c + count, 2):
-                last_product(first - NJ, chunks)
 
         def last_product(jq, count):
             width = count * JC
@@ -308,15 +332,19 @@ def tile_list_kinase_selectivity_kernel(
             else:
                 bank = psum.tile([P, 2, width], F32, name="out_bank", tag="gate", bufs=2)
                 banks = [bank[:, 0, :], bank[:, 1, :]]
+            step = count if min(run_left[jq], run_left[NJ + jq]) >= count else 1
             for nt in range(2):
                 cols = slice(nt * P, (nt + 1) * P)
-                for b in range(NB):
-                    entries = slice(b * S + jq * JC, b * S + jq * JC + width)
-                    nc.tensor.matmul_mx(
-                        banks[nt], lhsT=wo_codes[b][:, cols].bitcast(FP8X4), lhsT_scale=wo_plane[b][:, cols],
-                        rhs=h_codes[:, entries].bitcast(FP8X4), rhs_scale=h_plane[:, entries],
-                        start=(b == 0), stop=(b == NB - 1),
-                    )
+                for k in range(0, count, step):
+                    for b in range(NB):
+                        c = b * NJ + jq + k
+                        nc.tensor.matmul_mx(
+                            banks[nt][:, k * JC : (k + step) * JC],
+                            lhsT=wo_codes[b][:, cols].bitcast(FP8X4), lhsT_scale=wo_plane[b][:, cols],
+                            rhs=h_codes[:, c * JC : (c + step) * JC].bitcast(FP8X4),
+                            rhs_scale=h_plane[c][:, 0 : step * JC],
+                            start=(b == 0), stop=(b == NB - 1),
+                        )
             result = held([P, 2, width], F32, "result%d" % jq)
             if jq == NJ - 1:
                 nc.vector.tensor_copy(result[:, 0, :], banks[0])
@@ -327,34 +355,29 @@ def tile_list_kinase_selectivity_kernel(
                 out=out.rearrange("(nt p) j -> p nt j", p=P)[:, :, jq * JC : jq * JC + width], in_=result[:]
             )
 
-        def gpsimd_batch(i):
-            first, last = BATCHES[i]
-            h_bf[first] = held([P, (last - first) * JC, 4], BF16, "h_bf%d" % first, "h_bf")
-            c = first
-            while c < last:
-                after = min(c + (1 if i == 0 else 2), last, NJ if c < NJ else NCHUNK)
-                pending.append((after - 1, first, c * JC, after * JC - (VECTOR_SHARE[i] if after == last else 0)))
-                c = after
+        def visit():
+            order_w4(1)
+            order_w8(1)
+            quantise_wg(1)
 
-        def visit(i):
-            first, last = BATCHES[i]
-            if VECTOR_SHARE[i]:
-                apply_gain(nc.vector, first, last * JC - VECTOR_SHARE[i], last * JC)
-            if i == 0:
-                order_w4(1)
-                order_w8(1)
-                quantise_wg(1)
-            if i == 2:
-                quantise_wo()
-            for c, count in powers_of_two(first, last, 4):
-                quantise_h(first, c, count)
-            if i + 1 < len(BATCHES):
-                gpsimd_batch(i + 1)
-
-        def issue_gpsimd(done):
-            while pending and pending[0][0] <= done:
-                ready, base, first, last = pending.pop(0)
-                apply_gain(nc.gpsimd, base, first, last)
+        def tail():
+            quantise_wo()
+            quantise_h(0, 0, 2)
+            quantise_h(2, 8, 2)
+            last_product(0, 2)
+            quantise_h(2, 2, 2)
+            quantise_h(2, 10, 2)
+            last_product(2, 2)
+            apply_gain(nc.vector, 12, 12, 14)
+            quantise_h(2, 4, 4)
+            quantise_h(12, 12, 2)
+            last_product(4, 2)
+            apply_gain(nc.vector, 14, 14, 15)
+            apply_gain(nc.vector, 14, 15, 16)
+            quantise_h(14, 14, 1)
+            last_product(6, 1)
+            quantise_h(14, 15, 1)
+            last_product(7, 1)
 
         for c in range(NJ):
             gate_stage(c)
@@ -366,10 +389,8 @@ def tile_list_kinase_selectivity_kernel(
         v_words[1].extend(gather_words(tab_w[1], lists, "v_words1", (256,), 256))
 
         gains = held([P, NB, 4], F32, "gains")
-        nc.scalar.copy(gains[:], gain_raw[:, :, 0:13:4])
+        nc.gpsimd.tensor_copy(gains[:], gain_raw[:, :, 0:13:4])
 
-        pending = []
-        gpsimd_batch(0)
         for c in range(PRODUCTS_AHEAD):
             pocket_stage(c)
             shift_stage(c)
@@ -382,19 +403,17 @@ def tile_list_kinase_selectivity_kernel(
                 shift_stage(c + PRODUCTS_AHEAD)
             if c + 1 < NCHUNK:
                 gate_pocket(c + 1)
-            if c == 0:
-                v_words[1].extend(gather_words(tab_w[1], lists, "v_words1", (512,), 512))
-            if c in VISIT_AT[:-1]:
-                visit(VISIT_AT.index(c))
-            issue_gpsimd(c - 1)
+            if c == VISIT_AT:
+                visit()
             add_shift(c)
-            if 1 <= c < 5:
-                cast_wg(1, slice(c - 1, c))
-            if c in (8, 9, 10, 11):
-                cast_wo((c - 8) // 2, slice(32 * (c % 2), 32 * (c % 2 + 1)))
-        visit(len(BATCHES) - 1)
-        for c in range(BATCHES[-1][1], NCHUNK):
-            h_bf[c] = held([P, JC, 4], BF16, "h_bf%d" % c)
-            apply_gain(nc.vector, c, c * JC, (c + 1) * JC)
-        for c in range(BATCHES[-1][1], NCHUNK):
-            quantise_h(c, c, 1)
+            for first, last in GPSIMD_RUNS:
+                if max(last - 1, VISIT_AT if first >= 2 else 0) == c:
+                    apply_gain(nc.gpsimd, base_of[first], first, last)
+            if c == 1:
+                v_words[1].extend(gather_words(tab_w[1], lists, "v_words1", (512,), 512))
+            if c < 2:
+                cast_wg(1, slice(2 * c, 2 * c + 1))
+                cast_wg(1, slice(2 * c + 1, 2 * c + 2))
+            if c in (11, 12):
+                cast_wo(c - 11, slice(0, 64))
+        tail()

@@ -1,6 +1,7 @@
 from contextlib import ExitStack
 
 import concourse.mybir as mybir
+from concourse.masks import make_identity
 
 K, K2, T, T2, S, H, N = 1024, 512, 2048, 4096, 1024, 1024, 256
 FLOPS = 2 * S * (K * H + 2 * K2 * H + H * N)
@@ -22,22 +23,24 @@ JC = 128
 NJ = S // JC
 NB = H // 512
 NCHUNK = NB * NJ
-PRODUCTS_AHEAD = 2
 LATE_GATES_FROM = 4
-GPSIMD_RUNS = ((0, 1), (1, 2), (2, 3), (3, 4), (4, 6), (6, 8), (8, 10), (10, 12))
-SPANS = ((0, 2), (2, 12), (12, 14), (14, 16))
-VISIT_AT = 3
+GPSIMD_RUNS = ((0, 1), (1, 2), (2, 4), (4, 6), (6, 8), (8, 10), (10, 12))
+VECTOR_RUNS = ((12, 13), (13, 14), (14, 15), (15, 16))
+FIRST_VISIT, SECOND_VISIT, THIRD_VISIT = 3, 9, 14
+H_TILES = ((0, 2), (2, 6), (6, 10), (10, 12), (12, 16))
 KIB = 1024
 PLACE = {
     "tanh_half2": 0, "v_words1_512": 0,
-    "mixed3": 2 * KIB, "w8_raw1": 3 * KIB, "h_bf2": 4 * KIB, "w4_raw1": 6 * KIB, "wg_bf1": 12 * KIB, "gated5": 14 * KIB,
-    "silu0": 16 * KIB, "w4_codes1": 16 * KIB, "wg_plane1": 18 * KIB, "w8_codes1": 19 * KIB,
-    "tanh_half5": 26 * KIB, "tanh_half6": 28 * KIB, "tanh_half7": 30 * KIB, "tanh_half4": 32 * KIB,
-    "mixed11": 34 * KIB, "wo_bf": 34 * KIB, "h_bf12": 34 * KIB,
-    "silu2": 40 * KIB, "h_bf14": 42 * KIB, "wo_plane": 44 * KIB,
-    "h_plane0": 45 * KIB, "h_plane2": 46 * KIB, "h_plane4": 47 * KIB, "h_plane8": 48 * KIB, "h_plane10": 49 * KIB,
+    "mixed4": 2 * KIB, "w8_raw1": 5 * KIB, "h_bf2": 6 * KIB, "w4_raw1": 7 * KIB, "wg_bf1": 9 * KIB, "gated5": 11 * KIB,
+    "h_bf0": 14 * KIB, "h_bf6": 14 * KIB, "h_bf10": 14 * KIB,
+    "silu1": 24 * KIB, "w4_codes1": 22 * KIB + 64, "wg_plane1": 24 * KIB + 128, "w8_codes1": 26 * KIB - 64,
+    "tanh_half4": 28 * KIB, "tanh_half5": 30 * KIB, "tanh_half6": 32 * KIB, "tanh_half7": 34 * KIB,
+    "silu4": 40 * KIB, "gated11": 40 * KIB, "h_plane0": 42 * KIB, "h_plane2": 43 * KIB, "wo_plane": 43 * KIB + 512,
+    "silu8": 44 * KIB, "mixed14": 44 * KIB, "h_plane4": 47 * KIB, "h_plane6": 47 * KIB + 256,
+    "tab2_w": 52 * KIB, "mixed6": 52 * KIB, "silu6": 56 * KIB, "mixed10": 60 * KIB, "mixed8": 64 * KIB,
+    "tab_w0": 68 * KIB, "silu2": 68 * KIB, "mixed2": 72 * KIB,
+    "silu10": 48 * KIB, "h_plane10": 48 * KIB, "h_plane12": 49 * KIB,
 }
-EARLY_GATE_BANKS = ("gate", "gate", "shift", "shift", "shift", "gate", "gate", "shift")
 W8, W4A, W4B = range(3)
 LAST_ROWS = P - 16
 
@@ -62,7 +65,7 @@ def tile_list_kinase_selectivity_kernel(
         keep = ctx.enter_context(tc.tile_pool(name="keep", bufs=1))
         ring = ctx.enter_context(tc.tile_pool(name="ring", bufs=4))
         arena = ctx.enter_context(tc.tile_pool(name="arena", bufs=1))
-        psum = ctx.enter_context(tc.psum_pool(name="psum", bufs=3))
+        psum = ctx.enter_context(tc.psum_pool(name="psum", bufs=7))
 
         def held(shape, dtype, name, place=None):
             place = place or name
@@ -83,8 +86,12 @@ def tile_list_kinase_selectivity_kernel(
         nc.gpsimd.memset(tab2_s[:].bitcast(I32)[96:LAST_ROWS, :], 0)
         nc.gpsimd.memset(tab_s[:].bitcast(I32), 0)
         nc.vector.memset(ws_raw[:].bitcast(I32)[96:LAST_ROWS], 0)
+        gain_rows = held([P, P], F32, "gain_rows")
+        identity = held([P, P], F32, "identity")
+        nc.gpsimd.memset(gain_rows[:], 0.0)
         nc.gpsimd.memset(planes[:].bitcast(I32), 0)
         nc.gpsimd.memset(v_planes[1][:].bitcast(I32), 0)
+        make_identity(nc, identity[:])
 
         def load_wg(b):
             wg_raw[b] = held([P, 4, 512], F32, "wg_raw%d" % b)
@@ -222,10 +229,12 @@ def tile_list_kinase_selectivity_kernel(
         quantise_wg(0)
         v2_words = gather_words(tab2_w, list2, "v2_words", (512, 512))
         load_wg(1)
+        load_wo(0)
         gain_raw = held([P, NB, 16], F32, "gain_raw")
         gain_runs = gain.rearrange("(b u x) -> u b x", b=NB, x=16)
         for e in range(4):
             nc.sync.dma_start(out=gain_raw[e:P:4, :, 0:13], in_=gain_runs[:, :, e : e + 13])
+        load_wo(1)
         load_w4(1, held([P, 512], I32, "w4_raw1")[:])
         load_w8(1, held([P, 512], I32, "w8_raw1")[:])
 
@@ -242,8 +251,7 @@ def tile_list_kinase_selectivity_kernel(
         def gate_stage(c):
             b, jq = divmod(c, NJ)
             rhs, rhs_scale = moving(v2_words, v2_plane, jq)
-            tag = EARLY_GATE_BANKS[c] if c < NJ else "gate"
-            bank = psum.tile([P, 4, JC], F32, name="gate", tag=tag, bufs=2 if tag == "gate" else 3)
+            bank = psum.tile([P, 4, JC], F32, name="gate", tag="bank")
             for t in range(4):
                 cols = slice(t * P, (t + 1) * P)
                 nc.tensor.matmul_mx(
@@ -256,7 +264,7 @@ def tile_list_kinase_selectivity_kernel(
 
         def pocket_stage(c):
             b, jq = divmod(c, NJ)
-            pocket[c] = psum.tile([P, 4, JC], F32, name="pocket", tag="pocket")
+            pocket[c] = psum.tile([P, 4, JC], F32, name="pocket", tag="bank")
             for t in range(4):
                 for a in range(2):
                     rhs, rhs_scale = moving(v_words[a], v_plane[a], jq)
@@ -268,7 +276,7 @@ def tile_list_kinase_selectivity_kernel(
 
         def shift_stage(c):
             b, jq = divmod(c, NJ)
-            shift[c] = psum.tile([P, 4, JC], F32, name="shift", tag="shift")
+            shift[c] = psum.tile([P, 4, JC], F32, name="shift", tag="bank")
             rhs, rhs_scale = moving(v2_words, v2_plane, jq)
             for t in range(4):
                 nc.tensor.matmul_mx(
@@ -288,30 +296,30 @@ def tile_list_kinase_selectivity_kernel(
                 gated[c][:], tanh_half[c][:], 1.0, pocket[c][:].rearrange("p t j -> p j t"), ADD, MULT
             )
 
-        spans = SPANS
-        base_of = {c: first for first, last in spans for c in range(first, last)}
-        size_of = {first: last - first for first, last in spans}
+        runs = sorted(GPSIMD_RUNS + VECTOR_RUNS)
+        run_of = {c: run for run in runs for c in range(*run)}
+        mixed = {}
 
         def add_shift(c):
-            mixed = work_tile("mixed", c)
+            first, last = run_of[c]
+            if c == first:
+                mixed[first] = held([P, (last - first) * JC, 4], F32, "mixed%d" % first)
             nc.vector.scalar_tensor_tensor(
-                mixed[:], gated[c][:], 0.5, shift[c][:].rearrange("p t j -> p j t"), MULT, ADD
+                mixed[first][:, (c - first) * JC : (c - first + 1) * JC, :], gated[c][:], 0.5,
+                shift[c][:].rearrange("p t j -> p j t"), MULT, ADD,
             )
-            base = base_of[c]
-            if c == base:
-                silu[base] = held([P, size_of[base] * JC, 4], F32, "silu%d" % base)
-            nc.scalar.activation(silu[base][:, (c - base) * JC : (c - base + 1) * JC, :], mixed[:], ACT.Silu)
+            if c == last - 1:
+                silu[first] = held([P, (last - first) * JC, 4], F32, "silu%d" % first)
+                nc.scalar.activation(silu[first][:], mixed[first][:], ACT.Silu)
 
-        def apply_gain(engine, base, first, last):
+        def apply_gain(engine, source, first, last):
+            base, end = [span for span in H_TILES if span[0] <= first < span[1]][0]
             if base not in h_bf:
-                h_bf[base] = held([P, size_of[base] * JC, 4], BF16, "h_bf%d" % base)
-            cols = slice((first - base) * JC, (last - base) * JC)
-            halves = (last - 1) // NJ - first // NJ + 1
-            width = (last - first) * JC // halves
+                h_bf[base] = held([P, (end - base) * JC, 4], BF16, "h_bf%d" % base)
+            b = first // NJ
             engine.tensor_tensor(
-                h_bf[base][:, cols, :].rearrange("p (b j) t -> p b j t", b=halves),
-                silu[base][:, cols, :].rearrange("p (b j) t -> p b j t", b=halves),
-                gains[:, first // NJ : first // NJ + halves, :].unsqueeze(2).to_broadcast([P, halves, width, 4]), MULT,
+                h_bf[base][:, (first - base) * JC : (last - base) * JC, :], silu[first][:],
+                source[:, 4 * b : 4 * b + 4].unsqueeze(1).to_broadcast([P, (last - first) * JC, 4]), MULT,
             )
 
         def quantise_h(base, c, count):
@@ -327,26 +335,23 @@ def tile_list_kinase_selectivity_kernel(
 
         def last_product(jq, count):
             width = count * JC
-            if jq == NJ - 1:
-                banks = [psum.tile([P, width], F32, name="out_bank", tag=tag)[:] for tag in ("pocket", "shift")]
+            apart = jq == NJ - 1
+            if apart:
+                banks = [psum.tile([P, width], F32, name="out_bank", tag="bank")[:] for nt in range(2)]
             else:
-                bank = psum.tile([P, 2, width], F32, name="out_bank", tag="gate", bufs=2)
+                bank = psum.tile([P, 2, width], F32, name="out_bank", tag="bank")
                 banks = [bank[:, 0, :], bank[:, 1, :]]
-            step = count if min(run_left[jq], run_left[NJ + jq]) >= count else 1
-            for nt in range(2):
-                cols = slice(nt * P, (nt + 1) * P)
-                for k in range(0, count, step):
-                    for b in range(NB):
-                        c = b * NJ + jq + k
-                        nc.tensor.matmul_mx(
-                            banks[nt][:, k * JC : (k + step) * JC],
-                            lhsT=wo_codes[b][:, cols].bitcast(FP8X4), lhsT_scale=wo_plane[b][:, cols],
-                            rhs=h_codes[:, c * JC : (c + step) * JC].bitcast(FP8X4),
-                            rhs_scale=h_plane[c][:, 0 : step * JC],
-                            start=(b == 0), stop=(b == NB - 1),
-                        )
+            for b in range(NB):
+                c = b * NJ + jq
+                for nt in range(2):
+                    cols = slice(nt * P, (nt + 1) * P)
+                    nc.tensor.matmul_mx(
+                        banks[nt], lhsT=wo_codes[b][:, cols].bitcast(FP8X4), lhsT_scale=wo_plane[b][:, cols],
+                        rhs=h_codes[:, c * JC : c * JC + width].bitcast(FP8X4), rhs_scale=h_plane[c][:, 0:width],
+                        start=(b == 0 and (apart or nt == 0)), stop=(b == NB - 1 and (apart or nt == 1)),
+                    )
             result = held([P, 2, width], F32, "result%d" % jq)
-            if jq == NJ - 1:
+            if apart:
                 nc.vector.tensor_copy(result[:, 0, :], banks[0])
                 nc.scalar.copy(result[:, 1, :], banks[1])
             else:
@@ -355,65 +360,69 @@ def tile_list_kinase_selectivity_kernel(
                 out=out.rearrange("(nt p) j -> p nt j", p=P)[:, :, jq * JC : jq * JC + width], in_=result[:]
             )
 
-        def visit():
-            order_w4(1)
-            order_w8(1)
-            quantise_wg(1)
-
-        def tail():
-            quantise_wo()
-            quantise_h(0, 0, 2)
-            quantise_h(2, 8, 2)
-            last_product(0, 2)
-            quantise_h(2, 2, 2)
-            quantise_h(2, 10, 2)
-            last_product(2, 2)
-            apply_gain(nc.vector, 12, 12, 14)
-            quantise_h(2, 4, 4)
-            quantise_h(12, 12, 2)
-            last_product(4, 2)
-            apply_gain(nc.vector, 14, 14, 15)
-            apply_gain(nc.vector, 14, 15, 16)
-            quantise_h(14, 14, 1)
-            last_product(6, 1)
-            quantise_h(14, 15, 1)
-            last_product(7, 1)
-
         for c in range(NJ):
             gate_stage(c)
         v_words = [gather_words(tab_w[0], lists, "v_words0", (1024,))]
         for b in range(NB):
-            load_wo(b)
+            nc.sync.dma_start(
+                out=gain_rows[4 * b : 4 * b + 4, :].rearrange("t (u e) -> t u e", e=4),
+                in_=gain[512 * b : 512 * (b + 1)].rearrange("(u t e) -> t u e", t=4, e=4),
+            )
         v_words.append(gather_words(tab_w[1], lists, "v_words1", (256,)))
         order_w8(0)
         v_words[1].extend(gather_words(tab_w[1], lists, "v_words1", (256,), 256))
 
-        gains = held([P, NB, 4], F32, "gains")
-        nc.gpsimd.tensor_copy(gains[:], gain_raw[:, :, 0:13:4])
 
-        for c in range(PRODUCTS_AHEAD):
-            pocket_stage(c)
-            shift_stage(c)
+        pocket_stage(0)
+        pocket_stage(1)
+        shift_stage(0)
+        gains = held([P, NB * 4], F32, "gains")
+        nc.gpsimd.tensor_copy(gains[:].rearrange("p (b t) -> p b t", t=4), gain_raw[:, :, 0:13:4])
+        gain_bank = psum.tile([P, P], F32, name="gain_bank", tag="gain_bank", bufs=1)
         gate_pocket(0)
         for c in range(NCHUNK):
+            if c + 2 < NCHUNK:
+                pocket_stage(c + 2)
+            if c + 1 < NCHUNK:
+                shift_stage(c + 1)
             if LATE_GATES_FROM <= c < LATE_GATES_FROM + NJ:
                 gate_stage(NJ + c - LATE_GATES_FROM)
-            if c + PRODUCTS_AHEAD < NCHUNK:
-                pocket_stage(c + PRODUCTS_AHEAD)
-                shift_stage(c + PRODUCTS_AHEAD)
+            if c == LATE_GATES_FROM + NJ:
+                nc.tensor.transpose(gain_bank[:], gain_rows[:], identity[:])
             if c + 1 < NCHUNK:
                 gate_pocket(c + 1)
-            if c == VISIT_AT:
-                visit()
+            if c == SECOND_VISIT:
+                quantise_wo()
+                quantise_h(2, 2, 2)
+                quantise_h(0, 0, 2)
+                apply_gain(nc.gpsimd, gains, 6, 8)
+            if c == THIRD_VISIT:
+                quantise_h(2, 4, 2)
+                quantise_h(6, 6, 4)
+                last_product(0, 2)
+                apply_gain(nc.gpsimd, gains, 10, 12)
             add_shift(c)
+            if c == FIRST_VISIT:
+                order_w4(1)
+                order_w8(1)
+                quantise_wg(1)
             for first, last in GPSIMD_RUNS:
-                if max(last - 1, VISIT_AT if first >= 2 else 0) == c:
-                    apply_gain(nc.gpsimd, base_of[first], first, last)
+                if last - 1 == c and first not in (6, 10):
+                    apply_gain(nc.gpsimd, gains, first, last)
             if c == 1:
                 v_words[1].extend(gather_words(tab_w[1], lists, "v_words1", (512,), 512))
             if c < 2:
                 cast_wg(1, slice(2 * c, 2 * c + 1))
                 cast_wg(1, slice(2 * c + 1, 2 * c + 2))
-            if c in (11, 12):
-                cast_wo(c - 11, slice(0, 64))
-        tail()
+            if c in (2, 3):
+                cast_wo(c - 2, slice(0, 64))
+        for c in (12, 13, 14):
+            apply_gain(nc.vector, gain_bank, c, c + 1)
+        quantise_h(10, 10, 2)
+        last_product(2, 2)
+        quantise_h(12, 12, 2)
+        last_product(4, 2)
+        apply_gain(nc.vector, gain_bank, 15, 16)
+        for c in (14, 15):
+            quantise_h(12, c, 1)
+            last_product(c - NJ, 1)

@@ -262,17 +262,25 @@ def tile_list_kinase_selectivity_kernel(
             tanh_half[c] = held([P, JC, 4], F32, "tanh_half%d" % c, "tanh_half%d" % slot)
             nc.scalar.activation(tanh_half[c][:], bank[:].rearrange("p t j -> p j t"), ACT.Tanh, scale=0.5)
 
-        def pocket_stage(c):
+        def pocket_pass(c, t, a, start, stop):
             b, jq = divmod(c, NJ)
+            rhs, rhs_scale = moving(v_words[a], v_plane[a], jq)
+            nc.tensor.matmul_mx(
+                pocket[c][:, t, :], lhsT=w4_codes[b][:, a, t, :].bitcast(FP4X4),
+                lhsT_scale=weight_plane(W4A + a, b, t), rhs=rhs, rhs_scale=rhs_scale, start=start, stop=stop,
+            )
+
+        def pocket_stage(c):
             pocket[c] = psum.tile([P, 4, JC], F32, name="pocket", tag="bank")
             for t in range(4):
                 for a in range(2):
-                    rhs, rhs_scale = moving(v_words[a], v_plane[a], jq)
-                    nc.tensor.matmul_mx(
-                        pocket[c][:, t, :], lhsT=w4_codes[b][:, a, t, :].bitcast(FP4X4),
-                        lhsT_scale=weight_plane(W4A + a, b, t),
-                        rhs=rhs, rhs_scale=rhs_scale, start=(a == 0), stop=(a == 1),
-                    )
+                    pocket_pass(c, t, a, a == 0, a == 1)
+
+        def early_pocket(c, a):
+            if a == 0:
+                pocket[c] = psum.tile([P, 4, JC], F32, name="pocket", tag="bank")
+            for t in range(4):
+                pocket_pass(c, t, a, a == 0 and t == 0, a == 1 and t == 3)
 
         def shift_stage(c):
             b, jq = divmod(c, NJ)
@@ -317,10 +325,12 @@ def tile_list_kinase_selectivity_kernel(
             if base not in h_bf:
                 h_bf[base] = held([P, (end - base) * JC, 4], BF16, "h_bf%d" % base)
             b = first // NJ
-            engine.tensor_tensor(
-                h_bf[base][:, (first - base) * JC : (last - base) * JC, :], silu[first][:],
-                source[:, 4 * b : 4 * b + 4].unsqueeze(1).to_broadcast([P, (last - first) * JC, 4]), MULT,
-            )
+            target = h_bf[base][:, (first - base) * JC : (last - base) * JC, :]
+            factor = source[:, 4 * b : 4 * b + 4].unsqueeze(1).to_broadcast([P, (last - first) * JC, 4])
+            if source is gains:
+                engine.tensor_tensor(target, silu[first][:], factor, MULT)
+            else:
+                engine.scalar_tensor_tensor(target, silu[first][:], 1.0, factor, MULT, MULT)
 
         def quantise_h(base, c, count):
             cols = slice(c * JC, (c + count) * JC)
@@ -368,13 +378,15 @@ def tile_list_kinase_selectivity_kernel(
                 out=gain_rows[4 * b : 4 * b + 4, :].rearrange("t (u e) -> t u e", e=4),
                 in_=gain[512 * b : 512 * (b + 1)].rearrange("(u t e) -> t u e", t=4, e=4),
             )
+        for c in range(2):
+            early_pocket(c, 0)
         v_words.append(gather_words(tab_w[1], lists, "v_words1", (256,)))
         order_w8(0)
         v_words[1].extend(gather_words(tab_w[1], lists, "v_words1", (256,), 256))
 
 
-        pocket_stage(0)
-        pocket_stage(1)
+        for c in range(2):
+            early_pocket(c, 1)
         shift_stage(0)
         gains = held([P, NB * 4], F32, "gains")
         nc.gpsimd.tensor_copy(gains[:].rearrange("p (b t) -> p b t", t=4), gain_raw[:, :, 0:13:4])

@@ -30,6 +30,7 @@ FIRST_VISIT, SECOND_VISIT, THIRD_VISIT = 3, 9, 14
 H_TILES = ((0, 2), (2, 6), (6, 10), (10, 12), (12, 16))
 KIB = 1024
 PLACE = {
+    "w8_raw0": 14 * KIB + 6 * KIB, "gain_rows": 20 * KIB, "identity": 21 * KIB,
     "tanh_half2": 0, "v_words1_512": 0,
     "mixed4": 2 * KIB, "w8_raw1": 5 * KIB, "h_bf2": 6 * KIB, "w4_raw1": 7 * KIB, "wg_bf1": 9 * KIB, "gated5": 11 * KIB,
     "h_bf0": 14 * KIB, "h_bf6": 14 * KIB, "h_bf10": 14 * KIB,
@@ -42,7 +43,6 @@ PLACE = {
     "silu10": 48 * KIB, "h_plane10": 48 * KIB, "h_plane12": 49 * KIB,
 }
 W8, W4A, W4B = range(3)
-LAST_ROWS = P - 16
 
 
 def powers_of_two(first, last, most):
@@ -77,21 +77,16 @@ def tile_list_kinase_selectivity_kernel(
         list2 = keep.tile([P, S // 16], U16, name="list2")
         tab_s = held([P, T], U8, "tab_s")
         tab2_s = held([P, T2], U8, "tab2_s")
-        ws_raw = held([P, 3, H], U8, "ws_raw")
+        ws_raw = held([P, 3, 512], U8, "ws_raw")
         planes = held([P, S + 3 * H], U8, "planes")
         wg_raw, w4_raw, w8_raw, wo_raw, tab_w = {}, {}, {}, {}, {}
 
         v_planes = [held([P, S], U8, "v_plane%d" % a) for a in range(2)]
+        nc.gpsimd.memset(tab2_s[:].bitcast(I32)[96:P, :], 0)
         nc.vector.memset(tab2_s[:].bitcast(I32)[0:96, :], 0)
-        nc.gpsimd.memset(tab2_s[:].bitcast(I32)[96:LAST_ROWS, :], 0)
         nc.gpsimd.memset(tab_s[:].bitcast(I32), 0)
-        nc.vector.memset(ws_raw[:].bitcast(I32)[96:LAST_ROWS], 0)
-        gain_rows = held([P, P], F32, "gain_rows")
-        identity = held([P, P], F32, "identity")
-        nc.gpsimd.memset(gain_rows[:], 0.0)
-        nc.gpsimd.memset(planes[:].bitcast(I32), 0)
+        nc.vector.memset(planes[:].bitcast(I32), 0)
         nc.gpsimd.memset(v_planes[1][:].bitcast(I32), 0)
-        make_identity(nc, identity[:])
 
         def load_wg(b):
             wg_raw[b] = held([P, 4, 512], F32, "wg_raw%d" % b)
@@ -124,13 +119,16 @@ def tile_list_kinase_selectivity_kernel(
                 nc.sync.dma_start(out=wo_raw[b][:, t, :], in_=rows[t])
 
         nc.sync.dma_start(list2[:], offs2)
-        nc.sync.dma_start(out=tab2_s[:].bitcast(I32)[LAST_ROWS:P, :], in_=tab2_scales[0].bitcast(I32))
         nc.sync.dma_start(lists[:], offs)
         nc.sync.dma_start(
-            out=ws_raw[:].bitcast(I32)[LAST_ROWS:P, 1:3, :], in_=w4_scales.bitcast(I32).rearrange("a q c -> q a c")
+            out=ws_raw[:].bitcast(I32)[96:P, 1:3, :],
+            in_=w4_scales.bitcast(I32).rearrange("a q (b c) -> (q b) a c", b=NB),
         )
-        nc.sync.dma_start(out=ws_raw[:].bitcast(I32)[LAST_ROWS:P, 0, :], in_=w8_scales[0].bitcast(I32))
+        nc.sync.dma_start(
+            out=ws_raw[:].bitcast(I32)[96:P, 0, :], in_=w8_scales[0].bitcast(I32).rearrange("q (b c) -> (q b) c", b=NB)
+        )
         load_w4(0, held([P, 512], I32, "w4_raw0")[:])
+        nc.sync.dma_start(out=tab2_s[:].bitcast(I32)[96:P:2, :], in_=tab2_scales[0].bitcast(I32))
         load_wg(0)
         tab_s32 = tab_s[:].bitcast(I32)
         by_parity = tab_scales[0].bitcast(I32).rearrange("(i o) c -> o i c", o=2)
@@ -201,14 +199,15 @@ def tile_list_kinase_selectivity_kernel(
         v2_picked = held([P, S], U8, "v2_picked")
         nc.vector.tensor_copy(v2_picked[:], tab2_s[:].indirect(list2[:]))
         planes32 = planes[:].bitcast(I32)
-        staged = held([P, (S + 3 * H) // 4], I32, "staged")
+        half = 3 * 512 // 4
+        staged = held([P, S // 4 + half], I32, "staged")
         nc.vector.tensor_copy(
-            staged[96:P, S // 4 :].rearrange("p (b x t u) -> p b t x u", b=NB, x=3, t=4),
-            ws_raw[:].bitcast(I32)[96:P].rearrange("p x (b u t) -> p b t x u", b=NB, t=4),
+            staged[96:P, S // 4 :].rearrange("p (x t u) -> p t x u", x=3, t=4),
+            ws_raw[:].bitcast(I32)[96:P].rearrange("p x (u t) -> p t x u", t=4),
         )
         nc.vector.tensor_copy(staged[96:P, 0 : S // 4], v2_picked[:].bitcast(I32)[96:P, :])
         for r in range(4):
-            nc.sync.dma_start(out=planes32[r:P:32, :], in_=staged[LAST_ROWS + r : P : 4, :])
+            nc.sync.dma_start(out=planes32[r:P:32, 0 : S // 4 + half], in_=staged[96 + 2 * r : P : 8, :])
         tab_w[0] = load_table("tab_w0", tab_words[0], T)
         order_w4(0)
         cast_wg(0, slice(0, 4))
@@ -237,6 +236,8 @@ def tile_list_kinase_selectivity_kernel(
         load_wo(1)
         load_w4(1, held([P, 512], I32, "w4_raw1")[:])
         load_w8(1, held([P, 512], I32, "w8_raw1")[:])
+        for r in range(4):
+            nc.sync.dma_start(out=planes32[r:P:32, S // 4 + half :], in_=staged[97 + 2 * r : P : 8, S // 4 :])
 
         tanh_half, pocket, shift, gated, silu, h_bf = {}, {}, {}, {}, {}, {}
         h_codes = held([P, NCHUNK * JC], U32, "h_codes")
@@ -373,15 +374,19 @@ def tile_list_kinase_selectivity_kernel(
         for c in range(NJ):
             gate_stage(c)
         v_words = [gather_words(tab_w[0], lists, "v_words0", (1024,))]
+        for c in range(2):
+            early_pocket(c, 0)
+        v_words.append(gather_words(tab_w[1], lists, "v_words1", (256,)))
+        order_w8(0)
+        gain_rows = held([P, P], F32, "gain_rows")
+        identity = held([P, P], F32, "identity")
+        nc.gpsimd.memset(gain_rows[:], 0.0)
+        make_identity(nc, identity[:])
         for b in range(NB):
             nc.sync.dma_start(
                 out=gain_rows[4 * b : 4 * b + 4, :].rearrange("t (u e) -> t u e", e=4),
                 in_=gain[512 * b : 512 * (b + 1)].rearrange("(u t e) -> t u e", t=4, e=4),
             )
-        for c in range(2):
-            early_pocket(c, 0)
-        v_words.append(gather_words(tab_w[1], lists, "v_words1", (256,)))
-        order_w8(0)
         v_words[1].extend(gather_words(tab_w[1], lists, "v_words1", (256,), 256))
 
 

@@ -327,7 +327,8 @@ def tile_list_kinase_selectivity_kernel(
                 h_bf[base] = held([P, (end - base) * JC, 4], BF16, "h_bf%d" % base)
             b = first // NJ
             target = h_bf[base][:, (first - base) * JC : (last - base) * JC, :]
-            factor = source[:, 4 * b : 4 * b + 4].unsqueeze(1).to_broadcast([P, (last - first) * JC, 4])
+            columns = slice(4 * b, 4 * b + 4) if source is gains else slice(0, 4)
+            factor = source[:, columns].unsqueeze(1).to_broadcast([P, (last - first) * JC, 4])
             if source is gains:
                 engine.tensor_tensor(target, silu[first][:], factor, MULT)
             else:
@@ -382,11 +383,10 @@ def tile_list_kinase_selectivity_kernel(
         identity = held([P, P], F32, "identity")
         nc.gpsimd.memset(gain_rows[:], 0.0)
         make_identity(nc, identity[:])
-        for b in range(NB):
-            nc.sync.dma_start(
-                out=gain_rows[4 * b : 4 * b + 4, :].rearrange("t (u e) -> t u e", e=4),
-                in_=gain[512 * b : 512 * (b + 1)].rearrange("(u t e) -> t u e", t=4, e=4),
-            )
+        nc.sync.dma_start(
+            out=gain_rows[0:4, :].rearrange("t (u e) -> t u e", e=4),
+            in_=gain[512:H].rearrange("(u t e) -> t u e", t=4, e=4),
+        )
         v_words[1].extend(gather_words(tab_w[1], lists, "v_words1", (256,), 256))
 
 

@@ -17,43 +17,24 @@ FP4X4 = mybir.dt.float4_e2m1fn_x4
 ACT = mybir.ActivationFunctionType
 ADD = mybir.AluOpType.add
 MULT = mybir.AluOpType.mult
+BYTES_OF = {F32: 4, BF16: 2, I32: 4, U32: 4, U8: 1}
 
 P = 128
-JC = 128
-NJ = S // JC
-NB = H // 512
-NCHUNK = NB * NJ
-LATE_GATES_FROM = 4
-GPSIMD_RUNS = ((0, 1), (1, 2), (2, 4), (4, 6), (6, 8), (8, 10), (10, 12))
-VECTOR_RUNS = ((12, 13), (13, 14), (14, 15), (15, 16))
-FIRST_VISIT, SECOND_VISIT, THIRD_VISIT = 3, 9, 14
-H_TILES = ((0, 2), (2, 6), (6, 10), (10, 12), (12, 16))
 KIB = 1024
-PLACE = {
-    "w8_raw0": 14 * KIB + 6 * KIB, "gain_rows": 20 * KIB, "identity": 21 * KIB,
-    "tanh_half2": 0, "v_words1_512": 0,
-    "mixed4": 2 * KIB, "w8_raw1": 5 * KIB, "h_bf2": 6 * KIB, "w4_raw1": 7 * KIB, "wg_bf1": 9 * KIB, "gated5": 11 * KIB,
-    "h_bf0": 14 * KIB, "h_bf6": 14 * KIB, "h_bf10": 14 * KIB,
-    "silu1": 24 * KIB, "w4_codes1": 22 * KIB + 64, "wg_plane1": 24 * KIB + 128, "w8_codes1": 26 * KIB - 64,
-    "tanh_half4": 28 * KIB, "tanh_half5": 30 * KIB, "tanh_half6": 32 * KIB, "tanh_half7": 34 * KIB,
-    "silu4": 40 * KIB, "gated11": 40 * KIB, "h_plane0": 42 * KIB, "h_plane2": 43 * KIB, "wo_plane": 43 * KIB + 512,
-    "silu8": 44 * KIB, "mixed14": 44 * KIB, "h_plane4": 47 * KIB, "h_plane6": 47 * KIB + 256,
-    "tab2_w": 52 * KIB, "mixed6": 52 * KIB, "silu6": 56 * KIB, "mixed10": 60 * KIB, "mixed8": 64 * KIB,
-    "tab_w0": 68 * KIB, "silu2": 68 * KIB, "mixed2": 72 * KIB,
-    "silu10": 48 * KIB, "h_plane10": 48 * KIB, "h_plane12": 49 * KIB,
-}
-W8, W4A, W4B = range(3)
-
-
-def powers_of_two(first, last, most):
-    pieces = []
-    while first < last:
-        count = most
-        while first + count > last:
-            count = count // 2
-        pieces.append((first, count))
-        first = first + count
-    return pieces
+W4A, W4B, W8 = range(3)
+V2_ROW = 4
+SPANS = (
+    (0, 0, 128), (0, 128, 128), (0, 256, 256), (0, 512, 256), (0, 768, 256),
+    (1, 0, 256), (1, 256, 256), (1, 512, 256), (1, 768, 128), (1, 896, 128),
+)
+UNITS = [
+    (span, slots)
+    for span, (b, j0, width) in enumerate(SPANS)
+    for slots in (((0, 1, 2, 3),) if width == 128 else ((0, 1), (2, 3)))
+]
+NUNIT = len(UNITS)
+FIRST_VISIT, SECOND_VISIT = 4, 13
+EARLY_GATE_BANKS, LATE_GATE_BANKS, POCKET_BANKS, SHIFT_BANKS = (0, 1, 7), (0, 1), (2, 3, 4), (5, 6)
 
 
 def tile_list_kinase_selectivity_kernel(
@@ -63,30 +44,39 @@ def tile_list_kinase_selectivity_kernel(
     nc = tc.nc
     with ExitStack() as ctx:
         keep = ctx.enter_context(tc.tile_pool(name="keep", bufs=1))
-        ring = ctx.enter_context(tc.tile_pool(name="ring", bufs=4))
         arena = ctx.enter_context(tc.tile_pool(name="arena", bufs=1))
-        psum = ctx.enter_context(tc.psum_pool(name="psum", bufs=7))
+        psum = ctx.enter_context(tc.psum_pool(name="psum", bufs=1))
+        place = {"top": 0}
 
-        def held(shape, dtype, name, place=None):
-            place = place or name
-            if place in PLACE:
-                return arena.tile(shape, dtype, name=name, align_bytes=64, offset=PLACE[place])
-            return keep.tile(shape, dtype, name=name, align_bytes=64)
+        def held(shape, dtype, name, over=None, plus=0, room=0):
+            if over is None:
+                size = BYTES_OF[dtype]
+                for extent in shape[1:]:
+                    size = size * extent
+                place[name] = place["top"]
+                place["top"] = place["top"] + max(size, room, 64)
+            else:
+                place[name] = place[over] + plus
+            return arena.tile(shape, dtype, name=name, align_bytes=64, offset=place[name])
+
+        def bank(number, shape):
+            return psum.tile(shape, F32, name="bank%d" % number, tag="bank%d" % number)
 
         lists = keep.tile([P, S // 16], U16, name="lists")
         list2 = keep.tile([P, S // 16], U16, name="list2")
         tab_s = held([P, T], U8, "tab_s")
         tab2_s = held([P, T2], U8, "tab2_s")
-        ws_raw = held([P, 3, 512], U8, "ws_raw")
+        ws_raw = held([P, 3, H], U8, "ws_raw")
+        v2_plane = held([P, S], U8, "v2_plane")
         planes = held([P, S + 3 * H], U8, "planes")
-        wg_raw, w4_raw, w8_raw, wo_raw, tab_w = {}, {}, {}, {}, {}
-
-        v_planes = [held([P, S], U8, "v_plane%d" % a) for a in range(2)]
-        nc.gpsimd.memset(tab2_s[:].bitcast(I32)[96:P, :], 0)
-        nc.vector.memset(tab2_s[:].bitcast(I32)[0:96, :], 0)
+        stage = held([P, S + 3 * H], U8, "stage")
+        nc.vector.memset(tab2_s[:].bitcast(I32)[0:112, :], 0)
         nc.gpsimd.memset(tab_s[:].bitcast(I32), 0)
-        nc.vector.memset(planes[:].bitcast(I32), 0)
-        nc.gpsimd.memset(v_planes[1][:].bitcast(I32), 0)
+        nc.gpsimd.memset(ws_raw[:].bitcast(I32), 0)
+        nc.gpsimd.memset(v2_plane[:].bitcast(I32), 0)
+        nc.gpsimd.memset(planes[:].bitcast(I32), 0)
+
+        wg_raw, wg_bf, wg_codes, wg_plane, w4_codes, w8_codes, wo_raw = {}, {}, {}, {}, {}, {}, {}
 
         def load_wg(b):
             wg_raw[b] = held([P, 4, 512], F32, "wg_raw%d" % b)
@@ -94,17 +84,26 @@ def tile_list_kinase_selectivity_kernel(
                 out=wg_raw[b][:], in_=wg.rearrange("(p j) c -> p j c", j=4)[:, :, 512 * b : 512 * (b + 1)]
             )
 
-        def load_w8(b, raw):
-            w8_raw[b] = raw
-            nc.sync.dma_start(
-                out=raw, in_=w8_words[0].rearrange("p c i -> p (c i)").bitcast(I32)[:, 512 * b : 512 * (b + 1)]
+        def cast_wg_first():
+            wg_bf[0] = held([P, 4, P, 4], BF16, "wg_bf0")
+            nc.scalar.copy(
+                wg_bf[0][:].rearrange("p t (u e) j -> p t u j e", e=4),
+                wg_raw[0][:].rearrange("p j (u t e) -> p t u j e", t=4, e=4),
             )
 
-        def load_w4(b, raw):
-            w4_raw[b] = raw.rearrange("p (a c) -> p a c", a=2)
-            nc.sync.dma_start(
-                out=w4_raw[b],
-                in_=w4_words.bitcast(I32).rearrange("a p c -> p a c")[:, :, 256 * b : 256 * (b + 1)],
+        def cast_wg_second():
+            wg_bf[1] = held([P, 4, P, 4], BF16, "wg_bf1", "tab_w1", 2 * KIB)
+            nc.gpsimd.tensor_scalar(
+                wg_bf[1][:].rearrange("p t (u e) j -> p u t (e j)", e=4),
+                wg_raw[1][:].rearrange("p j c -> p c j"), 1.0, 0.0, MULT, ADD,
+            )
+
+        def quantise_wg(b, over=None):
+            wg_codes[b] = held([P, 512], U32, "wg_codes%d" % b, over)
+            wg_plane[b] = held([P, 512], U8, "wg_plane%d" % b)
+            nc.vector.quantize_mx(
+                out=wg_codes[b][:].bitcast(FP8X4), scales=wg_plane[b][:],
+                in_=wg_bf[b][:].rearrange("p t m j -> p (t m j)"),
             )
 
         def load_table(name, words, width):
@@ -112,83 +111,44 @@ def tile_list_kinase_selectivity_kernel(
             nc.sync.dma_start(out=tile[:].bitcast(I32), in_=words.rearrange("p t i -> p (t i)").bitcast(I32))
             return tile
 
+        w4_raw, w8_raw = {}, {}
+
+        def load_w4(b):
+            w4_raw[b] = held([P, 2, 256], U32, "w4_raw%d" % b)
+            nc.sync.dma_start(
+                out=w4_raw[b][:].bitcast(I32),
+                in_=w4_words.bitcast(I32).rearrange("a p c -> p a c")[:, :, 256 * b : 256 * (b + 1)],
+            )
+
+        def load_w8(b):
+            w8_raw[b] = held([P, 512], U32, "w8_raw%d" % b)
+            nc.sync.dma_start(
+                out=w8_raw[b][:].bitcast(I32),
+                in_=w8_words[0].rearrange("p c i -> p (c i)").bitcast(I32)[:, 512 * b : 512 * (b + 1)],
+            )
+
+        def order_w4(b, move, dtype, over=None):
+            w4_codes[b] = held([P, 2, 4, 256], U8, "w4_codes%d" % b, over)
+            move(
+                w4_codes[b][:].bitcast(dtype).rearrange("p a t (u w) -> p a t u w", w=2),
+                w4_raw[b][:].bitcast(dtype).rearrange("p a (u t w) -> p a t u w", t=4, w=2),
+            )
+
+        def order_w8(b, move, dtype, over=None):
+            w8_codes[b] = held([P, 4, P], U32, "w8_codes%d" % b, over)
+            move(
+                w8_codes[b][:].bitcast(dtype).rearrange("p t (u e) -> p t u e", e=4),
+                w8_raw[b][:].bitcast(dtype).rearrange("p (u t e) -> p t u e", t=4, e=4),
+            )
+
         def load_wo(b):
             wo_raw[b] = held([P, 4, N], F32, "wo_raw%d" % b)
             rows = wo[512 * b : 512 * (b + 1), :].rearrange("(u t e) n -> t u e n", t=4, e=4)
             for t in range(4):
                 nc.sync.dma_start(out=wo_raw[b][:, t, :], in_=rows[t])
 
-        nc.sync.dma_start(list2[:], offs2)
-        nc.sync.dma_start(lists[:], offs)
-        nc.sync.dma_start(
-            out=ws_raw[:].bitcast(I32)[96:P, 1:3, :],
-            in_=w4_scales.bitcast(I32).rearrange("a q (b c) -> (q b) a c", b=NB),
-        )
-        nc.sync.dma_start(
-            out=ws_raw[:].bitcast(I32)[96:P, 0, :], in_=w8_scales[0].bitcast(I32).rearrange("q (b c) -> (q b) c", b=NB)
-        )
-        load_w4(0, held([P, 512], I32, "w4_raw0")[:])
-        nc.sync.dma_start(out=tab2_s[:].bitcast(I32)[96:P:2, :], in_=tab2_scales[0].bitcast(I32))
-        load_wg(0)
-        tab_s32 = tab_s[:].bitcast(I32)
-        by_parity = tab_scales[0].bitcast(I32).rearrange("(i o) c -> o i c", o=2)
-        for o in range(2):
-            nc.sync.dma_start(out=tab_s32[o:P:16, :], in_=by_parity[o])
-        nc.sync.dma_start(out=tab_s32[4:P:8, :], in_=tab_scales[1].bitcast(I32))
-        tab2_w = load_table("tab2_w", tab2_words[0], T2)
-
-        wg_bf, wo_bf = {}, {}
-        wg_codes, wg_plane, w4_codes, w8_codes, wo_codes, wo_plane = {}, {}, {}, {}, {}, {}
-
-        def cast_wg(b, slots):
-            if b not in wg_bf:
-                wg_bf[b] = held([P, 4, P, 4], BF16, "wg_bf%d" % b)
-            nc.scalar.copy(
-                wg_bf[b][:].rearrange("p t (u e) j -> p t u j e", e=4)[:, slots],
-                wg_raw[b][:].rearrange("p j (u t e) -> p t u j e", t=4, e=4)[:, slots],
-            )
-
-        def quantise_wg(b):
-            wg_codes[b] = held([P, 512], U32, "wg_codes%d" % b)
-            wg_plane[b] = held([P, 512], U8, "wg_plane%d" % b)
-            nc.vector.quantize_mx(
-                out=wg_codes[b][:].bitcast(FP8X4), scales=wg_plane[b][:],
-                in_=wg_bf[b][:].rearrange("p t m j -> p (t m j)"),
-            )
-
-        def order_w8(b):
-            w8_codes[b] = held([P, 4, P], U32, "w8_codes%d" % b)
-            nc.vector.tensor_copy(
-                w8_codes[b][:].bitcast(I32).rearrange("p t (u e) -> p t u e", e=4),
-                w8_raw[b].rearrange("p (u t e) -> p t u e", t=4, e=4),
-            )
-
-        def order_w4(b):
-            w4_codes[b] = held([P, 2, 4, 256], U8, "w4_codes%d" % b)
-            nc.vector.tensor_copy(
-                w4_codes[b][:].bitcast(I32).rearrange("p a t (u w) -> p a t u w", w=2),
-                w4_raw[b].rearrange("p a (u t w) -> p a t u w", t=4, w=2),
-            )
-
-        wo_bf_both = held([P, NB, N, 4], BF16, "wo_bf")
-
-        def cast_wo(b, groups):
-            nc.scalar.copy(
-                wo_bf_both[:, b].rearrange("p (c i) t -> p c t i", i=4)[:, groups],
-                wo_raw[b][:].rearrange("p t (c i) -> p c t i", i=4)[:, groups],
-            )
-
-        def quantise_wo():
-            codes = held([P, NB * N], U32, "wo_codes")
-            plane = held([P, NB * N], U8, "wo_plane")
-            nc.vector.quantize_mx(
-                out=codes[:].bitcast(FP8X4), scales=plane[:], in_=wo_bf_both[:].rearrange("p b n t -> p (b n t)")
-            )
-            for b in range(NB):
-                wo_codes[b], wo_plane[b] = codes[:, b * N : (b + 1) * N], plane[:, b * N : (b + 1) * N]
-
-        def gather_words(window, offsets, name, widths, start=0):
-            pieces = []
+        def gather_words(window, offsets, name, widths):
+            pieces, start = [], 0
             for width in widths:
                 picked = held([P, width], U32, "%s_%d" % (name, start))
                 nc.vector.tensor_copy(picked[:], window[:].indirect(offsets[:, start // 16 : (start + width) // 16]))
@@ -196,250 +156,299 @@ def tile_list_kinase_selectivity_kernel(
                 start = start + width
             return pieces
 
+        nc.sync.dma_start(list2[:], offs2)
+        nc.sync.dma_start(out=tab2_s[:].bitcast(I32)[112:P, :], in_=tab2_scales[0].bitcast(I32))
+        load_wg(0)
+        nc.sync.dma_start(lists[:], offs)
+        nc.sync.dma_start(
+            out=tab_s[:].bitcast(I32)[0:P:4, :], in_=tab_scales.bitcast(I32).rearrange("a q c -> q a c")
+        )
+        nc.sync.dma_start(
+            out=ws_raw[:].bitcast(I32)[4:P:8, 0:2, :], in_=w4_scales.bitcast(I32).rearrange("a q c -> q a c")
+        )
+        nc.sync.dma_start(out=ws_raw[:].bitcast(I32)[4:P:8, 2, :], in_=w8_scales[0].bitcast(I32))
+        tab2_w = load_table("tab2_w", tab2_words[0], T2)
+
         v2_picked = held([P, S], U8, "v2_picked")
         nc.vector.tensor_copy(v2_picked[:], tab2_s[:].indirect(list2[:]))
-        planes32 = planes[:].bitcast(I32)
-        half = 3 * 512 // 4
-        staged = held([P, S // 4 + half], I32, "staged")
-        nc.vector.tensor_copy(
-            staged[96:P, S // 4 :].rearrange("p (x t u) -> p t x u", x=3, t=4),
-            ws_raw[:].bitcast(I32)[96:P].rearrange("p x (u t) -> p t x u", t=4),
-        )
-        nc.vector.tensor_copy(staged[96:P, 0 : S // 4], v2_picked[:].bitcast(I32)[96:P, :])
         for r in range(4):
-            nc.sync.dma_start(out=planes32[r:P:32, 0 : S // 4 + half], in_=staged[96 + 2 * r : P : 8, :])
-        tab_w[0] = load_table("tab_w0", tab_words[0], T)
-        order_w4(0)
-        cast_wg(0, slice(0, 4))
+            nc.sync.dma_start(
+                out=v2_plane[:].bitcast(I32)[V2_ROW + r : P : 32, :], in_=v2_picked[:].bitcast(I32)[112 + r : P : 4, :]
+            )
+        tab_w = [load_table("tab_w0", tab_words[0], T)]
+        cast_wg_first()
+        nc.scalar.copy(
+            stage[:].bitcast(U32)[:, S // 4 :].rearrange("p (b x t u) -> p b x u t", b=2, x=3, t=4),
+            ws_raw[:].bitcast(U32).rearrange("p x (b u t) -> p b x u t", b=2, t=4),
+        )
         v_picked = held([P, S], U8, "v_picked")
         nc.vector.tensor_copy(v_picked[:], tab_s[:].indirect(lists[:]))
-        picked32 = v_picked[:].bitcast(I32)
-        nc.vector.tensor_copy(v_planes[0][:].bitcast(I32), picked32)
-        for a, r, source in ((1, 0, 4), (1, 1, 12), (1, 2, 20), (1, 3, 28), (0, 2, 16), (0, 3, 17)):
-            nc.sync.dma_start(out=v_planes[a][:].bitcast(I32)[r:P:32, :], in_=picked32[source:P:32, :])
-        tab_w[1] = load_table("tab_w1", tab_words[1], T)
-        load_w8(0, held([P, 512], I32, "w8_raw0")[:])
-        v2_plane, v_plane = planes[:, 0:S], [v_planes[0][:], v_planes[1][:]]
+        picked32, stage32, planes32 = v_picked[:].bitcast(I32), stage[:].bitcast(I32), planes[:].bitcast(I32)
+        nc.vector.tensor_copy(stage32[:, 0 : S // 4], picked32)
+        quantise_wg(0)
+
+        def move_first_pass_row(r):
+            nc.sync.dma_start(out=stage32[r:P:32, 0 : S // 4], in_=picked32[8 * r : P : 32, :])
+
+        def move_rows(cols):
+            for r in range(4):
+                nc.sync.dma_start(out=planes32[r:P:32, cols], in_=stage32[4 + 8 * r : P : 32, cols])
+
+        early = (S + 3 * 512) // 4
+        for r in range(1, 4):
+            move_first_pass_row(r)
+        tab_w.append(load_table("tab_w1", tab_words[1], T))
+        v2_words = gather_words(tab2_w, list2, "v2_words", (256, 768))
+        v_plane = [stage[:, 0:S], planes[:, 0:S]]
 
         def weight_plane(x, b, t):
             start = S + (3 * b + x) * 512 + t * P
             return planes[:, start : start + P]
 
-        quantise_wg(0)
-        v2_words = gather_words(tab2_w, list2, "v2_words", (512, 512))
-        load_wg(1)
-        load_wo(0)
-        gain_raw = held([P, NB, 16], F32, "gain_raw")
-        gain_runs = gain.rearrange("(b u x) -> u b x", b=NB, x=16)
-        for e in range(4):
-            nc.sync.dma_start(out=gain_raw[e:P:4, :, 0:13], in_=gain_runs[:, :, e : e + 13])
-        load_wo(1)
-        load_w4(1, held([P, 512], I32, "w4_raw1")[:])
-        load_w8(1, held([P, 512], I32, "w8_raw1")[:])
-        for r in range(4):
-            nc.sync.dma_start(out=planes32[r:P:32, S // 4 + half :], in_=staged[97 + 2 * r : P : 8, S // 4 :])
+        def moving(pieces, j0, width):
+            first, size, picked = [piece for piece in pieces if piece[0] <= j0 < piece[0] + piece[1]][0]
+            return picked[:, j0 - first : j0 - first + width].bitcast(FP8X4)
 
-        tanh_half, pocket, shift, gated, silu, h_bf = {}, {}, {}, {}, {}, {}
-        h_codes = held([P, NCHUNK * JC], U32, "h_codes")
-        h_plane, run_left = {}, {}
+        tanh_half, pocket, shift, gated, mixed, silu = {}, {}, {}, {}, {}, {}
 
-        def moving(pieces, plane, jq):
-            start = jq * JC
-            first, width, picked = [piece for piece in pieces if piece[0] <= start < piece[0] + piece[1]][0]
-            words = picked[:, start - first : start - first + JC]
-            return words.bitcast(FP8X4), plane[:, start : start + JC]
-
-        def gate_stage(c):
-            b, jq = divmod(c, NJ)
-            rhs, rhs_scale = moving(v2_words, v2_plane, jq)
-            bank = psum.tile([P, 4, JC], F32, name="gate", tag="bank")
-            for t in range(4):
+        def gate_stage(c, number):
+            span, slots = UNITS[c]
+            b, j0, width = SPANS[span]
+            acc = bank(number, [P, len(slots), width])
+            for i, t in enumerate(slots):
                 cols = slice(t * P, (t + 1) * P)
                 nc.tensor.matmul_mx(
-                    bank[:, t, :], lhsT=wg_codes[b][:, cols].bitcast(FP8X4), lhsT_scale=wg_plane[b][:, cols],
-                    rhs=rhs, rhs_scale=rhs_scale, start=True, stop=True,
+                    acc[:, i, :], lhsT=wg_codes[b][:, cols].bitcast(FP8X4), lhsT_scale=wg_plane[b][:, cols],
+                    rhs=moving(v2_words, j0, width), rhs_scale=v2_plane[V2_ROW:P, j0 : j0 + width],
+                    start=True, stop=True,
                 )
-            slot = c if c < NJ else NJ - 4 + (c - NJ) % 4
-            tanh_half[c] = held([P, JC, 4], F32, "tanh_half%d" % c, "tanh_half%d" % slot)
-            nc.scalar.activation(tanh_half[c][:], bank[:].rearrange("p t j -> p j t"), ACT.Tanh, scale=0.5)
-
-        def pocket_pass(c, t, a, start, stop):
-            b, jq = divmod(c, NJ)
-            rhs, rhs_scale = moving(v_words[a], v_plane[a], jq)
-            nc.tensor.matmul_mx(
-                pocket[c][:, t, :], lhsT=w4_codes[b][:, a, t, :].bitcast(FP4X4),
-                lhsT_scale=weight_plane(W4A + a, b, t), rhs=rhs, rhs_scale=rhs_scale, start=start, stop=stop,
-            )
+            over = "tanh_half%d" % (c - 8) if c >= 8 else {5: "w8_raw0", 6: "w4_raw0"}.get(c)
+            tanh_half[c] = held([P, width, len(slots)], F32, "tanh_half%d" % c, over)
+            nc.scalar.activation(tanh_half[c][:], acc[:].rearrange("p t j -> p j t"), ACT.Tanh, scale=0.5)
 
         def pocket_stage(c):
-            pocket[c] = psum.tile([P, 4, JC], F32, name="pocket", tag="bank")
-            for t in range(4):
+            span, slots = UNITS[c]
+            b, j0, width = SPANS[span]
+            pocket[c] = bank(POCKET_BANKS[c % 3], [P, len(slots), width])
+            for i, t in enumerate(slots):
                 for a in range(2):
-                    pocket_pass(c, t, a, a == 0, a == 1)
-
-        def early_pocket(c, a):
-            if a == 0:
-                pocket[c] = psum.tile([P, 4, JC], F32, name="pocket", tag="bank")
-            for t in range(4):
-                pocket_pass(c, t, a, a == 0 and t == 0, a == 1 and t == 3)
+                    nc.tensor.matmul_mx(
+                        pocket[c][:, i, :], lhsT=w4_codes[b][:, a, t, :].bitcast(FP4X4),
+                        lhsT_scale=weight_plane(W4A + a, b, t), rhs=moving(v_words[a], j0, width),
+                        rhs_scale=v_plane[a][:, j0 : j0 + width], start=a == 0, stop=a == 1,
+                    )
 
         def shift_stage(c):
-            b, jq = divmod(c, NJ)
-            shift[c] = psum.tile([P, 4, JC], F32, name="shift", tag="bank")
-            rhs, rhs_scale = moving(v2_words, v2_plane, jq)
-            for t in range(4):
+            span, slots = UNITS[c]
+            b, j0, width = SPANS[span]
+            shift[c] = bank(SHIFT_BANKS[c % 2], [P, len(slots), width])
+            for i, t in enumerate(slots):
                 nc.tensor.matmul_mx(
-                    shift[c][:, t, :], lhsT=w8_codes[b][:, t, :].bitcast(FP8X4),
-                    lhsT_scale=weight_plane(W8, b, t),
-                    rhs=rhs, rhs_scale=rhs_scale, start=True, stop=True,
+                    shift[c][:, i, :], lhsT=w8_codes[b][:, t, :].bitcast(FP8X4), lhsT_scale=weight_plane(W8, b, t),
+                    rhs=moving(v2_words, j0, width), rhs_scale=v2_plane[V2_ROW:P, j0 : j0 + width],
+                    start=True, stop=True,
                 )
 
-        def work_tile(kind, c):
-            if "%s%d" % (kind, c) in PLACE:
-                return held([P, JC, 4], F32, "%s%d" % (kind, c))
-            return ring.tile([P, JC, 4], F32, name=kind, tag=kind)
-
         def gate_pocket(c):
-            gated[c] = work_tile("gated", c)
+            span, slots = UNITS[c]
+            width = SPANS[span][2]
+            if c == FIRST_VISIT + 2:
+                over, plus = "wg_bf1", 0
+            elif c == SECOND_VISIT + 2:
+                over, plus = "h_bf2", 0
+            else:
+                over, plus = (("tab2_w", "tab2_w", "tab_w0", "wg_raw0")[c // 4], 2 * KIB * (c % 8 if c < 8 else c % 4))
+            gated[c] = held([P, width, len(slots)], F32, "gated%d" % c, over, plus)
             nc.vector.scalar_tensor_tensor(
                 gated[c][:], tanh_half[c][:], 1.0, pocket[c][:].rearrange("p t j -> p j t"), ADD, MULT
             )
 
-        runs = sorted(GPSIMD_RUNS + VECTOR_RUNS)
-        run_of = {c: run for run in runs for c in range(*run)}
-        mixed = {}
+        MIXED_OVER = {1: ("mixed0", 2 * KIB), 5: ("mixed0", 0), 6: ("mixed2", 0), 7: ("mixed3", 0), 8: ("mixed4", 0), 9: ("mixed4", 2 * KIB)}
+        SILU_OVER = {
+            1: ("silu0", 2 * KIB), 5: ("silu0", 0), 6: ("wg_raw1", 4 * KIB), 7: ("silu3", 0), 8: ("silu4", 0),
+            9: ("silu4", 2 * KIB),
+        }
 
         def add_shift(c):
-            first, last = run_of[c]
-            if c == first:
-                mixed[first] = held([P, (last - first) * JC, 4], F32, "mixed%d" % first)
+            span, slots = UNITS[c]
+            width = SPANS[span][2]
+            parts = 4 // len(slots)
+            if slots[0] == 0:
+                over, plus = MIXED_OVER.get(span, (None, 0))
+                mixed[span] = held([P, parts, width, len(slots)], F32, "mixed%d" % span, over, plus, 4 * KIB)
             nc.vector.scalar_tensor_tensor(
-                mixed[first][:, (c - first) * JC : (c - first + 1) * JC, :], gated[c][:], 0.5,
+                mixed[span][:, slots[0] // len(slots)], gated[c][:], 0.5,
                 shift[c][:].rearrange("p t j -> p j t"), MULT, ADD,
             )
-            if c == last - 1:
-                silu[first] = held([P, (last - first) * JC, 4], F32, "silu%d" % first)
-                nc.scalar.activation(silu[first][:], mixed[first][:], ACT.Silu)
+            if slots[-1] == 3:
+                over, plus = SILU_OVER.get(span, (None, 0))
+                silu[span] = held([P, width, 4], F32, "silu%d" % span, over, plus, 4 * KIB)
+                nc.scalar.activation(
+                    silu[span][:].rearrange("p j (u e) -> p j u e", u=parts),
+                    mixed[span][:].rearrange("p u j e -> p j u e"), ACT.Silu,
+                )
 
-        def apply_gain(engine, source, first, last):
-            base, end = [span for span in H_TILES if span[0] <= first < span[1]][0]
-            if base not in h_bf:
-                h_bf[base] = held([P, (end - base) * JC, 4], BF16, "h_bf%d" % base)
-            b = first // NJ
-            target = h_bf[base][:, (first - base) * JC : (last - base) * JC, :]
-            columns = slice(4 * b, 4 * b + 4) if source is gains else slice(0, 4)
-            factor = source[:, columns].unsqueeze(1).to_broadcast([P, (last - first) * JC, 4])
-            if source is gains:
-                engine.tensor_tensor(target, silu[first][:], factor, MULT)
-            else:
-                engine.scalar_tensor_tensor(target, silu[first][:], 1.0, factor, MULT, MULT)
+        H_TILES = {0: (0, 1), 2: (2, 3), 4: (4, 5), 6: (6,), 7: (7,), 8: (8,), 9: (9,)}
+        H_OVER = {0: ("wg_raw1", 0), 2: ("wg_bf1", 2 * KIB), 6: ("h_bf2", 2 * KIB)}
+        h_bf, h_at, h_plane = {}, {}, {}
+        h_codes = held([P, 2 * S], U32, "h_codes")
 
-        def quantise_h(base, c, count):
-            cols = slice(c * JC, (c + count) * JC)
-            plane = held([P, count * JC], U8, "h_plane%d" % c)
-            for k in range(count):
-                h_plane[c + k] = plane[:, k * JC :]
-                run_left[c + k] = count - k
+        def h_target(span):
+            first = [key for key in H_TILES if span in H_TILES[key]][0]
+            if span == first:
+                over, plus = H_OVER.get(first, (None, 0))
+                total = sum(SPANS[member][2] for member in H_TILES[first])
+                h_bf[first] = held([P, total, 4], BF16, "h_bf%d" % first, over, plus)
+            start = 0 if span == first else SPANS[first][2]
+            return h_bf[first][:, start : start + SPANS[span][2], :]
+
+        def gain_on_gpsimd(span):
+            b, j0, width = SPANS[span]
+            factor = gains[:, 4 * b : 4 * b + 4].unsqueeze(1).to_broadcast([P, width, 4])
+            nc.gpsimd.tensor_tensor(h_target(span), silu[span][:], factor, MULT)
+
+        def gain_on_vector(span):
+            width = SPANS[span][2]
+            factor = gain_bank[:, 0:4].unsqueeze(1).to_broadcast([P, width, 4])
+            nc.vector.scalar_tensor_tensor(h_target(span), silu[span][:], 1.0, factor, MULT, MULT)
+
+        def quantise_h(first, over=None):
+            b, j0, width = SPANS[first]
+            total = sum(SPANS[member][2] for member in H_TILES[first])
+            start = b * S + j0
+            plane = held([P, total], U8, "h_plane%d" % first, over)
+            for k in range(0, total, P):
+                h_plane[start + k] = plane[:, k:]
             nc.vector.quantize_mx(
-                out=h_codes[:, cols].bitcast(FP8X4), scales=plane[:],
-                in_=h_bf[base][:, (c - base) * JC : (c - base + count) * JC, :].rearrange("p j t -> p (j t)"),
+                out=h_codes[:, start : start + total].bitcast(FP8X4), scales=plane[:],
+                in_=h_bf[first][:].rearrange("p j t -> p (j t)"),
             )
 
-        def last_product(jq, count):
-            width = count * JC
-            apart = jq == NJ - 1
-            if apart:
-                banks = [psum.tile([P, width], F32, name="out_bank", tag="bank")[:] for nt in range(2)]
-            else:
-                bank = psum.tile([P, 2, width], F32, name="out_bank", tag="bank")
-                banks = [bank[:, 0, :], bank[:, 1, :]]
-            for b in range(NB):
-                c = b * NJ + jq
-                for nt in range(2):
-                    cols = slice(nt * P, (nt + 1) * P)
-                    nc.tensor.matmul_mx(
-                        banks[nt], lhsT=wo_codes[b][:, cols].bitcast(FP8X4), lhsT_scale=wo_plane[b][:, cols],
-                        rhs=h_codes[:, c * JC : c * JC + width].bitcast(FP8X4), rhs_scale=h_plane[c][:, 0:width],
-                        start=(b == 0 and (apart or nt == 0)), stop=(b == NB - 1 and (apart or nt == 1)),
-                    )
-            result = held([P, 2, width], F32, "result%d" % jq)
-            if apart:
-                nc.vector.tensor_copy(result[:, 0, :], banks[0])
-                nc.scalar.copy(result[:, 1, :], banks[1])
-            else:
-                nc.scalar.copy(result[:], bank[:])
-            nc.sync.dma_start(
-                out=out.rearrange("(nt p) j -> p nt j", p=P)[:, :, jq * JC : jq * JC + width], in_=result[:]
+        wo_bf = held([P, 2, N, 4], BF16, "wo_bf")
+
+        def cast_wo(b, groups):
+            nc.scalar.copy(
+                wo_bf[:, b].rearrange("p (c i) t -> p c t i", i=4)[:, groups],
+                wo_raw[b][:].rearrange("p t (c i) -> p c t i", i=4)[:, groups],
             )
 
-        for c in range(NJ):
-            gate_stage(c)
+        wo_parts = {}
+
+        def quantise_wo(over):
+            wo_parts["codes"] = held([P, 2 * N], U32, "wo_codes", over)
+            wo_parts["plane"] = held([P, 2 * N], U8, "wo_plane")
+            nc.vector.quantize_mx(
+                out=wo_parts["codes"][:].bitcast(FP8X4), scales=wo_parts["plane"][:],
+                in_=wo_bf[:].rearrange("p b n t -> p (b n t)"),
+            )
+
+        sums = {}
+
+        def product_half(j0, width, b, numbers=None):
+            if b == 0:
+                sums[j0] = [bank(number, [P, 2 // len(numbers), width]) for number in numbers]
+            apart = len(sums[j0]) == 2
+            start = b * S + j0
+            for nt in range(2):
+                cols = slice(b * N + nt * P, b * N + (nt + 1) * P)
+                nc.tensor.matmul_mx(
+                    sums[j0][nt][:, 0, :] if apart else sums[j0][0][:, nt, :],
+                    lhsT=wo_parts["codes"][:, cols].bitcast(FP8X4), lhsT_scale=wo_parts["plane"][:, cols],
+                    rhs=h_codes[:, start : start + width].bitcast(FP8X4), rhs_scale=h_plane[start][:, 0:width],
+                    start=(b == 0 and (apart or nt == 0)), stop=(b == 1 and (apart or nt == 1)),
+                )
+            if b == 1:
+                result = held([P, 2, width], F32, "result%d" % j0)
+                if apart:
+                    nc.vector.tensor_copy(result[:, 0, :], sums[j0][0][:, 0, :])
+                    nc.scalar.copy(result[:, 1, :], sums[j0][1][:, 0, :])
+                else:
+                    nc.scalar.copy(result[:], sums[j0][0][:])
+                nc.sync.dma_start(out=out.rearrange("(nt p) j -> p nt j", p=P)[:, :, j0 : j0 + width], in_=result[:])
+
+        for c in range(5):
+            gate_stage(c, EARLY_GATE_BANKS[c % 3])
         v_words = [gather_words(tab_w[0], lists, "v_words0", (1024,))]
-        for c in range(2):
-            early_pocket(c, 0)
-        v_words.append(gather_words(tab_w[1], lists, "v_words1", (256,)))
-        order_w8(0)
-        gain_rows = held([P, P], F32, "gain_rows")
-        identity = held([P, P], F32, "identity")
+        load_w4(0)
+        move_rows(slice(0, early))
+        load_w8(0)
+        gain_raw = held([P, 2, 16], F32, "gain_raw")
+        gain_runs = gain.rearrange("(b u x) -> u b x", b=2, x=16)
+        for e in range(4):
+            nc.sync.dma_start(out=gain_raw[e:P:4, :, 0:13], in_=gain_runs[:, :, e : e + 13])
+        order_w4(0, nc.scalar.copy, U32)
+        gate_stage(6, EARLY_GATE_BANKS[0])
+        order_w8(0, nc.scalar.copy, U32)
+        gate_stage(5, EARLY_GATE_BANKS[2])
+        gate_stage(7, EARLY_GATE_BANKS[2])
+        v_words.append(gather_words(tab_w[1], lists, "v_words1", (256, 768)))
+        load_wg(1)
+        load_w4(1)
+        load_w8(1)
+        move_rows(slice(early, (S + 3 * H) // 4))
+        load_wo(0)
+        load_wo(1)
+        gains = held([P, 8], F32, "gains", "tab_w1")
+        gain_rows = held([P, P], F32, "gain_rows", "tab_w1", KIB // 2)
+        identity = held([P, P], F32, "identity", "tab_w1", KIB)
+        nc.gpsimd.tensor_copy(gains[:].rearrange("p (b t) -> p b t", t=4), gain_raw[:, :, 0:13:4])
         nc.gpsimd.memset(gain_rows[:], 0.0)
         make_identity(nc, identity[:])
         nc.sync.dma_start(
             out=gain_rows[0:4, :].rearrange("t (u e) -> t u e", e=4),
             in_=gain[512:H].rearrange("(u t e) -> t u e", t=4, e=4),
         )
-        v_words[1].extend(gather_words(tab_w[1], lists, "v_words1", (256,), 256))
+        gain_bank = bank(7, [P, P])
+        cast_wg_second()
 
-
-        for c in range(2):
-            early_pocket(c, 1)
+        pocket_stage(0)
+        pocket_stage(1)
         shift_stage(0)
-        gains = held([P, NB * 4], F32, "gains")
-        nc.gpsimd.tensor_copy(gains[:].rearrange("p (b t) -> p b t", t=4), gain_raw[:, :, 0:13:4])
-        gain_bank = psum.tile([P, P], F32, name="gain_bank", tag="gain_bank", bufs=1)
         gate_pocket(0)
-        for c in range(NCHUNK):
-            if c + 2 < NCHUNK:
+        for c in range(NUNIT):
+            if c + 2 < NUNIT:
                 pocket_stage(c + 2)
-            if c + 1 < NCHUNK:
+            if c + 1 < NUNIT:
                 shift_stage(c + 1)
-            if LATE_GATES_FROM <= c < LATE_GATES_FROM + NJ:
-                gate_stage(NJ + c - LATE_GATES_FROM)
-            if c == LATE_GATES_FROM + NJ:
+            if FIRST_VISIT < c <= FIRST_VISIT + 8:
+                gate_stage(c + 7 - FIRST_VISIT, LATE_GATE_BANKS[c % 2])
+            if c == FIRST_VISIT + 9:
                 nc.tensor.transpose(gain_bank[:], gain_rows[:], identity[:])
-            if c + 1 < NCHUNK:
+            if c + 1 < NUNIT:
                 gate_pocket(c + 1)
-            if c == SECOND_VISIT:
-                quantise_wo()
-                quantise_h(2, 2, 2)
-                quantise_h(0, 0, 2)
-                apply_gain(nc.gpsimd, gains, 6, 8)
-            if c == THIRD_VISIT:
-                quantise_h(2, 4, 2)
-                quantise_h(6, 6, 4)
-                last_product(0, 2)
-                apply_gain(nc.gpsimd, gains, 10, 12)
             add_shift(c)
-            if c == FIRST_VISIT:
-                order_w4(1)
-                order_w8(1)
-                quantise_wg(1)
-            for first, last in GPSIMD_RUNS:
-                if last - 1 == c and first not in (6, 10):
-                    apply_gain(nc.gpsimd, gains, first, last)
+            span, slots = UNITS[c]
             if c == 1:
-                v_words[1].extend(gather_words(tab_w[1], lists, "v_words1", (512,), 512))
-            if c < 2:
-                cast_wg(1, slice(2 * c, 2 * c + 1))
-                cast_wg(1, slice(2 * c + 1, 2 * c + 2))
-            if c in (2, 3):
-                cast_wo(c - 2, slice(0, 64))
-        for c in (12, 13, 14):
-            apply_gain(nc.vector, gain_bank, c, c + 1)
-        quantise_h(10, 10, 2)
-        last_product(2, 2)
-        quantise_h(12, 12, 2)
-        last_product(4, 2)
-        apply_gain(nc.vector, gain_bank, 15, 16)
-        for c in (14, 15):
-            quantise_h(12, c, 1)
-            last_product(c - NJ, 1)
+                order_w4(1, nc.scalar.copy, U32)
+                order_w8(1, nc.scalar.copy, U32)
+            if c == FIRST_VISIT:
+                quantise_h(0, "gated%d" % c)
+                quantise_wg(1, "h_bf0")
+            if c == SECOND_VISIT:
+                quantise_h(4, "gated%d" % c)
+                quantise_wo("h_bf4")
+                product_half(0, 256, 0, (0,))
+                product_half(0, 256, 1)
+                quantise_h(2, "wo_bf")
+                gain_on_gpsimd(6)
+                product_half(256, 256, 0, (1,))
+            if c == NUNIT - 2:
+                product_half(512, 256, 0, (POCKET_BANKS[(NUNIT - 1) % 3],))
+                product_half(768, 128, 0, (SHIFT_BANKS[c % 2],))
+            if c == NUNIT - 1:
+                product_half(896, 128, 0, (SHIFT_BANKS[c % 2], POCKET_BANKS[(c - 1) % 3]))
+            if slots[-1] == 3 and span < 6:
+                gain_on_gpsimd(span)
+            if 6 <= c < 10:
+                cast_wo((c - 6) // 2, slice(32 * (c % 2), 32 * (c % 2) + 32))
+        gain_on_vector(7)
+        quantise_h(6)
+        product_half(256, 256, 1)
+        quantise_h(7, "h_bf6")
+        product_half(512, 256, 1)
+        gain_on_vector(8)
+        gain_on_vector(9)
+        quantise_h(8, "h_bf7")
+        product_half(768, 128, 1)
+        quantise_h(9, "h_bf8")
+        product_half(896, 128, 1)

@@ -33,7 +33,7 @@ UNITS = [
     for slots in (((0, 1, 2, 3),) if width == 128 else ((0, 1), (2, 3)))
 ]
 NUNIT = len(UNITS)
-FIRST_VISIT, SECOND_VISIT = 4, 13
+FIRST_VISIT, SECOND_VISIT = 2, 13
 EARLY_GATE_BANKS, LATE_GATE_BANKS, POCKET_BANKS, SHIFT_BANKS = (0, 1, 7), (0, 1), (2, 3, 4), (5, 6)
 
 
@@ -222,7 +222,7 @@ def tile_list_kinase_selectivity_kernel(
                     rhs=moving(v2_words, j0, width), rhs_scale=v2_plane[V2_ROW:P, j0 : j0 + width],
                     start=True, stop=True,
                 )
-            over = "tanh_half%d" % (c - 8) if c >= 8 else {5: "w8_raw0", 6: "w4_raw0"}.get(c)
+            over = "tanh_half%d" % (c - 4) if c >= 8 else {5: "w8_raw0", 6: "w4_raw0"}.get(c)
             tanh_half[c] = held([P, width, len(slots)], F32, "tanh_half%d" % c, over)
             nc.scalar.activation(tanh_half[c][:], acc[:].rearrange("p t j -> p j t"), ACT.Tanh, scale=0.5)
 
@@ -289,7 +289,7 @@ def tile_list_kinase_selectivity_kernel(
                 )
 
         H_TILES = {0: (0, 1), 2: (2, 3), 4: (4, 5), 6: (6,), 7: (7,), 8: (8,), 9: (9,)}
-        H_OVER = {0: ("wg_raw1", 0), 2: ("wg_bf1", 2 * KIB), 6: ("h_bf2", 2 * KIB)}
+        H_OVER = {0: ("wg_bf1", 2 * KIB), 6: ("h_bf2", 2 * KIB)}
         h_bf, h_at, h_plane = {}, {}, {}
         h_codes = held([P, 2 * S], U32, "h_codes")
 
@@ -372,10 +372,6 @@ def tile_list_kinase_selectivity_kernel(
         load_w4(0)
         move_rows(slice(0, early))
         load_w8(0)
-        gain_raw = held([P, 2, 16], F32, "gain_raw")
-        gain_runs = gain.rearrange("(b u x) -> u b x", b=2, x=16)
-        for e in range(4):
-            nc.sync.dma_start(out=gain_raw[e:P:4, :, 0:13], in_=gain_runs[:, :, e : e + 13])
         order_w4(0, nc.scalar.copy, U32)
         gate_stage(6, EARLY_GATE_BANKS[0])
         order_w8(0, nc.scalar.copy, U32)
@@ -383,6 +379,10 @@ def tile_list_kinase_selectivity_kernel(
         gate_stage(7, EARLY_GATE_BANKS[2])
         v_words.append(gather_words(tab_w[1], lists, "v_words1", (256, 768)))
         load_wg(1)
+        gain_raw = held([P, 2, 16], F32, "gain_raw")
+        gain_runs = gain.rearrange("(b u x) -> u b x", b=2, x=16)
+        for e in range(4):
+            nc.sync.dma_start(out=gain_raw[e:P:4, :, 0:13], in_=gain_runs[:, :, e : e + 13])
         load_w4(1)
         load_w8(1)
         move_rows(slice(early, (S + 3 * H) // 4))
@@ -391,7 +391,6 @@ def tile_list_kinase_selectivity_kernel(
         gains = held([P, 8], F32, "gains", "tab_w1")
         gain_rows = held([P, P], F32, "gain_rows", "tab_w1", KIB // 2)
         identity = held([P, P], F32, "identity", "tab_w1", KIB)
-        nc.gpsimd.tensor_copy(gains[:].rearrange("p (b t) -> p b t", t=4), gain_raw[:, :, 0:13:4])
         nc.gpsimd.memset(gain_rows[:], 0.0)
         make_identity(nc, identity[:])
         nc.sync.dma_start(
@@ -400,6 +399,7 @@ def tile_list_kinase_selectivity_kernel(
         )
         gain_bank = bank(7, [P, P])
         cast_wg_second()
+        nc.gpsimd.tensor_copy(gains[:].rearrange("p (b t) -> p b t", t=4), gain_raw[:, :, 0:13:4])
 
         pocket_stage(0)
         pocket_stage(1)
@@ -422,14 +422,16 @@ def tile_list_kinase_selectivity_kernel(
                 order_w4(1, nc.scalar.copy, U32)
                 order_w8(1, nc.scalar.copy, U32)
             if c == FIRST_VISIT:
-                quantise_h(0, "gated%d" % c)
-                quantise_wg(1, "h_bf0")
+                quantise_wg(1, "gated%d" % c)
+                gain_on_gpsimd(0)
+                gain_on_gpsimd(1)
             if c == SECOND_VISIT:
                 quantise_h(4, "gated%d" % c)
                 quantise_wo("h_bf4")
+                quantise_h(0, "wo_bf")
                 product_half(0, 256, 0, (0,))
                 product_half(0, 256, 1)
-                quantise_h(2, "wo_bf")
+                quantise_h(2, "h_bf0")
                 gain_on_gpsimd(6)
                 product_half(256, 256, 0, (1,))
             if c == NUNIT - 2:
@@ -437,7 +439,7 @@ def tile_list_kinase_selectivity_kernel(
                 product_half(768, 128, 0, (SHIFT_BANKS[c % 2],))
             if c == NUNIT - 1:
                 product_half(896, 128, 0, (SHIFT_BANKS[c % 2], POCKET_BANKS[(c - 1) % 3]))
-            if slots[-1] == 3 and span < 6:
+            if slots[-1] == 3 and 2 <= span < 6:
                 gain_on_gpsimd(span)
             if 6 <= c < 10:
                 cast_wo((c - 6) // 2, slice(32 * (c % 2), 32 * (c % 2) + 32))

@@ -70,11 +70,11 @@ def tile_list_kinase_selectivity_kernel(
         v2_plane = held([P, S], U8, "v2_plane")
         planes = held([P, S + 3 * H], U8, "planes")
         stage = held([P, S + 3 * H], U8, "stage")
+        nc.vector.memset(tab_s[:].bitcast(I32), 0)
+        nc.vector.memset(ws_raw[:].bitcast(I32), 0)
         nc.vector.memset(tab2_s[:].bitcast(I32)[0:112, :], 0)
-        nc.gpsimd.memset(tab_s[:].bitcast(I32), 0)
-        nc.gpsimd.memset(ws_raw[:].bitcast(I32), 0)
-        nc.gpsimd.memset(v2_plane[:].bitcast(I32), 0)
-        nc.gpsimd.memset(planes[:].bitcast(I32), 0)
+        nc.vector.memset(v2_plane[:].bitcast(I32), 0)
+        nc.vector.memset(planes[:].bitcast(I32), 0)
 
         wg_raw, wg_bf, wg_codes, wg_plane, w4_codes, w8_codes, wo_raw = {}, {}, {}, {}, {}, {}, {}
 

@@ -114,7 +114,7 @@ def tile_list_kinase_selectivity_kernel(
         w4_raw, w8_raw = {}, {}
 
         def load_w4(b):
-            w4_raw[b] = held([P, 2, 256], U32, "w4_raw%d" % b)
+            w4_raw[b] = held([P, 2, 256], U32, "w4_raw%d" % b, room=4 * KIB if b else 0)
             nc.sync.dma_start(
                 out=w4_raw[b][:].bitcast(I32),
                 in_=w4_words.bitcast(I32).rearrange("a p c -> p a c")[:, :, 256 * b : 256 * (b + 1)],
@@ -222,7 +222,7 @@ def tile_list_kinase_selectivity_kernel(
                     rhs=moving(v2_words, j0, width), rhs_scale=v2_plane[V2_ROW:P, j0 : j0 + width],
                     start=True, stop=True,
                 )
-            over = "tanh_half%d" % (c - 4) if c >= 8 else {5: "w8_raw0", 6: "w4_raw0"}.get(c)
+            over = "tanh_half%d" % (c - 4) if c > 8 else {5: "w8_raw0", 6: "w4_raw0", 8: "w8_raw1"}.get(c)
             tanh_half[c] = held([P, width, len(slots)], F32, "tanh_half%d" % c, over)
             nc.scalar.activation(tanh_half[c][:], acc[:].rearrange("p t j -> p j t"), ACT.Tanh, scale=0.5)
 
@@ -254,6 +254,8 @@ def tile_list_kinase_selectivity_kernel(
             width = SPANS[span][2]
             if c == FIRST_VISIT + 2:
                 over, plus = "wg_bf1", 0
+            elif c == SECOND_VISIT:
+                over, plus = "silu0", 4 * KIB
             elif c == SECOND_VISIT + 2:
                 over, plus = "h_bf2", 0
             else:
@@ -265,7 +267,7 @@ def tile_list_kinase_selectivity_kernel(
 
         MIXED_OVER = {1: ("mixed0", 2 * KIB), 5: ("mixed0", 0), 6: ("mixed2", 0), 7: ("mixed3", 0), 8: ("mixed4", 0), 9: ("mixed4", 2 * KIB)}
         SILU_OVER = {
-            1: ("silu0", 2 * KIB), 5: ("silu0", 0), 6: ("wg_raw1", 4 * KIB), 7: ("silu3", 0), 8: ("silu4", 0),
+            1: ("silu0", 2 * KIB), 2: ("w4_raw1", 0), 5: ("silu0", 0), 6: ("wg_raw1", 4 * KIB), 7: ("silu3", 0), 8: ("silu4", 0),
             9: ("silu4", 2 * KIB),
         }
 
@@ -282,7 +284,7 @@ def tile_list_kinase_selectivity_kernel(
             )
             if slots[-1] == 3:
                 over, plus = SILU_OVER.get(span, (None, 0))
-                silu[span] = held([P, width, 4], F32, "silu%d" % span, over, plus, 4 * KIB)
+                silu[span] = held([P, width, 4], F32, "silu%d" % span, over, plus, 6 * KIB if span == 0 else 4 * KIB)
                 nc.scalar.activation(
                     silu[span][:].rearrange("p j (u e) -> p j u e", u=parts),
                     mixed[span][:].rearrange("p u j e -> p j u e"), ACT.Silu,
@@ -302,44 +304,46 @@ def tile_list_kinase_selectivity_kernel(
             start = 0 if span == first else SPANS[first][2]
             return h_bf[first][:, start : start + SPANS[span][2], :]
 
-        def gain_on_gpsimd(span):
-            b, j0, width = SPANS[span]
-            factor = gains[:, 4 * b : 4 * b + 4].unsqueeze(1).to_broadcast([P, width, 4])
-            nc.gpsimd.tensor_tensor(h_target(span), silu[span][:], factor, MULT)
+        def gain_on_gpsimd(span, cols=slice(None)):
+            b = SPANS[span][0]
+            source = silu[span][:, cols]
+            factor = gains[:, 4 * b : 4 * b + 4].unsqueeze(1).to_broadcast(source.shape)
+            nc.gpsimd.tensor_tensor(h_target(span)[:, cols], source, factor, MULT)
 
-        def gain_on_vector(span):
-            width = SPANS[span][2]
-            factor = gain_bank[:, 0:4].unsqueeze(1).to_broadcast([P, width, 4])
-            nc.vector.scalar_tensor_tensor(h_target(span), silu[span][:], 1.0, factor, MULT, MULT)
+        def gain_on_vector(span, cols=slice(None)):
+            source = silu[span][:, cols]
+            factor = gain_bank[:, 0:4].unsqueeze(1).to_broadcast(source.shape)
+            nc.vector.scalar_tensor_tensor(h_target(span)[:, cols], source, 1.0, factor, MULT, MULT)
 
-        def quantise_h(first, over=None):
+        def quantise_h(first, over=None, plane=None):
             b, j0, width = SPANS[first]
             total = sum(SPANS[member][2] for member in H_TILES[first])
             start = b * S + j0
-            plane = held([P, total], U8, "h_plane%d" % first, over)
+            if plane is None:
+                plane = held([P, total], U8, "h_plane%d" % first, over)[:]
             for k in range(0, total, P):
                 h_plane[start + k] = plane[:, k:]
             nc.vector.quantize_mx(
-                out=h_codes[:, start : start + total].bitcast(FP8X4), scales=plane[:],
+                out=h_codes[:, start : start + total].bitcast(FP8X4), scales=plane,
                 in_=h_bf[first][:].rearrange("p j t -> p (j t)"),
-            )
-
-        wo_bf = held([P, 2, N, 4], BF16, "wo_bf")
-
-        def cast_wo(b, groups):
-            nc.scalar.copy(
-                wo_bf[:, b].rearrange("p (c i) t -> p c t i", i=4)[:, groups],
-                wo_raw[b][:].rearrange("p t (c i) -> p c t i", i=4)[:, groups],
             )
 
         wo_parts = {}
 
-        def quantise_wo(over):
-            wo_parts["codes"] = held([P, 2 * N], U32, "wo_codes", over)
-            wo_parts["plane"] = held([P, 2 * N], U8, "wo_plane")
+        def cast_wo(b):
+            if b == 0:
+                wo_parts["bf"] = held([P, 2, N, 4], BF16, "wo_bf", "gated9")
+            nc.scalar.copy(
+                wo_parts["bf"][:, b].rearrange("p (c i) t -> p c t i", i=4),
+                wo_raw[b][:].rearrange("p t (c i) -> p c t i", i=4),
+            )
+
+        def quantise_wo(plane):
+            wo_parts["codes"] = held([P, 2 * N], U32, "wo_codes")
+            wo_parts["plane"] = plane
             nc.vector.quantize_mx(
-                out=wo_parts["codes"][:].bitcast(FP8X4), scales=wo_parts["plane"][:],
-                in_=wo_bf[:].rearrange("p b n t -> p (b n t)"),
+                out=wo_parts["codes"][:].bitcast(FP8X4), scales=plane,
+                in_=wo_parts["bf"][:].rearrange("p b n t -> p (b n t)"),
             )
 
         sums = {}
@@ -416,6 +420,9 @@ def tile_list_kinase_selectivity_kernel(
                 nc.tensor.transpose(gain_bank[:], gain_rows[:], identity[:])
             if c + 1 < NUNIT:
                 gate_pocket(c + 1)
+            if c == SECOND_VISIT - 2:
+                cast_wo(0)
+                cast_wo(1)
             add_shift(c)
             span, slots = UNITS[c]
             if c == 1:
@@ -426,12 +433,14 @@ def tile_list_kinase_selectivity_kernel(
                 gain_on_gpsimd(0)
                 gain_on_gpsimd(1)
             if c == SECOND_VISIT:
-                quantise_h(4, "gated%d" % c)
-                quantise_wo("h_bf4")
-                quantise_h(0, "wo_bf")
+                gain_on_vector(5, slice(P, 2 * P))
+                visit_planes = held([P, 7 * 256], U8, "visit_planes", "silu0", 3 * KIB)
+                quantise_h(4, plane=visit_planes[:, 0:512])
+                quantise_wo(visit_planes[:, 512:1024])
+                quantise_h(0, plane=visit_planes[:, 1024:1280])
                 product_half(0, 256, 0, (0,))
                 product_half(0, 256, 1)
-                quantise_h(2, "h_bf0")
+                quantise_h(2, plane=visit_planes[:, 1280:1792])
                 gain_on_gpsimd(6)
                 product_half(256, 256, 0, (1,))
             if c == NUNIT - 2:
@@ -439,10 +448,10 @@ def tile_list_kinase_selectivity_kernel(
                 product_half(768, 128, 0, (SHIFT_BANKS[c % 2],))
             if c == NUNIT - 1:
                 product_half(896, 128, 0, (SHIFT_BANKS[c % 2], POCKET_BANKS[(c - 1) % 3]))
-            if slots[-1] == 3 and 2 <= span < 6:
+            if slots[-1] == 3 and 2 <= span < 5:
                 gain_on_gpsimd(span)
-            if 6 <= c < 10:
-                cast_wo((c - 6) // 2, slice(32 * (c % 2), 32 * (c % 2) + 32))
+            if slots[-1] == 3 and span == 5:
+                gain_on_gpsimd(span, slice(0, P))
         gain_on_vector(7)
         quantise_h(6)
         product_half(256, 256, 1)

@@ -34,6 +34,7 @@ UNITS = [
 ]
 NUNIT = len(UNITS)
 FIRST_VISIT, SECOND_VISIT = 2, 13
+FIRST_TURNED = 14
 EARLY_GATE_BANKS, LATE_GATE_BANKS, POCKET_BANKS, SHIFT_BANKS = (0, 1, 7), (0, 1), (2, 3, 4), (5, 6)
 
 
@@ -201,9 +202,9 @@ def tile_list_kinase_selectivity_kernel(
         v2_words = gather_words(tab2_w, list2, "v2_words", (256, 768))
         v_plane = [stage[:, 0:S], planes[:, 0:S]]
 
-        def weight_plane(x, b, t):
+        def weight_plane(x, b, t, width=P):
             start = S + (3 * b + x) * 512 + t * P
-            return planes[:, start : start + P]
+            return planes[:, start : start + width]
 
         def moving(pieces, j0, width):
             first, size, picked = [piece for piece in pieces if piece[0] <= j0 < piece[0] + piece[1]][0]
@@ -214,6 +215,17 @@ def tile_list_kinase_selectivity_kernel(
         def gate_stage(c, number):
             span, slots = UNITS[c]
             b, j0, width = SPANS[span]
+            over = "tanh_half%d" % (c - 4) if c > 8 else {5: "w8_raw0", 6: "w4_raw0", 8: "w8_raw1"}.get(c)
+            if c >= FIRST_TURNED:
+                acc = bank(number, [P, 512])
+                nc.tensor.matmul_mx(
+                    acc[:], lhsT=moving(v2_words, j0, width), lhsT_scale=v2_plane[V2_ROW:P, j0 : j0 + width],
+                    rhs=wg_codes[b][:].bitcast(FP8X4), rhs_scale=wg_plane[b][:], start=True, stop=True,
+                )
+                over, plus = ("silu0", 4 * KIB) if c == NUNIT - 1 else (over, 0)
+                tanh_half[c] = held([P, 512], F32, "tanh_half%d" % c, over, plus)
+                nc.scalar.activation(tanh_half[c][:], acc[:], ACT.Tanh, scale=0.5)
+                return
             acc = bank(number, [P, len(slots), width])
             for i, t in enumerate(slots):
                 cols = slice(t * P, (t + 1) * P)
@@ -222,13 +234,21 @@ def tile_list_kinase_selectivity_kernel(
                     rhs=moving(v2_words, j0, width), rhs_scale=v2_plane[V2_ROW:P, j0 : j0 + width],
                     start=True, stop=True,
                 )
-            over = "tanh_half%d" % (c - 4) if c > 8 else {5: "w8_raw0", 6: "w4_raw0", 8: "w8_raw1"}.get(c)
             tanh_half[c] = held([P, width, len(slots)], F32, "tanh_half%d" % c, over)
             nc.scalar.activation(tanh_half[c][:], acc[:].rearrange("p t j -> p j t"), ACT.Tanh, scale=0.5)
 
         def pocket_stage(c):
             span, slots = UNITS[c]
             b, j0, width = SPANS[span]
+            if c >= FIRST_TURNED:
+                pocket[c] = bank(POCKET_BANKS[c % 3], [P, 512])
+                for a in range(2):
+                    nc.tensor.matmul_mx(
+                        pocket[c][:], lhsT=moving(v_words[a], j0, width), lhsT_scale=v_plane[a][:, j0 : j0 + width],
+                        rhs=w4_codes[b][:, a].rearrange("p t c -> p (t c)").bitcast(FP4X4),
+                        rhs_scale=weight_plane(W4A + a, b, 0, 512), start=a == 0, stop=a == 1,
+                    )
+                return
             pocket[c] = bank(POCKET_BANKS[c % 3], [P, len(slots), width])
             for i, t in enumerate(slots):
                 for a in range(2):
@@ -241,6 +261,16 @@ def tile_list_kinase_selectivity_kernel(
         def shift_stage(c):
             span, slots = UNITS[c]
             b, j0, width = SPANS[span]
+            if c >= FIRST_TURNED:
+                acc = bank(SHIFT_BANKS[c % 2], [P, 512])
+                nc.tensor.matmul_mx(
+                    acc[:], lhsT=moving(v2_words, j0, width), lhsT_scale=v2_plane[V2_ROW:P, j0 : j0 + width],
+                    rhs=w8_codes[b][:].rearrange("p t m -> p (t m)").bitcast(FP8X4),
+                    rhs_scale=weight_plane(W8, b, 0, 512), start=True, stop=True,
+                )
+                shift[c] = held([P, 512], F32, "shift_twice%d" % c, "mixed4", 2 * KIB * (c - FIRST_TURNED))
+                nc.scalar.activation(shift[c][:], acc[:], ACT.Copy, scale=2.0)
+                return
             shift[c] = bank(SHIFT_BANKS[c % 2], [P, len(slots), width])
             for i, t in enumerate(slots):
                 nc.tensor.matmul_mx(
@@ -254,18 +284,18 @@ def tile_list_kinase_selectivity_kernel(
             width = SPANS[span][2]
             if c == FIRST_VISIT + 2:
                 over, plus = "wg_bf1", 0
-            elif c == SECOND_VISIT:
-                over, plus = "silu0", 4 * KIB
-            elif c == SECOND_VISIT + 2:
-                over, plus = "h_bf2", 0
             else:
                 over, plus = (("tab2_w", "tab2_w", "tab_w0", "wg_raw0")[c // 4], 2 * KIB * (c % 8 if c < 8 else c % 4))
+            if c >= FIRST_TURNED:
+                gated[c] = held([P, 512], F32, "gated%d" % c, over, plus)
+                nc.vector.scalar_tensor_tensor(gated[c][:], tanh_half[c][:], 1.0, pocket[c][:], ADD, MULT)
+                return
             gated[c] = held([P, width, len(slots)], F32, "gated%d" % c, over, plus)
             nc.vector.scalar_tensor_tensor(
                 gated[c][:], tanh_half[c][:], 1.0, pocket[c][:].rearrange("p t j -> p j t"), ADD, MULT
             )
 
-        MIXED_OVER = {1: ("mixed0", 2 * KIB), 5: ("mixed0", 0), 6: ("mixed2", 0), 7: ("mixed3", 0), 8: ("mixed4", 0), 9: ("mixed4", 2 * KIB)}
+        MIXED_OVER = {1: ("mixed0", 2 * KIB), 5: ("mixed0", 0), 6: ("mixed2", 0), 7: ("mixed3", 0)}
         SILU_OVER = {
             1: ("silu0", 2 * KIB), 2: ("w4_raw1", 0), 5: ("silu0", 0), 6: ("wg_raw1", 4 * KIB), 7: ("silu3", 0), 8: ("silu4", 0),
             9: ("silu4", 2 * KIB),
@@ -289,6 +319,19 @@ def tile_list_kinase_selectivity_kernel(
                     silu[span][:].rearrange("p j (u e) -> p j u e", u=parts),
                     mixed[span][:].rearrange("p u j e -> p j u e"), ACT.Silu,
                 )
+
+        def turn_back(c):
+            span = UNITS[c][0]
+            total = bank(SHIFT_BANKS[c % 2], [P, 4, P])
+            for i, term in enumerate((shift[c], gated[c])):
+                for t in range(4):
+                    nc.tensor.matmul(
+                        total[:, t, :], lhsT=term[:, t * P : (t + 1) * P], rhs=identity[:], is_transpose=True,
+                        start=(i == 0 and t == 0), stop=(i == 1 and t == 3),
+                    )
+            over, plus = SILU_OVER[span]
+            silu[span] = held([P, P, 4], F32, "silu%d" % span, over, plus)
+            nc.scalar.activation(silu[span][:], total[:].rearrange("p t j -> p j t"), ACT.Silu, scale=0.5)
 
         H_TILES = {0: (0, 1), 2: (2, 3), 4: (4, 5), 6: (6,), 7: (7,), 8: (8,), 9: (9,)}
         H_OVER = {0: ("wg_bf1", 2 * KIB), 6: ("h_bf2", 2 * KIB)}
@@ -348,7 +391,7 @@ def tile_list_kinase_selectivity_kernel(
 
         sums = {}
 
-        def product_half(j0, width, b, numbers=None):
+        def product_half(j0, width, b, numbers=None, copy_out=nc.scalar.copy):
             if b == 0:
                 sums[j0] = [bank(number, [P, 2 // len(numbers), width]) for number in numbers]
             apart = len(sums[j0]) == 2
@@ -367,7 +410,7 @@ def tile_list_kinase_selectivity_kernel(
                     nc.vector.tensor_copy(result[:, 0, :], sums[j0][0][:, 0, :])
                     nc.scalar.copy(result[:, 1, :], sums[j0][1][:, 0, :])
                 else:
-                    nc.scalar.copy(result[:], sums[j0][0][:])
+                    copy_out(result[:], sums[j0][0][:])
                 nc.sync.dma_start(out=out.rearrange("(nt p) j -> p nt j", p=P)[:, :, j0 : j0 + width], in_=result[:])
 
         for c in range(5):
@@ -409,17 +452,14 @@ def tile_list_kinase_selectivity_kernel(
         pocket_stage(1)
         shift_stage(0)
         gate_pocket(0)
-        for c in range(NUNIT):
-            if c + 2 < NUNIT:
-                pocket_stage(c + 2)
-            if c + 1 < NUNIT:
-                shift_stage(c + 1)
+        for c in range(FIRST_TURNED):
+            pocket_stage(c + 2)
+            shift_stage(c + 1)
             if FIRST_VISIT < c <= FIRST_VISIT + 8:
                 gate_stage(c + 7 - FIRST_VISIT, LATE_GATE_BANKS[c % 2])
             if c == FIRST_VISIT + 9:
                 nc.tensor.transpose(gain_bank[:], gain_rows[:], identity[:])
-            if c + 1 < NUNIT:
-                gate_pocket(c + 1)
+            gate_pocket(c + 1)
             if c == SECOND_VISIT - 2:
                 cast_wo(0)
                 cast_wo(1)
@@ -432,34 +472,36 @@ def tile_list_kinase_selectivity_kernel(
                 quantise_wg(1, "gated%d" % c)
                 gain_on_gpsimd(0)
                 gain_on_gpsimd(1)
-            if c == SECOND_VISIT:
-                gain_on_vector(5, slice(P, 2 * P))
-                visit_planes = held([P, 7 * 256], U8, "visit_planes", "silu0", 3 * KIB)
-                quantise_h(4, plane=visit_planes[:, 0:512])
-                quantise_wo(visit_planes[:, 512:1024])
-                quantise_h(0, plane=visit_planes[:, 1024:1280])
-                product_half(0, 256, 0, (0,))
-                product_half(0, 256, 1)
-                quantise_h(2, plane=visit_planes[:, 1280:1792])
-                gain_on_gpsimd(6)
-                product_half(256, 256, 0, (1,))
-            if c == NUNIT - 2:
-                product_half(512, 256, 0, (POCKET_BANKS[(NUNIT - 1) % 3],))
-                product_half(768, 128, 0, (SHIFT_BANKS[c % 2],))
-            if c == NUNIT - 1:
-                product_half(896, 128, 0, (SHIFT_BANKS[c % 2], POCKET_BANKS[(c - 1) % 3]))
             if slots[-1] == 3 and 2 <= span < 5:
                 gain_on_gpsimd(span)
             if slots[-1] == 3 and span == 5:
                 gain_on_gpsimd(span, slice(0, P))
+        shift_stage(15)
+        gate_pocket(15)
+        turn_back(14)
+        turn_back(15)
+        gain_on_vector(5, slice(P, 2 * P))
+        visit_planes = held([P, 7 * 256], U8, "visit_planes", "silu0", 3 * KIB)
+        quantise_h(4, plane=visit_planes[:, 0:512])
+        quantise_wo(visit_planes[:, 512:1024])
+        quantise_h(0, plane=visit_planes[:, 1024:1280])
+        product_half(0, 256, 0, (0,))
+        product_half(0, 256, 1)
+        quantise_h(2, plane=visit_planes[:, 1280:1792])
+        gain_on_gpsimd(6)
+        product_half(256, 256, 0, (1,))
+        product_half(512, 256, 0, (POCKET_BANKS[0],))
+        product_half(768, 128, 0, (SHIFT_BANKS[0],))
+        product_half(896, 128, 0, (SHIFT_BANKS[1], POCKET_BANKS[2]))
         gain_on_vector(7)
-        quantise_h(6)
-        product_half(256, 256, 1)
-        quantise_h(7, "h_bf6")
-        product_half(512, 256, 1)
         gain_on_vector(8)
         gain_on_vector(9)
-        quantise_h(8, "h_bf7")
-        product_half(768, 128, 1)
-        quantise_h(9, "h_bf8")
+        last_planes = held([P, 3 * 256], U8, "last_planes", "silu6")
+        quantise_h(6, plane=last_planes[:, 0:256])
+        product_half(256, 256, 1)
+        quantise_h(7, plane=last_planes[:, 256:512])
+        product_half(512, 256, 1)
+        quantise_h(8, plane=last_planes[:, 512:640])
+        quantise_h(9, plane=last_planes[:, 640:768])
+        product_half(768, 128, 1, copy_out=nc.vector.tensor_copy)
         product_half(896, 128, 1)

@@ -297,7 +297,7 @@ def tile_list_kinase_selectivity_kernel(
 
         MIXED_OVER = {1: ("mixed0", 2 * KIB), 5: ("mixed0", 0), 6: ("mixed2", 0), 7: ("mixed3", 0)}
         SILU_OVER = {
-            1: ("silu0", 2 * KIB), 2: ("w4_raw1", 0), 5: ("silu0", 0), 6: ("wg_raw1", 4 * KIB), 7: ("silu3", 0), 8: ("silu4", 0),
+            2: ("w4_raw1", 0), 5: ("silu0", 0), 6: ("wg_raw1", 4 * KIB), 7: ("silu3", 0), 8: ("silu4", 0),
             9: ("silu4", 2 * KIB),
         }
 
@@ -314,7 +314,12 @@ def tile_list_kinase_selectivity_kernel(
             )
             if slots[-1] == 3:
                 over, plus = SILU_OVER.get(span, (None, 0))
-                silu[span] = held([P, width, 4], F32, "silu%d" % span, over, plus, 6 * KIB if span == 0 else 4 * KIB)
+                if span == 0:
+                    silu["first two"] = held([P, 2 * width, 4], F32, "silu0", room=6 * KIB)
+                if span < 2:
+                    silu[span] = silu["first two"][:, span * width : (span + 1) * width]
+                else:
+                    silu[span] = held([P, width, 4], F32, "silu%d" % span, over, plus)
                 nc.scalar.activation(
                     silu[span][:].rearrange("p j (u e) -> p j u e", u=parts),
                     mixed[span][:].rearrange("p u j e -> p j u e"), ACT.Silu,
@@ -373,12 +378,12 @@ def tile_list_kinase_selectivity_kernel(
 
         wo_parts = {}
 
-        def cast_wo(b):
-            if b == 0:
-                wo_parts["bf"] = held([P, 2, N, 4], BF16, "wo_bf", "gated9")
+        def cast_wo(b, groups):
+            if "bf" not in wo_parts:
+                wo_parts["bf"] = held([P, 2, N, 4], BF16, "wo_bf")
             nc.scalar.copy(
-                wo_parts["bf"][:, b].rearrange("p (c i) t -> p c t i", i=4),
-                wo_raw[b][:].rearrange("p t (c i) -> p c t i", i=4),
+                wo_parts["bf"][:, b].rearrange("p (c i) t -> p c t i", i=4)[:, groups],
+                wo_raw[b][:].rearrange("p t (c i) -> p c t i", i=4)[:, groups],
             )
 
         def quantise_wo(plane):
@@ -432,8 +437,8 @@ def tile_list_kinase_selectivity_kernel(
             nc.sync.dma_start(out=gain_raw[e:P:4, :, 0:13], in_=gain_runs[:, :, e : e + 13])
         load_w4(1)
         load_w8(1)
-        move_rows(slice(early, (S + 3 * H) // 4))
         load_wo(0)
+        move_rows(slice(early, (S + 3 * H) // 4))
         load_wo(1)
         gains = held([P, 8], F32, "gains", "tab_w1")
         gain_rows = held([P, P], F32, "gain_rows", "tab_w1", KIB // 2)
@@ -461,8 +466,8 @@ def tile_list_kinase_selectivity_kernel(
                 nc.tensor.transpose(gain_bank[:], gain_rows[:], identity[:])
             gate_pocket(c + 1)
             if c == SECOND_VISIT - 2:
-                cast_wo(0)
-                cast_wo(1)
+                for piece in range(4):
+                    cast_wo(piece // 2, slice(32 * (piece % 2), 32 * (piece % 2) + 32))
             add_shift(c)
             span, slots = UNITS[c]
             if c == 1:
@@ -470,8 +475,9 @@ def tile_list_kinase_selectivity_kernel(
                 order_w8(1, nc.scalar.copy, U32)
             if c == FIRST_VISIT:
                 quantise_wg(1, "gated%d" % c)
-                gain_on_gpsimd(0)
-                gain_on_gpsimd(1)
+                h_target(0)
+                factor = gains[:, 0:4].unsqueeze(1).to_broadcast([P, 256, 4])
+                nc.gpsimd.tensor_tensor(h_bf[0][:], silu["first two"][:], factor, MULT)
             if slots[-1] == 3 and 2 <= span < 5:
                 gain_on_gpsimd(span)
             if slots[-1] == 3 and span == 5:
@@ -489,19 +495,19 @@ def tile_list_kinase_selectivity_kernel(
         product_half(0, 256, 1)
         quantise_h(2, plane=visit_planes[:, 1280:1792])
         gain_on_gpsimd(6)
-        product_half(256, 256, 0, (1,))
-        product_half(512, 256, 0, (POCKET_BANKS[0],))
+        product_half(256, 256, 0, (1, 0))
+        product_half(512, 256, 0, (POCKET_BANKS[0], POCKET_BANKS[1]))
         product_half(768, 128, 0, (SHIFT_BANKS[0],))
-        product_half(896, 128, 0, (SHIFT_BANKS[1], POCKET_BANKS[2]))
+        product_half(896, 128, 0, (SHIFT_BANKS[1],))
         gain_on_vector(7)
         gain_on_vector(8)
         gain_on_vector(9)
         last_planes = held([P, 3 * 256], U8, "last_planes", "silu6")
+        quantise_h(8, plane=last_planes[:, 512:640])
+        product_half(768, 128, 1)
+        quantise_h(9, plane=last_planes[:, 640:768])
+        product_half(896, 128, 1)
         quantise_h(6, plane=last_planes[:, 0:256])
         product_half(256, 256, 1)
         quantise_h(7, plane=last_planes[:, 256:512])
         product_half(512, 256, 1)
-        quantise_h(8, plane=last_planes[:, 512:640])
-        quantise_h(9, plane=last_planes[:, 640:768])
-        product_half(768, 128, 1, copy_out=nc.vector.tensor_copy)
-        product_half(896, 128, 1)

@@ -24,7 +24,7 @@ KIB = 1024
 W4A, W4B, W8 = range(3)
 V2_ROW = 4
 SPANS = (
-    (0, 0, 128), (0, 128, 128), (0, 256, 256), (0, 512, 256), (0, 768, 256),
+    (0, 0, 128), (0, 128, 128), (0, 256, 256), (0, 512, 256), (0, 768, 128), (0, 896, 128),
     (1, 0, 256), (1, 256, 256), (1, 512, 256), (1, 768, 128), (1, 896, 128),
 )
 UNITS = [
@@ -33,8 +33,15 @@ UNITS = [
     for slots in (((0, 1, 2, 3),) if width == 128 else ((0, 1), (2, 3)))
 ]
 NUNIT = len(UNITS)
-FIRST_VISIT, SECOND_VISIT = 2, 13
-FIRST_TURNED = 14
+FIRST_VISIT = 1
+ORDER = (0, 1, 2, 3, 4, 5, 8, 9, 10, 11, 12, 13, 14, 15)
+LATE_GATE_STEP = {8: 1, 9: 3, 10: 4, 11: 5, 12: 6, 13: 7, 14: 8, 15: 9}
+TANH_OVER = {
+    5: "w8_raw0", 6: "w4_raw0", 8: "w8_raw1", 9: "tanh_half1", 10: "tanh_half2", 11: "tanh_half3", 12: "tanh_half4",
+    13: "gated9", 14: "tanh_half8", 15: "gated11",
+}
+TURNED = (6, 7, 14, 15)
+TURNED_BANKS = {6: 1, 7: 0, 14: 5, 15: 6}
 EARLY_GATE_BANKS, LATE_GATE_BANKS, POCKET_BANKS, SHIFT_BANKS = (0, 1, 7), (0, 1), (2, 3, 4), (5, 6)
 
 
@@ -60,8 +67,11 @@ def tile_list_kinase_selectivity_kernel(
                 place[name] = place[over] + plus
             return arena.tile(shape, dtype, name=name, align_bytes=64, offset=place[name])
 
+        tenants = []
+
         def bank(number, shape):
-            return psum.tile(shape, F32, name="bank%d" % number, tag="bank%d" % number)
+            tenants.append(number)
+            return psum.tile(shape, F32, name="bank%d_%d" % (number, len(tenants)), offset=2 * KIB * number)
 
         lists = keep.tile([P, S // 16], U16, name="lists")
         list2 = keep.tile([P, S // 16], U16, name="list2")
@@ -76,6 +86,12 @@ def tile_list_kinase_selectivity_kernel(
         nc.vector.memset(tab2_s[:].bitcast(I32)[0:112, :], 0)
         nc.vector.memset(v2_plane[:].bitcast(I32), 0)
         nc.vector.memset(planes[:].bitcast(I32), 0)
+        gain_rows = held([P, P], F32, "gain_rows")
+        nc.gpsimd.memset(gain_rows[:], 0.0)
+
+        warm = held([P, 2], F32, "warm")
+        nc.vector.memset(warm[:, 0:1], 0.0)
+        nc.scalar.activation(warm[:, 1:2], warm[:, 0:1], ACT.Silu)
 
         wg_raw, wg_bf, wg_codes, wg_plane, w4_codes, w8_codes, wo_raw = {}, {}, {}, {}, {}, {}, {}
 
@@ -92,11 +108,19 @@ def tile_list_kinase_selectivity_kernel(
                 wg_raw[0][:].rearrange("p j (u t e) -> p t u j e", t=4, e=4),
             )
 
-        def cast_wg_second():
-            wg_bf[1] = held([P, 4, P, 4], BF16, "wg_bf1", "tab_w1", 2 * KIB)
+        def load_wg_second(half):
+            wg_raw[1, half] = held([P, 4, 256], F32, "wg_raw1_%d" % half)
+            start = 512 + 256 * half
+            nc.sync.dma_start(
+                out=wg_raw[1, half][:], in_=wg.rearrange("(p j) c -> p j c", j=4)[:, :, start : start + 256]
+            )
+
+        def cast_wg_second(half):
+            if half == 0:
+                wg_bf[1] = held([P, 4, P, 4], BF16, "wg_bf1", "tab_w1", 5 * KIB // 2)
             nc.gpsimd.tensor_scalar(
-                wg_bf[1][:].rearrange("p t (u e) j -> p u t (e j)", e=4),
-                wg_raw[1][:].rearrange("p j c -> p c j"), 1.0, 0.0, MULT, ADD,
+                wg_bf[1][:].rearrange("p t (u e) j -> p u t (e j)", e=4)[:, 16 * half : 16 * (half + 1)],
+                wg_raw[1, half][:].rearrange("p j c -> p c j"), 1.0, 0.0, MULT, ADD,
             )
 
         def quantise_wg(b, over=None):
@@ -215,15 +239,14 @@ def tile_list_kinase_selectivity_kernel(
         def gate_stage(c, number):
             span, slots = UNITS[c]
             b, j0, width = SPANS[span]
-            over = "tanh_half%d" % (c - 4) if c > 8 else {5: "w8_raw0", 6: "w4_raw0", 8: "w8_raw1"}.get(c)
-            if c >= FIRST_TURNED:
+            over = TANH_OVER.get(c)
+            if c in TURNED:
                 acc = bank(number, [P, 512])
                 nc.tensor.matmul_mx(
                     acc[:], lhsT=moving(v2_words, j0, width), lhsT_scale=v2_plane[V2_ROW:P, j0 : j0 + width],
                     rhs=wg_codes[b][:].bitcast(FP8X4), rhs_scale=wg_plane[b][:], start=True, stop=True,
                 )
-                over, plus = ("silu0", 4 * KIB) if c == NUNIT - 1 else (over, 0)
-                tanh_half[c] = held([P, 512], F32, "tanh_half%d" % c, over, plus)
+                tanh_half[c] = held([P, 512], F32, "tanh_half%d" % c, over)
                 nc.scalar.activation(tanh_half[c][:], acc[:], ACT.Tanh, scale=0.5)
                 return
             acc = bank(number, [P, len(slots), width])
@@ -238,10 +261,11 @@ def tile_list_kinase_selectivity_kernel(
             nc.scalar.activation(tanh_half[c][:], acc[:].rearrange("p t j -> p j t"), ACT.Tanh, scale=0.5)
 
         def pocket_stage(c):
+            number = POCKET_BANKS[ORDER.index(c) % 3] if c in ORDER else TURNED_BANKS[c]
             span, slots = UNITS[c]
             b, j0, width = SPANS[span]
-            if c >= FIRST_TURNED:
-                pocket[c] = bank(POCKET_BANKS[c % 3], [P, 512])
+            if c in TURNED:
+                pocket[c] = bank(number, [P, 512])
                 for a in range(2):
                     nc.tensor.matmul_mx(
                         pocket[c][:], lhsT=moving(v_words[a], j0, width), lhsT_scale=v_plane[a][:, j0 : j0 + width],
@@ -249,7 +273,7 @@ def tile_list_kinase_selectivity_kernel(
                         rhs_scale=weight_plane(W4A + a, b, 0, 512), start=a == 0, stop=a == 1,
                     )
                 return
-            pocket[c] = bank(POCKET_BANKS[c % 3], [P, len(slots), width])
+            pocket[c] = bank(number, [P, len(slots), width])
             for i, t in enumerate(slots):
                 for a in range(2):
                     nc.tensor.matmul_mx(
@@ -261,14 +285,15 @@ def tile_list_kinase_selectivity_kernel(
         def shift_stage(c):
             span, slots = UNITS[c]
             b, j0, width = SPANS[span]
-            if c >= FIRST_TURNED:
-                acc = bank(SHIFT_BANKS[c % 2], [P, 512])
+            if c in TURNED:
+                acc = bank(TURNED_BANKS[c], [P, 512])
                 nc.tensor.matmul_mx(
                     acc[:], lhsT=moving(v2_words, j0, width), lhsT_scale=v2_plane[V2_ROW:P, j0 : j0 + width],
                     rhs=w8_codes[b][:].rearrange("p t m -> p (t m)").bitcast(FP8X4),
                     rhs_scale=weight_plane(W8, b, 0, 512), start=True, stop=True,
                 )
-                shift[c] = held([P, 512], F32, "shift_twice%d" % c, "mixed4", 2 * KIB * (c - FIRST_TURNED))
+                over = "mixed3" if c > 7 else None
+                shift[c] = held([P, 512], F32, "shift_twice%d" % c, over, 2 * KIB * (c % 2))
                 nc.scalar.activation(shift[c][:], acc[:], ACT.Copy, scale=2.0)
                 return
             shift[c] = bank(SHIFT_BANKS[c % 2], [P, len(slots), width])
@@ -282,11 +307,11 @@ def tile_list_kinase_selectivity_kernel(
         def gate_pocket(c):
             span, slots = UNITS[c]
             width = SPANS[span][2]
-            if c == FIRST_VISIT + 2:
-                over, plus = "wg_bf1", 0
+            if c in (FIRST_VISIT + 2, FIRST_VISIT + 3):
+                over, plus = "wg_bf1", -KIB + 4 * KIB * (c - FIRST_VISIT - 2)
             else:
                 over, plus = (("tab2_w", "tab2_w", "tab_w0", "wg_raw0")[c // 4], 2 * KIB * (c % 8 if c < 8 else c % 4))
-            if c >= FIRST_TURNED:
+            if c in TURNED:
                 gated[c] = held([P, 512], F32, "gated%d" % c, over, plus)
                 nc.vector.scalar_tensor_tensor(gated[c][:], tanh_half[c][:], 1.0, pocket[c][:], ADD, MULT)
                 return
@@ -295,10 +320,10 @@ def tile_list_kinase_selectivity_kernel(
                 gated[c][:], tanh_half[c][:], 1.0, pocket[c][:].rearrange("p t j -> p j t"), ADD, MULT
             )
 
-        MIXED_OVER = {1: ("mixed0", 2 * KIB), 5: ("mixed0", 0), 6: ("mixed2", 0), 7: ("mixed3", 0)}
+        MIXED_OVER = {1: ("mixed0", 2 * KIB), 6: ("mixed0", 0), 7: ("mixed2", 0)}
         SILU_OVER = {
-            2: ("w4_raw1", 0), 5: ("silu0", 0), 6: ("wg_raw1", 4 * KIB), 7: ("silu3", 0), 8: ("silu4", 0),
-            9: ("silu4", 2 * KIB),
+            2: ("w4_raw1", 0), 4: ("silu7", 4 * KIB), 6: ("silu0", 0), 8: ("silu3", 0), 9: ("silu2", 0),
+            10: ("silu2", 2 * KIB),
         }
 
         def add_shift(c):
@@ -315,11 +340,11 @@ def tile_list_kinase_selectivity_kernel(
             if slots[-1] == 3:
                 over, plus = SILU_OVER.get(span, (None, 0))
                 if span == 0:
-                    silu["first two"] = held([P, 2 * width, 4], F32, "silu0", room=6 * KIB)
+                    silu["first two"] = held([P, 2 * width, 4], F32, "silu0")
                 if span < 2:
                     silu[span] = silu["first two"][:, span * width : (span + 1) * width]
                 else:
-                    silu[span] = held([P, width, 4], F32, "silu%d" % span, over, plus)
+                    silu[span] = held([P, width, 4], F32, "silu%d" % span, over, plus, 6 * KIB if span == 7 else 0)
                 nc.scalar.activation(
                     silu[span][:].rearrange("p j (u e) -> p j u e", u=parts),
                     mixed[span][:].rearrange("p u j e -> p j u e"), ACT.Silu,
@@ -327,25 +352,25 @@ def tile_list_kinase_selectivity_kernel(
 
         def turn_back(c):
             span = UNITS[c][0]
-            total = bank(SHIFT_BANKS[c % 2], [P, 4, P])
+            total = bank(TURNED_BANKS[c], [P, 4, P])
             for i, term in enumerate((shift[c], gated[c])):
                 for t in range(4):
                     nc.tensor.matmul(
                         total[:, t, :], lhsT=term[:, t * P : (t + 1) * P], rhs=identity[:], is_transpose=True,
                         start=(i == 0 and t == 0), stop=(i == 1 and t == 3),
                     )
-            over, plus = SILU_OVER[span]
+            over, plus = SILU_OVER.get(span, (None, 0))
             silu[span] = held([P, P, 4], F32, "silu%d" % span, over, plus)
             nc.scalar.activation(silu[span][:], total[:].rearrange("p t j -> p j t"), ACT.Silu, scale=0.5)
 
-        H_TILES = {0: (0, 1), 2: (2, 3), 4: (4, 5), 6: (6,), 7: (7,), 8: (8,), 9: (9,)}
-        H_OVER = {0: ("wg_bf1", 2 * KIB), 6: ("h_bf2", 2 * KIB)}
+        H_TILES = {0: (0, 1), 2: (2, 3), 4: (4, 5), 6: (6, 7), 8: (8,), 9: (9, 10)}
+        H_OVER = {0: ("wg_bf1", KIB), 8: ("h_bf2", 2 * KIB)}
         h_bf, h_at, h_plane = {}, {}, {}
         h_codes = held([P, 2 * S], U32, "h_codes")
 
         def h_target(span):
             first = [key for key in H_TILES if span in H_TILES[key]][0]
-            if span == first:
+            if first not in h_bf:
                 over, plus = H_OVER.get(first, (None, 0))
                 total = sum(SPANS[member][2] for member in H_TILES[first])
                 h_bf[first] = held([P, total, 4], BF16, "h_bf%d" % first, over, plus)
@@ -359,8 +384,9 @@ def tile_list_kinase_selectivity_kernel(
             nc.gpsimd.tensor_tensor(h_target(span)[:, cols], source, factor, MULT)
 
         def gain_on_vector(span, cols=slice(None)):
+            b = SPANS[span][0]
             source = silu[span][:, cols]
-            factor = gain_bank[:, 0:4].unsqueeze(1).to_broadcast(source.shape)
+            factor = gain_bank[:, 4 * b : 4 * b + 4].unsqueeze(1).to_broadcast(source.shape)
             nc.vector.scalar_tensor_tensor(h_target(span)[:, cols], source, 1.0, factor, MULT, MULT)
 
         def quantise_h(first, over=None, plane=None):
@@ -428,86 +454,86 @@ def tile_list_kinase_selectivity_kernel(
         gate_stage(6, EARLY_GATE_BANKS[0])
         order_w8(0, nc.scalar.copy, U32)
         gate_stage(5, EARLY_GATE_BANKS[2])
-        gate_stage(7, EARLY_GATE_BANKS[2])
         v_words.append(gather_words(tab_w[1], lists, "v_words1", (256, 768)))
-        load_wg(1)
-        gain_raw = held([P, 2, 16], F32, "gain_raw")
-        gain_runs = gain.rearrange("(b u x) -> u b x", b=2, x=16)
-        for e in range(4):
-            nc.sync.dma_start(out=gain_raw[e:P:4, :, 0:13], in_=gain_runs[:, :, e : e + 13])
+        load_wg_second(0)
+        load_wg_second(1)
+        for b in range(2):
+            nc.sync.dma_start(
+                out=gain_rows[4 * b : 4 * b + 4, :].rearrange("t (u e) -> t u e", e=4),
+                in_=gain[512 * b : 512 * (b + 1)].rearrange("(u t e) -> t u e", t=4, e=4),
+            )
         load_w4(1)
         load_w8(1)
-        load_wo(0)
         move_rows(slice(early, (S + 3 * H) // 4))
+        load_wo(0)
         load_wo(1)
-        gains = held([P, 8], F32, "gains", "tab_w1")
-        gain_rows = held([P, P], F32, "gain_rows", "tab_w1", KIB // 2)
         identity = held([P, P], F32, "identity", "tab_w1", KIB)
-        nc.gpsimd.memset(gain_rows[:], 0.0)
         make_identity(nc, identity[:])
-        nc.sync.dma_start(
-            out=gain_rows[0:4, :].rearrange("t (u e) -> t u e", e=4),
-            in_=gain[512:H].rearrange("(u t e) -> t u e", t=4, e=4),
-        )
-        gain_bank = bank(7, [P, P])
-        cast_wg_second()
-        nc.gpsimd.tensor_copy(gains[:].rearrange("p (b t) -> p b t", t=4), gain_raw[:, :, 0:13:4])
+        cast_wg_second(0)
+        cast_wg_second(1)
 
         pocket_stage(0)
         pocket_stage(1)
         shift_stage(0)
+        shift_stage(6)
+        shift_stage(7)
+        gate_stage(7, EARLY_GATE_BANKS[2])
+        gain_bank = bank(7, [P, P])
+        gains = held([P, 8], F32, "gains")
         gate_pocket(0)
-        for c in range(FIRST_TURNED):
-            pocket_stage(c + 2)
-            shift_stage(c + 1)
-            if FIRST_VISIT < c <= FIRST_VISIT + 8:
-                gate_stage(c + 7 - FIRST_VISIT, LATE_GATE_BANKS[c % 2])
-            if c == FIRST_VISIT + 9:
-                nc.tensor.transpose(gain_bank[:], gain_rows[:], identity[:])
-            gate_pocket(c + 1)
-            if c == SECOND_VISIT - 2:
-                for piece in range(4):
-                    cast_wo(piece // 2, slice(32 * (piece % 2), 32 * (piece % 2) + 32))
+        for step, c in enumerate(ORDER[:-2]):
+            pocket_stage(ORDER[step + 2])
+            shift_stage(ORDER[step + 1])
+            gate_pocket(ORDER[step + 1])
             add_shift(c)
             span, slots = UNITS[c]
-            if c == 1:
+            if step == 1:
                 order_w4(1, nc.scalar.copy, U32)
                 order_w8(1, nc.scalar.copy, U32)
-            if c == FIRST_VISIT:
+            if step == FIRST_VISIT:
                 quantise_wg(1, "gated%d" % c)
+                nc.tensor.transpose(gain_bank[:], gain_rows[:], identity[:])
+                nc.vector.tensor_copy(gains[:], gain_bank[:, 0:8])
                 h_target(0)
                 factor = gains[:, 0:4].unsqueeze(1).to_broadcast([P, 256, 4])
                 nc.gpsimd.tensor_tensor(h_bf[0][:], silu["first two"][:], factor, MULT)
-            if slots[-1] == 3 and 2 <= span < 5:
+            for late in LATE_GATE_STEP:
+                if LATE_GATE_STEP[late] == step:
+                    gate_stage(late, LATE_GATE_BANKS[(late + 1) % 2])
+            if slots[-1] == 3 and span in (2, 3, 6, 7):
                 gain_on_gpsimd(span)
-            if slots[-1] == 3 and span == 5:
-                gain_on_gpsimd(span, slice(0, P))
+            if c in (11, 12):
+                pocket_stage(c - 5)
+                gate_pocket(c - 5)
+            if c == 11:
+                turn_back(6)
+                for piece in range(4):
+                    cast_wo(piece // 2, slice(32 * (piece % 2), 32 * (piece % 2) + 32))
         shift_stage(15)
         gate_pocket(15)
+        turn_back(7)
         turn_back(14)
         turn_back(15)
-        gain_on_vector(5, slice(P, 2 * P))
-        visit_planes = held([P, 7 * 256], U8, "visit_planes", "silu0", 3 * KIB)
-        quantise_h(4, plane=visit_planes[:, 0:512])
+        gain_on_vector(4)
+        visit_planes = held([P, 7 * 256], U8, "visit_planes", "silu7", 3 * KIB)
+        quantise_h(6, plane=visit_planes[:, 0:512])
         quantise_wo(visit_planes[:, 512:1024])
         quantise_h(0, plane=visit_planes[:, 1024:1280])
-        product_half(0, 256, 0, (0,))
+        product_half(0, 256, 0, (4,))
         product_half(0, 256, 1)
         quantise_h(2, plane=visit_planes[:, 1280:1792])
-        gain_on_gpsimd(6)
-        product_half(256, 256, 0, (1, 0))
-        product_half(512, 256, 0, (POCKET_BANKS[0], POCKET_BANKS[1]))
-        product_half(768, 128, 0, (SHIFT_BANKS[0],))
-        product_half(896, 128, 0, (SHIFT_BANKS[1],))
-        gain_on_vector(7)
-        gain_on_vector(8)
-        gain_on_vector(9)
-        last_planes = held([P, 3 * 256], U8, "last_planes", "silu6")
-        quantise_h(8, plane=last_planes[:, 512:640])
-        product_half(768, 128, 1)
-        quantise_h(9, plane=last_planes[:, 640:768])
-        product_half(896, 128, 1)
-        quantise_h(6, plane=last_planes[:, 0:256])
+        product_half(256, 256, 0, (2,))
         product_half(256, 256, 1)
-        quantise_h(7, plane=last_planes[:, 256:512])
+        gain_on_gpsimd(8, slice(0, 192))
+        product_half(512, 256, 0, (3, 1))
+        gain_on_vector(5)
+        gain_on_vector(9)
+        gain_on_vector(10)
+        gain_on_vector(8, slice(192, 256))
+        last_planes = held([P, 3 * 256], U8, "last_planes", "silu8")
+        quantise_h(4, plane=last_planes[:, 0:256])
+        product_half(768, 256, 0, (0,))
+        quantise_h(9, plane=last_planes[:, 256:512])
+        product_half(768, 256, 1)
+        quantise_h(8, plane=last_planes[:, 512:768])
         product_half(512, 256, 1)

@@ -292,8 +292,8 @@ def tile_list_kinase_selectivity_kernel(
                     rhs=w8_codes[b][:].rearrange("p t m -> p (t m)").bitcast(FP8X4),
                     rhs_scale=weight_plane(W8, b, 0, 512), start=True, stop=True,
                 )
-                over = "mixed3" if c > 7 else None
-                shift[c] = held([P, 512], F32, "shift_twice%d" % c, over, 2 * KIB * (c % 2))
+                over = "shift_twice%d" % (c - 8) if c > 7 else None
+                shift[c] = held([P, 512], F32, "shift_twice%d" % c, over)
                 nc.scalar.activation(shift[c][:], acc[:], ACT.Copy, scale=2.0)
                 return
             shift[c] = bank(SHIFT_BANKS[c % 2], [P, len(slots), width])
@@ -322,7 +322,7 @@ def tile_list_kinase_selectivity_kernel(
 
         MIXED_OVER = {1: ("mixed0", 2 * KIB), 6: ("mixed0", 0), 7: ("mixed2", 0)}
         SILU_OVER = {
-            2: ("w4_raw1", 0), 4: ("silu7", 4 * KIB), 6: ("silu0", 0), 8: ("silu3", 0), 9: ("silu2", 0),
+            2: ("w4_raw1", 0), 6: ("silu0", 0), 8: ("gated5", 0), 9: ("silu2", 0),
             10: ("silu2", 2 * KIB),
         }
 
@@ -344,7 +344,7 @@ def tile_list_kinase_selectivity_kernel(
                 if span < 2:
                     silu[span] = silu["first two"][:, span * width : (span + 1) * width]
                 else:
-                    silu[span] = held([P, width, 4], F32, "silu%d" % span, over, plus, 6 * KIB if span == 7 else 0)
+                    silu[span] = held([P, width, 4], F32, "silu%d" % span, over, plus)
                 nc.scalar.activation(
                     silu[span][:].rearrange("p j (u e) -> p j u e", u=parts),
                     mixed[span][:].rearrange("p u j e -> p j u e"), ACT.Silu,
@@ -364,7 +364,7 @@ def tile_list_kinase_selectivity_kernel(
             nc.scalar.activation(silu[span][:], total[:].rearrange("p t j -> p j t"), ACT.Silu, scale=0.5)
 
         H_TILES = {0: (0, 1), 2: (2, 3), 4: (4, 5), 6: (6, 7), 8: (8,), 9: (9, 10)}
-        H_OVER = {0: ("wg_bf1", KIB), 8: ("h_bf2", 2 * KIB)}
+        H_OVER = {0: ("wg_bf1", KIB), 4: ("h_bf2", 0), 8: ("h_bf2", 2 * KIB), 9: ("wo_bf0", 0)}
         h_bf, h_at, h_plane = {}, {}, {}
         h_codes = held([P, 2 * S], U32, "h_codes")
 
@@ -402,22 +402,22 @@ def tile_list_kinase_selectivity_kernel(
                 in_=h_bf[first][:].rearrange("p j t -> p (j t)"),
             )
 
-        wo_parts = {}
+        wo_bf, wo_plane = {}, {}
+        wo_codes = held([P, 2 * N], U32, "wo_codes")
 
-        def cast_wo(b, groups):
-            if "bf" not in wo_parts:
-                wo_parts["bf"] = held([P, 2, N, 4], BF16, "wo_bf")
-            nc.scalar.copy(
-                wo_parts["bf"][:, b].rearrange("p (c i) t -> p c t i", i=4)[:, groups],
+        def cast_wo(b, groups, move, over=None):
+            if b not in wo_bf:
+                wo_bf[b] = held([P, N, 4], BF16, "wo_bf%d" % b, over)
+            move(
+                wo_bf[b][:].rearrange("p (c i) t -> p c t i", i=4)[:, groups],
                 wo_raw[b][:].rearrange("p t (c i) -> p c t i", i=4)[:, groups],
             )
 
-        def quantise_wo(plane):
-            wo_parts["codes"] = held([P, 2 * N], U32, "wo_codes")
-            wo_parts["plane"] = plane
+        def quantise_wo(b, plane):
+            wo_plane[b] = plane
             nc.vector.quantize_mx(
-                out=wo_parts["codes"][:].bitcast(FP8X4), scales=plane,
-                in_=wo_parts["bf"][:].rearrange("p b n t -> p (b n t)"),
+                out=wo_codes[:, b * N : (b + 1) * N].bitcast(FP8X4), scales=plane,
+                in_=wo_bf[b][:].rearrange("p n t -> p (n t)"),
             )
 
         sums = {}
@@ -431,7 +431,7 @@ def tile_list_kinase_selectivity_kernel(
                 cols = slice(b * N + nt * P, b * N + (nt + 1) * P)
                 nc.tensor.matmul_mx(
                     sums[j0][nt][:, 0, :] if apart else sums[j0][0][:, nt, :],
-                    lhsT=wo_parts["codes"][:, cols].bitcast(FP8X4), lhsT_scale=wo_parts["plane"][:, cols],
+                    lhsT=wo_codes[:, cols].bitcast(FP8X4), lhsT_scale=wo_plane[b][:, nt * P : (nt + 1) * P],
                     rhs=h_codes[:, start : start + width].bitcast(FP8X4), rhs_scale=h_plane[start][:, 0:width],
                     start=(b == 0 and (apart or nt == 0)), stop=(b == 1 and (apart or nt == 1)),
                 )
@@ -500,40 +500,45 @@ def tile_list_kinase_selectivity_kernel(
             for late in LATE_GATE_STEP:
                 if LATE_GATE_STEP[late] == step:
                     gate_stage(late, LATE_GATE_BANKS[(late + 1) % 2])
-            if slots[-1] == 3 and span in (2, 3, 6, 7):
+            if slots[-1] == 3 and span in (2, 3, 6):
                 gain_on_gpsimd(span)
+            if slots[-1] == 3 and span == 7:
+                gain_on_gpsimd(span, slice(0, P))
             if c in (11, 12):
                 pocket_stage(c - 5)
                 gate_pocket(c - 5)
             if c == 11:
                 turn_back(6)
-                for piece in range(4):
-                    cast_wo(piece // 2, slice(32 * (piece % 2), 32 * (piece % 2) + 32))
+                for piece in range(2):
+                    cast_wo(0, slice(32 * piece, 32 * piece + 32), nc.scalar.copy)
         shift_stage(15)
         gate_pocket(15)
         turn_back(7)
         turn_back(14)
         turn_back(15)
-        gain_on_vector(4)
-        visit_planes = held([P, 7 * 256], U8, "visit_planes", "silu7", 3 * KIB)
+        gain_on_vector(7, slice(P, 2 * P))
+        visit_planes = held([P, 7 * 256], U8, "visit_planes", "silu7", 2 * KIB)
+        cast_wo(1, slice(0, 64), nc.vector.tensor_copy, "silu7")
         quantise_h(6, plane=visit_planes[:, 0:512])
-        quantise_wo(visit_planes[:, 512:1024])
+        quantise_wo(0, visit_planes[:, 512:768])
         quantise_h(0, plane=visit_planes[:, 1024:1280])
+        quantise_wo(1, visit_planes[:, 768:1024])
         product_half(0, 256, 0, (4,))
         product_half(0, 256, 1)
         quantise_h(2, plane=visit_planes[:, 1280:1792])
-        product_half(256, 256, 0, (2,))
+        product_half(256, 256, 0, (6,))
         product_half(256, 256, 1)
-        gain_on_gpsimd(8, slice(0, 192))
-        product_half(512, 256, 0, (3, 1))
+        gain_on_gpsimd(8, slice(0, 224))
+        product_half(512, 256, 0, (3,))
+        gain_on_vector(4)
         gain_on_vector(5)
         gain_on_vector(9)
         gain_on_vector(10)
-        gain_on_vector(8, slice(192, 256))
+        gain_on_vector(8, slice(224, 256))
         last_planes = held([P, 3 * 256], U8, "last_planes", "silu8")
-        quantise_h(4, plane=last_planes[:, 0:256])
-        product_half(768, 256, 0, (0,))
-        quantise_h(9, plane=last_planes[:, 256:512])
-        product_half(768, 256, 1)
         quantise_h(8, plane=last_planes[:, 512:768])
         product_half(512, 256, 1)
+        quantise_h(4, plane=last_planes[:, 0:256])
+        product_half(768, 256, 0, (0, 1))
+        quantise_h(9, plane=last_planes[:, 256:512])
+        product_half(768, 256, 1)

@@ -24,7 +24,7 @@ KIB = 1024
 W4A, W4B, W8 = range(3)
 V2_ROW = 4
 SPANS = (
-    (0, 0, 128), (0, 128, 128), (0, 256, 256), (0, 512, 256), (0, 768, 128), (0, 896, 128),
+    (0, 0, 256), (0, 256, 256), (0, 512, 256), (0, 768, 128), (0, 896, 128),
     (1, 0, 256), (1, 256, 256), (1, 512, 256), (1, 768, 128), (1, 896, 128),
 )
 UNITS = [
@@ -37,7 +37,7 @@ FIRST_VISIT = 1
 ORDER = (0, 1, 2, 3, 4, 5, 8, 9, 10, 11, 12, 13, 14, 15)
 LATE_GATE_STEP = {8: 1, 9: 3, 10: 4, 11: 5, 12: 6, 13: 7, 14: 8, 15: 9}
 TANH_OVER = {
-    5: "w8_raw0", 6: "w4_raw0", 8: "w8_raw1", 9: "tanh_half1", 10: "tanh_half2", 11: "tanh_half3", 12: "tanh_half4",
+    5: "w8_room", 6: "w4_raw0", 7: "w8_room_end", 8: "w8_raw1", 9: "tanh_half1", 10: "tanh_half2", 11: "tanh_half3", 12: "tanh_half4",
     13: "gated9", 14: "tanh_half8", 15: "gated11",
 }
 TURNED = (6, 7, 14, 15)
@@ -146,7 +146,10 @@ def tile_list_kinase_selectivity_kernel(
             )
 
         def load_w8(b):
-            w8_raw[b] = held([P, 512], U32, "w8_raw%d" % b)
+            if b == 0:
+                place["w8_room"], place["w8_room_end"] = place["top"], place["top"] + 2 * KIB
+                place["top"] = place["top"] + 4 * KIB
+            w8_raw[b] = held([P, 512], U32, "w8_raw%d" % b, None if b else "w8_room", KIB)
             nc.sync.dma_start(
                 out=w8_raw[b][:].bitcast(I32),
                 in_=w8_words[0].rearrange("p c i -> p (c i)").bitcast(I32)[:, 512 * b : 512 * (b + 1)],
@@ -292,8 +295,8 @@ def tile_list_kinase_selectivity_kernel(
                     rhs=w8_codes[b][:].rearrange("p t m -> p (t m)").bitcast(FP8X4),
                     rhs_scale=weight_plane(W8, b, 0, 512), start=True, stop=True,
                 )
-                over = "shift_twice%d" % (c - 8) if c > 7 else None
-                shift[c] = held([P, 512], F32, "shift_twice%d" % c, over)
+                over = "mixed2" if c > 7 else None
+                shift[c] = held([P, 512], F32, "shift_twice%d" % c, over, 2 * KIB * (c % 2))
                 nc.scalar.activation(shift[c][:], acc[:], ACT.Copy, scale=2.0)
                 return
             shift[c] = bank(SHIFT_BANKS[c % 2], [P, len(slots), width])
@@ -320,10 +323,9 @@ def tile_list_kinase_selectivity_kernel(
                 gated[c][:], tanh_half[c][:], 1.0, pocket[c][:].rearrange("p t j -> p j t"), ADD, MULT
             )
 
-        MIXED_OVER = {1: ("mixed0", 2 * KIB), 6: ("mixed0", 0), 7: ("mixed2", 0)}
+        MIXED_OVER = {5: ("mixed0", 0), 6: ("mixed1", 0)}
         SILU_OVER = {
-            2: ("w4_raw1", 0), 6: ("silu0", 0), 8: ("gated5", 0), 9: ("silu2", 0),
-            10: ("silu2", 2 * KIB),
+            1: ("w4_raw1", 0), 5: ("silu0", 0), 7: ("silu2", 0), 8: ("silu1", 0), 9: ("silu1", 2 * KIB),
         }
 
         def add_shift(c):
@@ -339,12 +341,7 @@ def tile_list_kinase_selectivity_kernel(
             )
             if slots[-1] == 3:
                 over, plus = SILU_OVER.get(span, (None, 0))
-                if span == 0:
-                    silu["first two"] = held([P, 2 * width, 4], F32, "silu0")
-                if span < 2:
-                    silu[span] = silu["first two"][:, span * width : (span + 1) * width]
-                else:
-                    silu[span] = held([P, width, 4], F32, "silu%d" % span, over, plus)
+                silu[span] = held([P, width, 4], F32, "silu%d" % span, over, plus)
                 nc.scalar.activation(
                     silu[span][:].rearrange("p j (u e) -> p j u e", u=parts),
                     mixed[span][:].rearrange("p u j e -> p j u e"), ACT.Silu,
@@ -363,8 +360,8 @@ def tile_list_kinase_selectivity_kernel(
             silu[span] = held([P, P, 4], F32, "silu%d" % span, over, plus)
             nc.scalar.activation(silu[span][:], total[:].rearrange("p t j -> p j t"), ACT.Silu, scale=0.5)
 
-        H_TILES = {0: (0, 1), 2: (2, 3), 4: (4, 5), 6: (6, 7), 8: (8,), 9: (9, 10)}
-        H_OVER = {0: ("wg_bf1", KIB), 4: ("h_bf2", 0), 8: ("h_bf2", 2 * KIB), 9: ("wo_bf0", 0)}
+        H_TILES = {0: (0,), 1: (1, 2), 3: (3, 4), 5: (5, 6), 7: (7,), 8: (8, 9)}
+        H_OVER = {0: ("wg_bf1", KIB), 3: ("h_bf1", 0), 7: ("h_bf1", 2 * KIB), 8: ("wo_bf0", 0)}
         h_bf, h_at, h_plane = {}, {}, {}
         h_codes = held([P, 2 * S], U32, "h_codes")
 
@@ -423,7 +420,8 @@ def tile_list_kinase_selectivity_kernel(
         sums = {}
 
         def product_half(j0, width, b, numbers=None, copy_out=nc.scalar.copy):
-            if b == 0:
+            first = j0 not in sums
+            if first:
                 sums[j0] = [bank(number, [P, 2 // len(numbers), width]) for number in numbers]
             apart = len(sums[j0]) == 2
             start = b * S + j0
@@ -433,9 +431,9 @@ def tile_list_kinase_selectivity_kernel(
                     sums[j0][nt][:, 0, :] if apart else sums[j0][0][:, nt, :],
                     lhsT=wo_codes[:, cols].bitcast(FP8X4), lhsT_scale=wo_plane[b][:, nt * P : (nt + 1) * P],
                     rhs=h_codes[:, start : start + width].bitcast(FP8X4), rhs_scale=h_plane[start][:, 0:width],
-                    start=(b == 0 and (apart or nt == 0)), stop=(b == 1 and (apart or nt == 1)),
+                    start=(first and (apart or nt == 0)), stop=(not first and (apart or nt == 1)),
                 )
-            if b == 1:
+            if not first:
                 result = held([P, 2, width], F32, "result%d" % j0)
                 if apart:
                     nc.vector.tensor_copy(result[:, 0, :], sums[j0][0][:, 0, :])
@@ -453,6 +451,7 @@ def tile_list_kinase_selectivity_kernel(
         order_w4(0, nc.scalar.copy, U32)
         gate_stage(6, EARLY_GATE_BANKS[0])
         order_w8(0, nc.scalar.copy, U32)
+        gate_stage(7, SHIFT_BANKS[1])
         gate_stage(5, EARLY_GATE_BANKS[2])
         v_words.append(gather_words(tab_w[1], lists, "v_words1", (256, 768)))
         load_wg_second(0)
@@ -475,9 +474,6 @@ def tile_list_kinase_selectivity_kernel(
         pocket_stage(0)
         pocket_stage(1)
         shift_stage(0)
-        shift_stage(6)
-        shift_stage(7)
-        gate_stage(7, EARLY_GATE_BANKS[2])
         gain_bank = bank(7, [P, P])
         gains = held([P, 8], F32, "gains")
         gate_pocket(0)
@@ -485,6 +481,9 @@ def tile_list_kinase_selectivity_kernel(
             pocket_stage(ORDER[step + 2])
             shift_stage(ORDER[step + 1])
             gate_pocket(ORDER[step + 1])
+            if step == 1:
+                shift_stage(6)
+                shift_stage(7)
             add_shift(c)
             span, slots = UNITS[c]
             if step == 1:
@@ -494,51 +493,43 @@ def tile_list_kinase_selectivity_kernel(
                 quantise_wg(1, "gated%d" % c)
                 nc.tensor.transpose(gain_bank[:], gain_rows[:], identity[:])
                 nc.vector.tensor_copy(gains[:], gain_bank[:, 0:8])
-                h_target(0)
-                factor = gains[:, 0:4].unsqueeze(1).to_broadcast([P, 256, 4])
-                nc.gpsimd.tensor_tensor(h_bf[0][:], silu["first two"][:], factor, MULT)
             for late in LATE_GATE_STEP:
                 if LATE_GATE_STEP[late] == step:
                     gate_stage(late, LATE_GATE_BANKS[(late + 1) % 2])
-            if slots[-1] == 3 and span in (2, 3, 6):
+            if slots[-1] == 3 and span in (0, 1, 2, 5):
                 gain_on_gpsimd(span)
-            if slots[-1] == 3 and span == 7:
+            if slots[-1] == 3 and span == 6:
                 gain_on_gpsimd(span, slice(0, P))
-            if c in (11, 12):
-                pocket_stage(c - 5)
-                gate_pocket(c - 5)
-            if c == 11:
-                turn_back(6)
                 for piece in range(2):
                     cast_wo(0, slice(32 * piece, 32 * piece + 32), nc.scalar.copy)
         shift_stage(15)
         gate_pocket(15)
-        turn_back(7)
-        turn_back(14)
-        turn_back(15)
-        gain_on_vector(7, slice(P, 2 * P))
-        visit_planes = held([P, 7 * 256], U8, "visit_planes", "silu7", 2 * KIB)
-        cast_wo(1, slice(0, 64), nc.vector.tensor_copy, "silu7")
-        quantise_h(6, plane=visit_planes[:, 0:512])
+        for c in (6, 7):
+            pocket_stage(c)
+            gate_pocket(c)
+        for c in (14, 15, 6, 7):
+            turn_back(c)
+        gain_on_vector(6, slice(P, 2 * P))
+        visit_planes = held([P, 7 * 256], U8, "visit_planes", "silu6", 2 * KIB)
+        cast_wo(1, slice(0, 64), nc.vector.tensor_copy, "silu6")
+        quantise_h(5, plane=visit_planes[:, 0:512])
         quantise_wo(0, visit_planes[:, 512:768])
         quantise_h(0, plane=visit_planes[:, 1024:1280])
         quantise_wo(1, visit_planes[:, 768:1024])
         product_half(0, 256, 0, (4,))
         product_half(0, 256, 1)
-        quantise_h(2, plane=visit_planes[:, 1280:1792])
-        product_half(256, 256, 0, (6,))
+        quantise_h(1, plane=visit_planes[:, 1280:1792])
+        product_half(256, 256, 0, (0,))
         product_half(256, 256, 1)
-        gain_on_gpsimd(8, slice(0, 224))
+        gain_on_gpsimd(7, slice(0, 224))
         product_half(512, 256, 0, (3,))
-        gain_on_vector(4)
-        gain_on_vector(5)
-        gain_on_vector(9)
-        gain_on_vector(10)
-        gain_on_vector(8, slice(224, 256))
-        last_planes = held([P, 3 * 256], U8, "last_planes", "silu8")
-        quantise_h(8, plane=last_planes[:, 512:768])
+        for span in (8, 9, 3, 4):
+            gain_on_vector(span)
+        gain_on_vector(7, slice(224, 256))
+        last_planes = held([P, 3 * 256], U8, "last_planes", "silu7")
+        quantise_h(7, plane=last_planes[:, 512:768])
         product_half(512, 256, 1)
-        quantise_h(4, plane=last_planes[:, 0:256])
-        product_half(768, 256, 0, (0, 1))
-        quantise_h(9, plane=last_planes[:, 256:512])
-        product_half(768, 256, 1)
+        quantise_h(8, plane=last_planes[:, 256:512])
+        product_half(768, 256, 1, (5, 6))
+        quantise_h(3, plane=last_planes[:, 0:256])
+        product_half(768, 256, 0)

@@ -499,7 +499,6 @@ def tile_list_kinase_selectivity_kernel(
             if slots[-1] == 3 and span in (0, 1, 2, 5):
                 gain_on_gpsimd(span)
             if slots[-1] == 3 and span == 6:
-                gain_on_gpsimd(span, slice(0, P))
                 for piece in range(2):
                     cast_wo(0, slice(32 * piece, 32 * piece + 32), nc.scalar.copy)
         shift_stage(15)
@@ -509,7 +508,7 @@ def tile_list_kinase_selectivity_kernel(
             gate_pocket(c)
         for c in (14, 15, 6, 7):
             turn_back(c)
-        gain_on_vector(6, slice(P, 2 * P))
+        gain_on_vector(6)
         visit_planes = held([P, 7 * 256], U8, "visit_planes", "silu6", 2 * KIB)
         cast_wo(1, slice(0, 64), nc.vector.tensor_copy, "silu6")
         quantise_h(5, plane=visit_planes[:, 0:512])
@@ -521,11 +520,11 @@ def tile_list_kinase_selectivity_kernel(
         quantise_h(1, plane=visit_planes[:, 1280:1792])
         product_half(256, 256, 0, (0,))
         product_half(256, 256, 1)
-        gain_on_gpsimd(7, slice(0, 224))
+        gain_on_gpsimd(7, slice(0, 192))
         product_half(512, 256, 0, (3,))
         for span in (8, 9, 3, 4):
             gain_on_vector(span)
-        gain_on_vector(7, slice(224, 256))
+        gain_on_vector(7, slice(192, 256))
         last_planes = held([P, 3 * 256], U8, "last_planes", "silu7")
         quantise_h(7, plane=last_planes[:, 512:768])
         product_half(512, 256, 1)

@@ -37,11 +37,12 @@ FIRST_VISIT = 1
 ORDER = (0, 1, 2, 3, 4, 5, 8, 9, 10, 11, 12, 13, 14, 15)
 LATE_GATE_STEP = {8: 1, 9: 3, 10: 4, 11: 5, 12: 6, 13: 7, 14: 8, 15: 9}
 TANH_OVER = {
-    5: "w8_room", 6: "w4_raw0", 7: "w8_room_end", 8: "w8_raw1", 9: "tanh_half1", 10: "tanh_half2", 11: "tanh_half3", 12: "tanh_half4",
+    5: "w8_room", 6: "w4_raw0", 7: "w8_room_end", 8: "tanh_half0", 9: "tanh_half1", 10: "tanh_half2", 11: "tanh_half3", 12: "tanh_half4",
     13: "gated9", 14: "tanh_half8", 15: "gated11",
 }
 TURNED = (6, 7, 14, 15)
 TURNED_BANKS = {6: 1, 7: 0, 14: 5, 15: 6}
+TURNED_SHIFT_BANKS = {6: 0, 7: 7, 14: 5, 15: 6}
 EARLY_GATE_BANKS, LATE_GATE_BANKS, POCKET_BANKS, SHIFT_BANKS = (0, 1, 7), (0, 1), (2, 3, 4), (5, 6)
 
 
@@ -289,7 +290,7 @@ def tile_list_kinase_selectivity_kernel(
             span, slots = UNITS[c]
             b, j0, width = SPANS[span]
             if c in TURNED:
-                acc = bank(TURNED_BANKS[c], [P, 512])
+                acc = bank(TURNED_SHIFT_BANKS[c], [P, 512])
                 nc.tensor.matmul_mx(
                     acc[:], lhsT=moving(v2_words, j0, width), lhsT_scale=v2_plane[V2_ROW:P, j0 : j0 + width],
                     rhs=w8_codes[b][:].rearrange("p t m -> p (t m)").bitcast(FP8X4),
@@ -474,14 +475,13 @@ def tile_list_kinase_selectivity_kernel(
         pocket_stage(0)
         pocket_stage(1)
         shift_stage(0)
-        gain_bank = bank(7, [P, P])
         gains = held([P, 8], F32, "gains")
         gate_pocket(0)
         for step, c in enumerate(ORDER[:-2]):
             pocket_stage(ORDER[step + 2])
             shift_stage(ORDER[step + 1])
             gate_pocket(ORDER[step + 1])
-            if step == 1:
+            if step == 0:
                 shift_stage(6)
                 shift_stage(7)
             add_shift(c)
@@ -491,6 +491,7 @@ def tile_list_kinase_selectivity_kernel(
                 order_w8(1, nc.scalar.copy, U32)
             if step == FIRST_VISIT:
                 quantise_wg(1, "gated%d" % c)
+                gain_bank = bank(7, [P, P])
                 nc.tensor.transpose(gain_bank[:], gain_rows[:], identity[:])
                 nc.vector.tensor_copy(gains[:], gain_bank[:, 0:8])
             for late in LATE_GATE_STEP:
@@ -499,8 +500,9 @@ def tile_list_kinase_selectivity_kernel(
             if slots[-1] == 3 and span in (0, 1, 2, 5):
                 gain_on_gpsimd(span)
             if slots[-1] == 3 and span == 6:
-                for piece in range(2):
-                    cast_wo(0, slice(32 * piece, 32 * piece + 32), nc.scalar.copy)
+                gain_on_gpsimd(span, slice(0, 64))
+                for piece in range(4):
+                    cast_wo(piece // 2, slice(32 * (piece % 2), 32 * (piece % 2) + 32), nc.scalar.copy)
         shift_stage(15)
         gate_pocket(15)
         for c in (6, 7):
@@ -508,9 +510,8 @@ def tile_list_kinase_selectivity_kernel(
             gate_pocket(c)
         for c in (14, 15, 6, 7):
             turn_back(c)
-        gain_on_vector(6)
+        gain_on_vector(6, slice(64, 256))
         visit_planes = held([P, 7 * 256], U8, "visit_planes", "silu6", 2 * KIB)
-        cast_wo(1, slice(0, 64), nc.vector.tensor_copy, "silu6")
         quantise_h(5, plane=visit_planes[:, 0:512])
         quantise_wo(0, visit_planes[:, 512:768])
         quantise_h(0, plane=visit_planes[:, 1024:1280])

@@ -435,7 +435,7 @@ def tile_list_kinase_selectivity_kernel(
                     start=(first and (apart or nt == 0)), stop=(not first and (apart or nt == 1)),
                 )
             if not first:
-                result = held([P, 2, width], F32, "result%d" % j0)
+                result = held([P, 2, width], F32, "result%d" % j0, "silu8" if j0 == 0 else None)
                 if apart:
                     nc.vector.tensor_copy(result[:, 0, :], sums[j0][0][:, 0, :])
                     nc.scalar.copy(result[:, 1, :], sums[j0][1][:, 0, :])
@@ -501,8 +501,8 @@ def tile_list_kinase_selectivity_kernel(
                 gain_on_gpsimd(span)
             if slots[-1] == 3 and span == 6:
                 gain_on_gpsimd(span, slice(0, 64))
-                for piece in range(4):
-                    cast_wo(piece // 2, slice(32 * (piece % 2), 32 * (piece % 2) + 32), nc.scalar.copy)
+                for piece in range(2):
+                    cast_wo(0, slice(32 * piece, 32 * piece + 32), nc.scalar.copy)
         shift_stage(15)
         gate_pocket(15)
         for c in (6, 7):
@@ -512,20 +512,22 @@ def tile_list_kinase_selectivity_kernel(
             turn_back(c)
         gain_on_vector(6, slice(64, 256))
         visit_planes = held([P, 7 * 256], U8, "visit_planes", "silu6", 2 * KIB)
+        cast_wo(1, slice(0, 64), nc.vector.tensor_copy, "silu6")
         quantise_h(5, plane=visit_planes[:, 0:512])
         quantise_wo(0, visit_planes[:, 512:768])
         quantise_h(0, plane=visit_planes[:, 1024:1280])
         quantise_wo(1, visit_planes[:, 768:1024])
         product_half(0, 256, 0, (4,))
-        product_half(0, 256, 1)
         quantise_h(1, plane=visit_planes[:, 1280:1792])
-        product_half(256, 256, 0, (0,))
-        product_half(256, 256, 1)
         gain_on_gpsimd(7, slice(0, 192))
+        gain_on_vector(8)
+        product_half(0, 256, 1)
         product_half(512, 256, 0, (3,))
-        for span in (8, 9, 3, 4):
-            gain_on_vector(span)
+        product_half(256, 256, 0, (4,))
+        product_half(256, 256, 1)
         gain_on_vector(7, slice(192, 256))
+        for span in (9, 3, 4):
+            gain_on_vector(span)
         last_planes = held([P, 3 * 256], U8, "last_planes", "silu7")
         quantise_h(7, plane=last_planes[:, 512:768])
         product_half(512, 256, 1)

@@ -34,11 +34,11 @@ UNITS = [
 ]
 NUNIT = len(UNITS)
 FIRST_VISIT = 1
-ORDER = (0, 1, 2, 3, 4, 5, 8, 9, 10, 11, 12, 13, 14, 15)
-LATE_GATE_STEP = {8: 1, 9: 3, 10: 4, 11: 5, 12: 6, 13: 7, 14: 8, 15: 9}
+ORDER = (0, 1, 2, 3, 4, 5, 8, 9, 10, 11, 12, 13, 14, 6, 7, 15)
+LATE_GATE_STEP = {8: 1, 9: 3, 10: 4, 11: 5, 12: 6, 13: 6, 14: 8, 15: 8}
 TANH_OVER = {
     5: "w8_room", 6: "w4_raw0", 7: "w8_room_end", 8: "tanh_half0", 9: "tanh_half1", 10: "tanh_half2", 11: "tanh_half3", 12: "tanh_half4",
-    13: "gated9", 14: "tanh_half8", 15: "gated11",
+    13: "tanh_half5", 14: "tanh_half8", 15: "tanh_half9",
 }
 TURNED = (6, 7, 14, 15)
 TURNED_BANKS = {6: 1, 7: 0, 14: 5, 15: 6}
@@ -265,7 +265,7 @@ def tile_list_kinase_selectivity_kernel(
             nc.scalar.activation(tanh_half[c][:], acc[:].rearrange("p t j -> p j t"), ACT.Tanh, scale=0.5)
 
         def pocket_stage(c):
-            number = POCKET_BANKS[ORDER.index(c) % 3] if c in ORDER else TURNED_BANKS[c]
+            number = POCKET_BANKS[ORDER.index(c) % 3]
             span, slots = UNITS[c]
             b, j0, width = SPANS[span]
             if c in TURNED:
@@ -477,7 +477,7 @@ def tile_list_kinase_selectivity_kernel(
         shift_stage(0)
         gains = held([P, 8], F32, "gains")
         gate_pocket(0)
-        for step, c in enumerate(ORDER[:-2]):
+        for step, c in enumerate(ORDER[:-4]):
             pocket_stage(ORDER[step + 2])
             shift_stage(ORDER[step + 1])
             gate_pocket(ORDER[step + 1])
@@ -500,17 +500,17 @@ def tile_list_kinase_selectivity_kernel(
             if slots[-1] == 3 and span in (0, 1, 2, 5):
                 gain_on_gpsimd(span)
             if slots[-1] == 3 and span == 6:
-                gain_on_gpsimd(span, slice(0, 64))
                 for piece in range(2):
                     cast_wo(0, slice(32 * piece, 32 * piece + 32), nc.scalar.copy)
+        pocket_stage(7)
         shift_stage(15)
+        gate_pocket(6)
+        pocket_stage(15)
+        gate_pocket(7)
         gate_pocket(15)
-        for c in (6, 7):
-            pocket_stage(c)
-            gate_pocket(c)
-        for c in (14, 15, 6, 7):
+        for c in (14, 6, 7, 15):
             turn_back(c)
-        gain_on_vector(6, slice(64, 256))
+        gain_on_vector(6)
         visit_planes = held([P, 7 * 256], U8, "visit_planes", "silu6", 2 * KIB)
         cast_wo(1, slice(0, 64), nc.vector.tensor_copy, "silu6")
         quantise_h(5, plane=visit_planes[:, 0:512])
@@ -526,12 +526,12 @@ def tile_list_kinase_selectivity_kernel(
         product_half(256, 256, 0, (4,))
         product_half(256, 256, 1)
         gain_on_vector(7, slice(192, 256))
-        for span in (9, 3, 4):
+        for span in (3, 4, 9):
             gain_on_vector(span)
         last_planes = held([P, 3 * 256], U8, "last_planes", "silu7")
         quantise_h(7, plane=last_planes[:, 512:768])
         product_half(512, 256, 1)
-        quantise_h(8, plane=last_planes[:, 256:512])
-        product_half(768, 256, 1, (5, 6))
         quantise_h(3, plane=last_planes[:, 0:256])
-        product_half(768, 256, 0)
+        product_half(768, 256, 0, (0, 1))
+        quantise_h(8, plane=last_planes[:, 256:512])
+        product_half(768, 256, 1)

@@ -326,7 +326,7 @@ def tile_list_kinase_selectivity_kernel(
 
         MIXED_OVER = {5: ("mixed0", 0), 6: ("mixed1", 0)}
         SILU_OVER = {
-            1: ("w4_raw1", 0), 5: ("silu0", 0), 7: ("silu2", 0), 8: ("silu1", 0), 9: ("silu1", 2 * KIB),
+            0: ("w4_raw1", 0), 5: ("silu0", 0), 7: ("silu2", 0), 8: ("silu1", 0), 9: ("silu1", 2 * KIB),
         }
 
         def add_shift(c):
@@ -411,6 +411,19 @@ def tile_list_kinase_selectivity_kernel(
                 wo_raw[b][:].rearrange("p t (c i) -> p c t i", i=4)[:, groups],
             )
 
+        def cast_wo_quarter(half, move, over=None):
+            wo_bf[1, half] = held([P, P, 4], BF16, "wo_bf1_%d" % half, over)
+            move(
+                wo_bf[1, half][:].rearrange("p (c i) t -> p c t i", i=4),
+                wo_raw[1][:, :, half * P : (half + 1) * P].rearrange("p t (c i) -> p c t i", i=4),
+            )
+
+        def quantise_wo_quarter(half, plane):
+            nc.vector.quantize_mx(
+                out=wo_codes[:, N + half * P : N + (half + 1) * P].bitcast(FP8X4), scales=plane,
+                in_=wo_bf[1, half][:].rearrange("p n t -> p (n t)"),
+            )
+
         def quantise_wo(b, plane):
             wo_plane[b] = plane
             nc.vector.quantize_mx(
@@ -457,13 +470,13 @@ def tile_list_kinase_selectivity_kernel(
         v_words.append(gather_words(tab_w[1], lists, "v_words1", (256, 768)))
         load_wg_second(0)
         load_wg_second(1)
+        load_w4(1)
+        load_w8(1)
         for b in range(2):
             nc.sync.dma_start(
                 out=gain_rows[4 * b : 4 * b + 4, :].rearrange("t (u e) -> t u e", e=4),
                 in_=gain[512 * b : 512 * (b + 1)].rearrange("(u t e) -> t u e", t=4, e=4),
             )
-        load_w4(1)
-        load_w8(1)
         move_rows(slice(early, (S + 3 * H) // 4))
         load_wo(0)
         load_wo(1)
@@ -484,10 +497,11 @@ def tile_list_kinase_selectivity_kernel(
             if step == 0:
                 shift_stage(6)
                 shift_stage(7)
+            if step == 1:
+                order_w4(1, nc.scalar.copy, U32)
             add_shift(c)
             span, slots = UNITS[c]
             if step == 1:
-                order_w4(1, nc.scalar.copy, U32)
                 order_w8(1, nc.scalar.copy, U32)
             if step == FIRST_VISIT:
                 quantise_wg(1, "gated%d" % c)
@@ -500,8 +514,10 @@ def tile_list_kinase_selectivity_kernel(
             if slots[-1] == 3 and span in (0, 1, 2, 5):
                 gain_on_gpsimd(span)
             if slots[-1] == 3 and span == 6:
+                gain_on_gpsimd(span, slice(0, 48))
                 for piece in range(2):
                     cast_wo(0, slice(32 * piece, 32 * piece + 32), nc.scalar.copy)
+                cast_wo_quarter(0, nc.scalar.copy)
         pocket_stage(7)
         shift_stage(15)
         gate_pocket(6)
@@ -510,13 +526,15 @@ def tile_list_kinase_selectivity_kernel(
         gate_pocket(15)
         for c in (14, 6, 7, 15):
             turn_back(c)
-        gain_on_vector(6)
+        gain_on_vector(6, slice(48, 256))
         visit_planes = held([P, 7 * 256], U8, "visit_planes", "silu6", 2 * KIB)
-        cast_wo(1, slice(0, 64), nc.vector.tensor_copy, "silu6")
+        cast_wo_quarter(1, nc.vector.tensor_copy, "silu6")
         quantise_h(5, plane=visit_planes[:, 0:512])
         quantise_wo(0, visit_planes[:, 512:768])
         quantise_h(0, plane=visit_planes[:, 1024:1280])
-        quantise_wo(1, visit_planes[:, 768:1024])
+        wo_plane[1] = visit_planes[:, 768:1024]
+        quantise_wo_quarter(0, visit_planes[:, 768:896])
+        quantise_wo_quarter(1, visit_planes[:, 896:1024])
         product_half(0, 256, 0, (4,))
         quantise_h(1, plane=visit_planes[:, 1280:1792])
         gain_on_gpsimd(7, slice(0, 192))

from contextlib import ExitStack

import concourse.mybir as mybir
from concourse.masks import make_identity

K, K2, T, T2, S, H, N = 1024, 512, 2048, 4096, 1024, 1024, 256
FLOPS = 2 * S * (K * H + 2 * K2 * H + H * N)

F32 = mybir.dt.float32
BF16 = mybir.dt.bfloat16
I32 = mybir.dt.int32
U32 = mybir.dt.uint32
U16 = mybir.dt.uint16
U8 = mybir.dt.uint8
FP8X4 = mybir.dt.float8_e4m3fn_x4
FP4X4 = mybir.dt.float4_e2m1fn_x4
ACT = mybir.ActivationFunctionType
ADD = mybir.AluOpType.add
MULT = mybir.AluOpType.mult
BYTES_OF = {F32: 4, BF16: 2, I32: 4, U32: 4, U8: 1}

P = 128
KIB = 1024
W4A, W4B, W8 = range(3)
V2_ROW = 4
SPANS = (
    (0, 0, 256), (0, 256, 256), (0, 512, 256), (0, 768, 128), (0, 896, 128),
    (1, 0, 256), (1, 256, 256), (1, 512, 256), (1, 768, 128), (1, 896, 128),
)
UNITS = [
    (span, slots)
    for span, (b, j0, width) in enumerate(SPANS)
    for slots in (((0, 1, 2, 3),) if width == 128 else ((0, 1), (2, 3)))
]
NUNIT = len(UNITS)
FIRST_VISIT = 1
ORDER = (0, 1, 2, 3, 4, 5, 8, 9, 10, 11, 12, 13, 14, 6, 7, 15)
LATE_GATE_STEP = {8: 1, 9: 3, 10: 4, 11: 5, 12: 6, 13: 6, 14: 8, 15: 8}
TANH_OVER = {
    5: "w8_room", 6: "w4_raw0", 7: "w8_room_end", 8: "tanh_half0", 9: "tanh_half1", 10: "tanh_half2", 11: "tanh_half3", 12: "tanh_half4",
    13: "tanh_half5", 14: "tanh_half8", 15: "tanh_half9",
}
TURNED = (6, 7, 14, 15)
TURNED_BANKS = {6: 1, 7: 0, 14: 5, 15: 6}
TURNED_SHIFT_BANKS = {6: 0, 7: 7, 14: 5, 15: 6}
EARLY_GATE_BANKS, LATE_GATE_BANKS, POCKET_BANKS, SHIFT_BANKS = (0, 1, 7), (0, 1), (2, 3, 4), (5, 6)


def tile_list_kinase_selectivity_kernel(
    tc, tab_words, tab_scales, offs, tab2_words, tab2_scales, offs2,
    w4_words, w4_scales, wg, w8_words, w8_scales, gain, wo, out,
):
    nc = tc.nc
    with ExitStack() as ctx:
        keep = ctx.enter_context(tc.tile_pool(name="keep", bufs=1))
        arena = ctx.enter_context(tc.tile_pool(name="arena", bufs=1))
        psum = ctx.enter_context(tc.psum_pool(name="psum", bufs=1))
        place = {"top": 0}

        def held(shape, dtype, name, over=None, plus=0, room=0):
            if over is None:
                size = BYTES_OF[dtype]
                for extent in shape[1:]:
                    size = size * extent
                place[name] = place["top"]
                place["top"] = place["top"] + max(size, room, 64)
            else:
                place[name] = place[over] + plus
            return arena.tile(shape, dtype, name=name, align_bytes=64, offset=place[name])

        tenants = []

        def bank(number, shape):
            tenants.append(number)
            return psum.tile(shape, F32, name="bank%d_%d" % (number, len(tenants)), offset=2 * KIB * number)

        lists = keep.tile([P, S // 16], U16, name="lists")
        list2 = keep.tile([P, S // 16], U16, name="list2")
        tab_s = held([P, T], U8, "tab_s")
        tab2_s = held([P, T2], U8, "tab2_s")
        ws_raw = held([P, 3, H], U8, "ws_raw")
        v2_plane = held([P, S], U8, "v2_plane")
        planes = held([P, S + 3 * H], U8, "planes")
        stage = held([P, S + 3 * H], U8, "stage")
        nc.vector.memset(tab_s[:].bitcast(I32), 0)
        nc.vector.memset(ws_raw[:].bitcast(I32), 0)
        nc.vector.memset(tab2_s[:].bitcast(I32)[0:112, :], 0)
        nc.vector.memset(v2_plane[:].bitcast(I32), 0)
        nc.vector.memset(planes[:].bitcast(I32), 0)
        gain_rows = held([P, P], F32, "gain_rows")
        nc.gpsimd.memset(gain_rows[:], 0.0)

        warm = held([P, 2], F32, "warm")
        nc.vector.memset(warm[:, 0:1], 0.0)
        nc.scalar.activation(warm[:, 1:2], warm[:, 0:1], ACT.Silu)

        wg_raw, wg_bf, wg_codes, wg_plane, w4_codes, w8_codes, wo_raw = {}, {}, {}, {}, {}, {}, {}

        def load_wg(b):
            wg_raw[b] = held([P, 4, 512], F32, "wg_raw%d" % b)
            nc.sync.dma_start(
                out=wg_raw[b][:], in_=wg.rearrange("(p j) c -> p j c", j=4)[:, :, 512 * b : 512 * (b + 1)]
            )

        def cast_wg_first():
            wg_bf[0] = held([P, 4, P, 4], BF16, "wg_bf0")
            nc.scalar.copy(
                wg_bf[0][:].rearrange("p t (u e) j -> p t u j e", e=4),
                wg_raw[0][:].rearrange("p j (u t e) -> p t u j e", t=4, e=4),
            )

        def load_wg_second(half):
            wg_raw[1, half] = held([P, 4, 256], F32, "wg_raw1_%d" % half)
            start = 512 + 256 * half
            nc.sync.dma_start(
                out=wg_raw[1, half][:], in_=wg.rearrange("(p j) c -> p j c", j=4)[:, :, start : start + 256]
            )

        def cast_wg_second(half):
            if half == 0:
                wg_bf[1] = held([P, 4, P, 4], BF16, "wg_bf1", "tab_w1", 5 * KIB // 2)
            nc.gpsimd.tensor_scalar(
                wg_bf[1][:].rearrange("p t (u e) j -> p u t (e j)", e=4)[:, 16 * half : 16 * (half + 1)],
                wg_raw[1, half][:].rearrange("p j c -> p c j"), 1.0, 0.0, MULT, ADD,
            )

        def quantise_wg(b, over=None):
            wg_codes[b] = held([P, 512], U32, "wg_codes%d" % b, over)
            wg_plane[b] = held([P, 512], U8, "wg_plane%d" % b)
            nc.vector.quantize_mx(
                out=wg_codes[b][:].bitcast(FP8X4), scales=wg_plane[b][:],
                in_=wg_bf[b][:].rearrange("p t m j -> p (t m j)"),
            )

        def load_table(name, words, width):
            tile = held([P, width], U32, name)
            nc.sync.dma_start(out=tile[:].bitcast(I32), in_=words.rearrange("p t i -> p (t i)").bitcast(I32))
            return tile

        w4_raw, w8_raw = {}, {}

        def load_w4(b):
            w4_raw[b] = held([P, 2, 256], U32, "w4_raw%d" % b, room=4 * KIB if b else 0)
            nc.sync.dma_start(
                out=w4_raw[b][:].bitcast(I32),
                in_=w4_words.bitcast(I32).rearrange("a p c -> p a c")[:, :, 256 * b : 256 * (b + 1)],
            )

        def load_w8(b):
            if b == 0:
                place["w8_room"], place["w8_room_end"] = place["top"], place["top"] + 2 * KIB
                place["top"] = place["top"] + 4 * KIB
            w8_raw[b] = held([P, 512], U32, "w8_raw%d" % b, None if b else "w8_room", KIB)
            nc.sync.dma_start(
                out=w8_raw[b][:].bitcast(I32),
                in_=w8_words[0].rearrange("p c i -> p (c i)").bitcast(I32)[:, 512 * b : 512 * (b + 1)],
            )

        def order_w4(b, move, dtype, over=None):
            w4_codes[b] = held([P, 2, 4, 256], U8, "w4_codes%d" % b, over)
            move(
                w4_codes[b][:].bitcast(dtype).rearrange("p a t (u w) -> p a t u w", w=2),
                w4_raw[b][:].bitcast(dtype).rearrange("p a (u t w) -> p a t u w", t=4, w=2),
            )

        def order_w8(b, move, dtype, over=None):
            w8_codes[b] = held([P, 4, P], U32, "w8_codes%d" % b, over)
            move(
                w8_codes[b][:].bitcast(dtype).rearrange("p t (u e) -> p t u e", e=4),
                w8_raw[b][:].bitcast(dtype).rearrange("p (u t e) -> p t u e", t=4, e=4),
            )

        def load_wo(b):
            wo_raw[b] = held([P, 4, N], F32, "wo_raw%d" % b)
            rows = wo[512 * b : 512 * (b + 1), :].rearrange("(u t e) n -> t u e n", t=4, e=4)
            for t in range(4):
                nc.sync.dma_start(out=wo_raw[b][:, t, :], in_=rows[t])

        def gather_words(window, offsets, name, widths):
            pieces, start = [], 0
            for width in widths:
                picked = held([P, width], U32, "%s_%d" % (name, start))
                nc.vector.tensor_copy(picked[:], window[:].indirect(offsets[:, start // 16 : (start + width) // 16]))
                pieces.append((start, width, picked))
                start = start + width
            return pieces

        nc.sync.dma_start(list2[:], offs2)
        nc.sync.dma_start(out=tab2_s[:].bitcast(I32)[112:P, :], in_=tab2_scales[0].bitcast(I32))
        load_wg(0)
        nc.sync.dma_start(lists[:], offs)
        nc.sync.dma_start(
            out=tab_s[:].bitcast(I32)[0:P:4, :], in_=tab_scales.bitcast(I32).rearrange("a q c -> q a c")
        )
        nc.sync.dma_start(
            out=ws_raw[:].bitcast(I32)[4:P:8, 0:2, :], in_=w4_scales.bitcast(I32).rearrange("a q c -> q a c")
        )
        nc.sync.dma_start(out=ws_raw[:].bitcast(I32)[4:P:8, 2, :], in_=w8_scales[0].bitcast(I32))
        tab2_w = load_table("tab2_w", tab2_words[0], T2)

        v2_picked = held([P, S], U8, "v2_picked")
        nc.vector.tensor_copy(v2_picked[:], tab2_s[:].indirect(list2[:]))
        for r in range(4):
            nc.sync.dma_start(
                out=v2_plane[:].bitcast(I32)[V2_ROW + r : P : 32, :], in_=v2_picked[:].bitcast(I32)[112 + r : P : 4, :]
            )
        tab_w = [load_table("tab_w0", tab_words[0], T)]
        cast_wg_first()
        nc.scalar.copy(
            stage[:].bitcast(U32)[:, S // 4 :].rearrange("p (b x t u) -> p b x u t", b=2, x=3, t=4),
            ws_raw[:].bitcast(U32).rearrange("p x (b u t) -> p b x u t", b=2, t=4),
        )
        v_picked = held([P, S], U8, "v_picked")
        nc.vector.tensor_copy(v_picked[:], tab_s[:].indirect(lists[:]))
        picked32, stage32, planes32 = v_picked[:].bitcast(I32), stage[:].bitcast(I32), planes[:].bitcast(I32)
        nc.vector.tensor_copy(stage32[:, 0 : S // 4], picked32)
        quantise_wg(0)

        def move_first_pass_row(r):
            nc.sync.dma_start(out=stage32[r:P:32, 0 : S // 4], in_=picked32[8 * r : P : 32, :])

        def move_rows(cols):
            for r in range(4):
                nc.sync.dma_start(out=planes32[r:P:32, cols], in_=stage32[4 + 8 * r : P : 32, cols])

        early = (S + 3 * 512) // 4
        for r in range(1, 4):
            move_first_pass_row(r)
        tab_w.append(load_table("tab_w1", tab_words[1], T))
        v2_words = gather_words(tab2_w, list2, "v2_words", (256, 768))
        v_plane = [stage[:, 0:S], planes[:, 0:S]]

        def weight_plane(x, b, t, width=P):
            start = S + (3 * b + x) * 512 + t * P
            return planes[:, start : start + width]

        def moving(pieces, j0, width):
            first, size, picked = [piece for piece in pieces if piece[0] <= j0 < piece[0] + piece[1]][0]
            return picked[:, j0 - first : j0 - first + width].bitcast(FP8X4)

        tanh_half, pocket, shift, gated, mixed, silu = {}, {}, {}, {}, {}, {}

        def gate_stage(c, number):
            span, slots = UNITS[c]
            b, j0, width = SPANS[span]
            over = TANH_OVER.get(c)
            if c in TURNED:
                acc = bank(number, [P, 512])
                nc.tensor.matmul_mx(
                    acc[:], lhsT=moving(v2_words, j0, width), lhsT_scale=v2_plane[V2_ROW:P, j0 : j0 + width],
                    rhs=wg_codes[b][:].bitcast(FP8X4), rhs_scale=wg_plane[b][:], start=True, stop=True,
                )
                tanh_half[c] = held([P, 512], F32, "tanh_half%d" % c, over)
                nc.scalar.activation(tanh_half[c][:], acc[:], ACT.Tanh, scale=0.5)
                return
            acc = bank(number, [P, len(slots), width])
            for i, t in enumerate(slots):
                cols = slice(t * P, (t + 1) * P)
                nc.tensor.matmul_mx(
                    acc[:, i, :], lhsT=wg_codes[b][:, cols].bitcast(FP8X4), lhsT_scale=wg_plane[b][:, cols],
                    rhs=moving(v2_words, j0, width), rhs_scale=v2_plane[V2_ROW:P, j0 : j0 + width],
                    start=True, stop=True,
                )
            tanh_half[c] = held([P, width, len(slots)], F32, "tanh_half%d" % c, over)
            nc.scalar.activation(tanh_half[c][:], acc[:].rearrange("p t j -> p j t"), ACT.Tanh, scale=0.5)

        def pocket_stage(c):
            number = POCKET_BANKS[ORDER.index(c) % 3]
            span, slots = UNITS[c]
            b, j0, width = SPANS[span]
            if c in TURNED:
                pocket[c] = bank(number, [P, 512])
                for a in range(2):
                    nc.tensor.matmul_mx(
                        pocket[c][:], lhsT=moving(v_words[a], j0, width), lhsT_scale=v_plane[a][:, j0 : j0 + width],
                        rhs=w4_codes[b][:, a].rearrange("p t c -> p (t c)").bitcast(FP4X4),
                        rhs_scale=weight_plane(W4A + a, b, 0, 512), start=a == 0, stop=a == 1,
                    )
                return
            pocket[c] = bank(number, [P, len(slots), width])
            for i, t in enumerate(slots):
                for a in range(2):
                    nc.tensor.matmul_mx(
                        pocket[c][:, i, :], lhsT=w4_codes[b][:, a, t, :].bitcast(FP4X4),
                        lhsT_scale=weight_plane(W4A + a, b, t), rhs=moving(v_words[a], j0, width),
                        rhs_scale=v_plane[a][:, j0 : j0 + width], start=a == 0, stop=a == 1,
                    )

        def shift_stage(c):
            span, slots = UNITS[c]
            b, j0, width = SPANS[span]
            if c in TURNED:
                acc = bank(TURNED_SHIFT_BANKS[c], [P, 512])
                nc.tensor.matmul_mx(
                    acc[:], lhsT=moving(v2_words, j0, width), lhsT_scale=v2_plane[V2_ROW:P, j0 : j0 + width],
                    rhs=w8_codes[b][:].rearrange("p t m -> p (t m)").bitcast(FP8X4),
                    rhs_scale=weight_plane(W8, b, 0, 512), start=True, stop=True,
                )
                over = "mixed2" if c > 7 else None
                shift[c] = held([P, 512], F32, "shift_twice%d" % c, over, 2 * KIB * (c % 2))
                nc.scalar.activation(shift[c][:], acc[:], ACT.Copy, scale=2.0)
                return
            shift[c] = bank(SHIFT_BANKS[c % 2], [P, len(slots), width])
            for i, t in enumerate(slots):
                nc.tensor.matmul_mx(
                    shift[c][:, i, :], lhsT=w8_codes[b][:, t, :].bitcast(FP8X4), lhsT_scale=weight_plane(W8, b, t),
                    rhs=moving(v2_words, j0, width), rhs_scale=v2_plane[V2_ROW:P, j0 : j0 + width],
                    start=True, stop=True,
                )

        def gate_pocket(c):
            span, slots = UNITS[c]
            width = SPANS[span][2]
            if c in (FIRST_VISIT + 2, FIRST_VISIT + 3):
                over, plus = "wg_bf1", -KIB + 4 * KIB * (c - FIRST_VISIT - 2)
            else:
                over, plus = (("tab2_w", "tab2_w", "tab_w0", "wg_raw0")[c // 4], 2 * KIB * (c % 8 if c < 8 else c % 4))
            if c in TURNED:
                gated[c] = held([P, 512], F32, "gated%d" % c, over, plus)
                nc.vector.scalar_tensor_tensor(gated[c][:], tanh_half[c][:], 1.0, pocket[c][:], ADD, MULT)
                return
            gated[c] = held([P, width, len(slots)], F32, "gated%d" % c, over, plus)
            nc.vector.scalar_tensor_tensor(
                gated[c][:], tanh_half[c][:], 1.0, pocket[c][:].rearrange("p t j -> p j t"), ADD, MULT
            )

        MIXED_OVER = {5: ("mixed0", 0), 6: ("mixed1", 0)}
        SILU_OVER = {
            0: ("w4_raw1", 0), 5: ("silu0", 0), 7: ("silu2", 0), 8: ("silu1", 0), 9: ("silu1", 2 * KIB),
        }

        def add_shift(c):
            span, slots = UNITS[c]
            width = SPANS[span][2]
            parts = 4 // len(slots)
            if slots[0] == 0:
                over, plus = MIXED_OVER.get(span, (None, 0))
                mixed[span] = held([P, parts, width, len(slots)], F32, "mixed%d" % span, over, plus, 4 * KIB)
            nc.vector.scalar_tensor_tensor(
                mixed[span][:, slots[0] // len(slots)], gated[c][:], 0.5,
                shift[c][:].rearrange("p t j -> p j t"), MULT, ADD,
            )
            if slots[-1] == 3:
                over, plus = SILU_OVER.get(span, (None, 0))
                silu[span] = held([P, width, 4], F32, "silu%d" % span, over, plus)
                nc.scalar.activation(
                    silu[span][:].rearrange("p j (u e) -> p j u e", u=parts),
                    mixed[span][:].rearrange("p u j e -> p j u e"), ACT.Silu,
                )

        def turn_back(c):
            span = UNITS[c][0]
            total = bank(TURNED_BANKS[c], [P, 4, P])
            for i, term in enumerate((shift[c], gated[c])):
                for t in range(4):
                    nc.tensor.matmul(
                        total[:, t, :], lhsT=term[:, t * P : (t + 1) * P], rhs=identity[:], is_transpose=True,
                        start=(i == 0 and t == 0), stop=(i == 1 and t == 3),
                    )
            over, plus = SILU_OVER.get(span, (None, 0))
            silu[span] = held([P, P, 4], F32, "silu%d" % span, over, plus)
            nc.scalar.activation(silu[span][:], total[:].rearrange("p t j -> p j t"), ACT.Silu, scale=0.5)

        H_TILES = {0: (0,), 1: (1, 2), 3: (3, 4), 5: (5, 6), 7: (7,), 8: (8, 9)}
        H_OVER = {0: ("wg_bf1", KIB), 3: ("h_bf1", 0), 7: ("h_bf1", 2 * KIB), 8: ("wo_bf0", 0)}
        h_bf, h_at, h_plane = {}, {}, {}
        h_codes = held([P, 2 * S], U32, "h_codes")

        def h_target(span):
            first = [key for key in H_TILES if span in H_TILES[key]][0]
            if first not in h_bf:
                over, plus = H_OVER.get(first, (None, 0))
                total = sum(SPANS[member][2] for member in H_TILES[first])
                h_bf[first] = held([P, total, 4], BF16, "h_bf%d" % first, over, plus)
            start = 0 if span == first else SPANS[first][2]
            return h_bf[first][:, start : start + SPANS[span][2], :]

        def gain_on_gpsimd(span, cols=slice(None)):
            b = SPANS[span][0]
            source = silu[span][:, cols]
            factor = gains[:, 4 * b : 4 * b + 4].unsqueeze(1).to_broadcast(source.shape)
            nc.gpsimd.tensor_tensor(h_target(span)[:, cols], source, factor, MULT)

        def gain_on_vector(span, cols=slice(None)):
            b = SPANS[span][0]
            source = silu[span][:, cols]
            factor = gain_bank[:, 4 * b : 4 * b + 4].unsqueeze(1).to_broadcast(source.shape)
            nc.vector.scalar_tensor_tensor(h_target(span)[:, cols], source, 1.0, factor, MULT, MULT)

        def quantise_h(first, over=None, plane=None):
            b, j0, width = SPANS[first]
            total = sum(SPANS[member][2] for member in H_TILES[first])
            start = b * S + j0
            if plane is None:
                plane = held([P, total], U8, "h_plane%d" % first, over)[:]
            for k in range(0, total, P):
                h_plane[start + k] = plane[:, k:]
            nc.vector.quantize_mx(
                out=h_codes[:, start : start + total].bitcast(FP8X4), scales=plane,
                in_=h_bf[first][:].rearrange("p j t -> p (j t)"),
            )

        wo_bf, wo_plane = {}, {}
        wo_codes = held([P, 2 * N], U32, "wo_codes")

        def cast_wo(b, groups, move, over=None):
            if b not in wo_bf:
                wo_bf[b] = held([P, N, 4], BF16, "wo_bf%d" % b, over)
            move(
                wo_bf[b][:].rearrange("p (c i) t -> p c t i", i=4)[:, groups],
                wo_raw[b][:].rearrange("p t (c i) -> p c t i", i=4)[:, groups],
            )

        def cast_wo_quarter(half, move, over=None):
            wo_bf[1, half] = held([P, P, 4], BF16, "wo_bf1_%d" % half, over)
            move(
                wo_bf[1, half][:].rearrange("p (c i) t -> p c t i", i=4),
                wo_raw[1][:, :, half * P : (half + 1) * P].rearrange("p t (c i) -> p c t i", i=4),
            )

        def quantise_wo_quarter(half, plane):
            nc.vector.quantize_mx(
                out=wo_codes[:, N + half * P : N + (half + 1) * P].bitcast(FP8X4), scales=plane,
                in_=wo_bf[1, half][:].rearrange("p n t -> p (n t)"),
            )

        def quantise_wo(b, plane):
            wo_plane[b] = plane
            nc.vector.quantize_mx(
                out=wo_codes[:, b * N : (b + 1) * N].bitcast(FP8X4), scales=plane,
                in_=wo_bf[b][:].rearrange("p n t -> p (n t)"),
            )

        sums = {}

        def product_half(j0, width, b, numbers=None, copy_out=nc.scalar.copy):
            first = j0 not in sums
            if first:
                sums[j0] = [bank(number, [P, 2 // len(numbers), width]) for number in numbers]
            apart = len(sums[j0]) == 2
            start = b * S + j0
            for nt in range(2):
                cols = slice(b * N + nt * P, b * N + (nt + 1) * P)
                nc.tensor.matmul_mx(
                    sums[j0][nt][:, 0, :] if apart else sums[j0][0][:, nt, :],
                    lhsT=wo_codes[:, cols].bitcast(FP8X4), lhsT_scale=wo_plane[b][:, nt * P : (nt + 1) * P],
                    rhs=h_codes[:, start : start + width].bitcast(FP8X4), rhs_scale=h_plane[start][:, 0:width],
                    start=(first and (apart or nt == 0)), stop=(not first and (apart or nt == 1)),
                )
            if not first:
                result = held([P, 2, width], F32, "result%d" % j0, "silu8" if j0 == 0 else None)
                if apart:
                    nc.vector.tensor_copy(result[:, 0, :], sums[j0][0][:, 0, :])
                    nc.scalar.copy(result[:, 1, :], sums[j0][1][:, 0, :])
                else:
                    copy_out(result[:], sums[j0][0][:])
                nc.sync.dma_start(out=out.rearrange("(nt p) j -> p nt j", p=P)[:, :, j0 : j0 + width], in_=result[:])

        for c in range(5):
            gate_stage(c, EARLY_GATE_BANKS[c % 3])
        v_words = [gather_words(tab_w[0], lists, "v_words0", (1024,))]
        load_w4(0)
        move_rows(slice(0, early))
        load_w8(0)
        order_w4(0, nc.scalar.copy, U32)
        gate_stage(6, EARLY_GATE_BANKS[0])
        order_w8(0, nc.scalar.copy, U32)
        gate_stage(7, SHIFT_BANKS[1])
        gate_stage(5, EARLY_GATE_BANKS[2])
        v_words.append(gather_words(tab_w[1], lists, "v_words1", (256, 768)))
        load_wg_second(0)
        load_wg_second(1)
        load_w4(1)
        load_w8(1)
        for b in range(2):
            nc.sync.dma_start(
                out=gain_rows[4 * b : 4 * b + 4, :].rearrange("t (u e) -> t u e", e=4),
                in_=gain[512 * b : 512 * (b + 1)].rearrange("(u t e) -> t u e", t=4, e=4),
            )
        move_rows(slice(early, (S + 3 * H) // 4))
        load_wo(0)
        load_wo(1)
        identity = held([P, P], F32, "identity", "tab_w1", KIB)
        make_identity(nc, identity[:])
        cast_wg_second(0)
        cast_wg_second(1)

        pocket_stage(0)
        pocket_stage(1)
        shift_stage(0)
        gains = held([P, 8], F32, "gains")
        gate_pocket(0)
        for step, c in enumerate(ORDER[:-4]):
            pocket_stage(ORDER[step + 2])
            shift_stage(ORDER[step + 1])
            gate_pocket(ORDER[step + 1])
            if step == 0:
                shift_stage(6)
                shift_stage(7)
            if step == 1:
                order_w4(1, nc.scalar.copy, U32)
            add_shift(c)
            span, slots = UNITS[c]
            if step == 1:
                order_w8(1, nc.scalar.copy, U32)
            if step == FIRST_VISIT:
                quantise_wg(1, "gated%d" % c)
                gain_bank = bank(7, [P, P])
                nc.tensor.transpose(gain_bank[:], gain_rows[:], identity[:])
                nc.vector.tensor_copy(gains[:], gain_bank[:, 0:8])
            for late in LATE_GATE_STEP:
                if LATE_GATE_STEP[late] == step:
                    gate_stage(late, LATE_GATE_BANKS[(late + 1) % 2])
            if slots[-1] == 3 and span in (0, 1, 2, 5):
                gain_on_gpsimd(span)
            if slots[-1] == 3 and span == 6:
                gain_on_gpsimd(span, slice(0, 48))
                for piece in range(2):
                    cast_wo(0, slice(32 * piece, 32 * piece + 32), nc.scalar.copy)
                cast_wo_quarter(0, nc.scalar.copy)
        pocket_stage(7)
        shift_stage(15)
        gate_pocket(6)
        pocket_stage(15)
        gate_pocket(7)
        gate_pocket(15)
        for c in (14, 6, 7, 15):
            turn_back(c)
        gain_on_vector(6, slice(48, 256))
        visit_planes = held([P, 7 * 256], U8, "visit_planes", "silu6", 2 * KIB)
        cast_wo_quarter(1, nc.vector.tensor_copy, "silu6")
        quantise_h(5, plane=visit_planes[:, 0:512])
        quantise_wo(0, visit_planes[:, 512:768])
        quantise_h(0, plane=visit_planes[:, 1024:1280])
        wo_plane[1] = visit_planes[:, 768:1024]
        quantise_wo_quarter(0, visit_planes[:, 768:896])
        quantise_wo_quarter(1, visit_planes[:, 896:1024])
        product_half(0, 256, 0, (4,))
        quantise_h(1, plane=visit_planes[:, 1280:1792])
        gain_on_gpsimd(7, slice(0, 192))
        gain_on_vector(8)
        product_half(0, 256, 1)
        product_half(512, 256, 0, (3,))
        product_half(256, 256, 0, (4,))
        product_half(256, 256, 1)
        gain_on_vector(7, slice(192, 256))
        for span in (3, 4, 9):
            gain_on_vector(span)
        last_planes = held([P, 3 * 256], U8, "last_planes", "silu7")
        quantise_h(7, plane=last_planes[:, 512:768])
        product_half(512, 256, 1)
        quantise_h(3, plane=last_planes[:, 0:256])
        product_half(768, 256, 0, (0, 1))
        quantise_h(8, plane=last_planes[:, 256:512])
        product_half(768, 256, 1)
